import numpy as np, ml_dtypes
CORES = [16,18,20,22]
N = 4
BF = ml_dtypes.bfloat16
def gentries(a):
    return np.ascontiguousarray(a.reshape(8, 16, -1).transpose(0, 2, 1)).reshape(8, -1)
def gtable(e):
    e = np.asarray(e); return np.ascontiguousarray(e.reshape(8, -1, 16).transpose(0, 2, 1)).reshape(128, -1).astype(np.int32)
V, C, H, NCL, ST, Q = 2048, 128, 4096, 8, 5, 32
LANE = np.arange(16)
def look(xs, l):
    a = np.take_along_axis(xs, l[:, None, :], 2).reshape(8, 16, C, 16)
    return a, np.max(a, axis=3) - np.min(a, axis=3)
def best(s, w, tag):
    u = np.add.reduce(w[:, :, :, None] * s[:, :, None, :], axis=1) & (H - 1)
    u1, u2 = u[:, 0], u[:, 1]
    h = (((u1 * u2) >> 5)[:, None, :] + (2 * LANE[:, None] + 1) * u2[:, None, :]) & (H - 1)
    cost = np.stack([np.add.reduce(np.abs(np.take_along_axis(tag, h[:, m:m + 1], 2) - s), axis=1) for m in range(16)], axis=1)
    m = np.argmin(cost, axis=1)
    return h, np.min(cost, axis=1), np.take_along_axis(h, m[:, None, :], 1)[:, 0]
def start(x, l, w, tag):
    o = []
    for r in range(N):
        s = look(x[r], l[r, :, r % NCL])[1]; h, least, hs = best(s, w[r], tag[r]); o.append((s, h, least))
    return [np.stack(z) for z in zip(*o)]
def mid(rng, least):
    return np.take_along_axis(np.sort(least, axis=-1), rng.integers(C // 5, 4 * C // 5, (N, 8, 1)), -1)[..., 0]
def parts(rng):
    x = rng.integers(0, 256, (N, 8, 16, V)); l = np.argsort(rng.random((N, 8, NCL, V)), axis=-1)
    tag = np.minimum((256 * rng.beta(15.0, 2.0, (N, 8, 16, H))).astype(np.int64), 255)
    e = np.argsort(rng.random((N, 8, H, 16)), axis=-1); f = np.argsort(e, axis=-1)
    return x, l, tag, np.ascontiguousarray((e + 16 * f).transpose(0, 1, 3, 2)), rng.integers(1, 256, (N, 8, 16, 2))
def plant(rng, s, h, tag, ids, n, dev, used, copies=1):
    done = []
    for i in ids:
        if len(done) == n: break
        i = int(i); free = sorted(set(int(z) for z in h[:, i]) - used)
        if len(free) < copies: continue
        for j in rng.permutation(len(free))[:copies]:
            z = free[int(j)]; used.add(z); p = int(rng.integers(0, 16)); tag[:, z] = s[:, i]
            tag[p, z] = s[p, i] + (dev if s[p, i] < 128 else -dev)
        done.append(i)
    return done
def wear(rng, x, ix, s):
    lo = (rng.random(s.shape) * (256 - s)).astype(np.int64); k = rng.integers(0, 16, s.shape); k2 = (k + rng.integers(1, 16, s.shape)) & 15
    a = lo[..., None] + (rng.random(s.shape + (16,)) * (s[..., None] + 1)).astype(np.int64)
    np.put_along_axis(a, k[..., None], lo[..., None], 2); np.put_along_axis(a, k2[..., None], (lo + s)[..., None], 2)
    x[:, ix] = a.reshape(16, -1)
def still(rng, x, ix, tag):
    s = rng.integers(20, 181, (16, C)); s[:2] = 0; z = np.zeros(C, np.int64)
    o = rng.permutation(C); a = np.sort(o[:Q + 3]); b = o[Q + 3:]
    z[a] = H // 2 + 2 + 2 * rng.permutation(H // 4 - 1)[:Q + 3]; z[b] = 1 + 2 * rng.permutation(H // 2 - 1)[:C - Q - 3]
    z[b[0]] = H - 1
    z[a[Q - 1]] = z[a[0]]; z[a[Q - 3]] = z[a[1]]; z[a[Q - 2]] = z[a[1]]
    s[2] = z >> 4; s[3] = z & 15
    v = s[4:, a[0]]; s[4:, a[Q - 1]] = np.where(v < 100, v + 100, v - 100)
    s[4:, a[Q - 3]] = s[4:, a[1]] - 3; s[4:, a[Q - 2]] = s[4:, a[1]] + 3
    s[:, a[2]] = 0; s[:, b[1]] = np.where(LANE < 4, 0, 3); tag[:, 0] = np.where(LANE < 4, 0, 6)
    c = np.concatenate([b[:1], b[10:]]); tag[:, z[c]] = s[:, c]
    for j in range(8):
        i = int(b[2 + j]); s[:4, i] = np.array([255, 9, 255, 7] if j < 4 else [255, 7, 255, 9])
        u1 = (4080 + int(s[1, i])) & (H - 1); u2 = (4080 + int(s[3, i])) & (H - 1)
        tag[:, (((u1 * u2) >> 5) + (8 * (j & 3) + 1) * u2) & (H - 1)] = s[:, i]
    wear(rng, x, ix, s)
def pack(x, l, tag, ef, w, th):
    b = lambda a, n: np.ascontiguousarray(a).reshape(N, 128, n).astype(np.float32).astype(BF)
    return {"x": b(x, V), "nb": np.stack([gtable(a.reshape(8, -1)) for a in l]), "tag": b(tag, H), "ef": b(ef, H), "w": b(w, 2),
            "th": np.ascontiguousarray(np.repeat(th, 16, axis=1)[:, :, None]).astype(np.int32)}
def setup_inputs(rng):
    x, l, tag, ef, w = parts(rng); s, h, least = start(x, l, w, tag)
    return pack(x, l, tag, ef, w, mid(rng, least))
def setup_inputs_room(rng):
    x, l, tag, ef, w = parts(rng); s, h, least = start(x, l, w, tag); th = np.zeros((N, 8), np.int64)
    for r in range(N):
        for g in range(8):
            n = int(rng.choice(np.array([0, 1, Q - 1, Q, Q + 1, C]))); t = int(rng.choice(np.array([0, 1, 20])))
            if r == 0: n = (Q, Q + 1, Q - 1, 0, 1, C, Q, Q + 1)[g]
            if n == 0:
                th[r, g] = 4080; continue
            used = set(); ids = rng.permutation(C); done = set(plant(rng, s[r, g], h[r, g], tag[r, g], ids, C - n, t, used))
            plant(rng, s[r, g], h[r, g], tag[r, g], [i for i in ids if int(i) not in done], n // 2, t + 1, used); th[r, g] = t
    return pack(x, l, tag, ef, w, th)
def setup_inputs_ties(rng):
    x, l, tag, ef, w = parts(rng); s, h, least = start(x, l, w, tag); th = np.zeros((N, 8), np.int64)
    for r in range(N):
        for g in range(8):
            th[r, g] = int(rng.choice(np.array([0, 1, 20])))
            plant(rng, s[r, g], h[r, g], tag[r, g], rng.permutation(C), C // 2, int(th[r, g]), set(), 2)
    for g in (3, 5): tag[:, g] = tag[:, g, :, :1].copy()
    t = mid(rng, start(x, l, w, tag)[2])
    for g in (3, 5): th[:, g] = t[:, g]
    return pack(x, l, tag, ef, w, th)
def setup_inputs_hash(rng):
    x, l, tag, ef, w = parts(rng)
    w[:, 0, :, 1] = 0; w[:, 1, :, 0] = 0; w[:, 2] = 0; w[:, 2, 5] = np.array([3, 255]); w[:, 3] = 255; w[:, 4, :, 1] = 128
    x[:, 5] = 255 * rng.integers(0, 2, (N, 16, V)); x[:, 6] = rng.integers(0, 256, (N, 16, 1))
    tag[0, 5] = rng.integers(0, 5, (16, H)); tag[1, 5] = 0
    w[:, 7] = 0; w[:, 7, :4] = np.array([[16, 0], [1, 0], [0, 16], [0, 1]]); l[:, 7] = l[:, 7, :1].copy()
    for r in range(N): still(rng, x[r, 7], l[r, 7, 0], tag[r, 7])
    th = mid(rng, start(x, l, w, tag)[2]); th[::2, 5] = np.maximum(th[::2, 5] - 1, 0); th[1::2, 0] = 4080; th[:, 7] = 40
    return pack(x, l, tag, ef, w, th)
def setup_inputs_ends(rng):
    x, l, tag, ef, w = parts(rng)
    l[:, 0] = np.arange(V); l[:, 1] = np.arange(V)[::-1]; l[:, 2] = l[:, 2, :1].copy()
    ef[:, 4] = (17 * LANE)[:, None]; ef[:, 5] = (17 * (15 - LANE))[:, None]; ef[:, 6] = (((LANE + 1) & 15) + 16 * ((LANE + 15) & 15))[:, None]
    q = rng.permutation(N); x[q[2:4]] = rng.integers(0, 8, (2, 8, 16, V)); tag[q[2:4]] = rng.integers(240, 256, (2, 8, 16, H))
    th = mid(rng, start(x, l, w, tag)[2]); th[q[0]] = 0; th[q[1]] = 4080
    return pack(x, l, tag, ef, w, th)
def setup_inputs_spread(rng):
    x, l, tag, ef, w = parts(rng)
    x = (np.exp2(8 * rng.random((N, 8, 1, V))) * rng.random((N, 8, 16, V))).astype(np.int64)
    tag = (np.exp2(8 * rng.random((N, 8, 1, H))) * rng.random((N, 8, 16, H))).astype(np.int64)
    x = np.minimum(x, 255); tag = np.minimum(tag, 255)
    w = np.minimum(np.exp2(8 * rng.random((N, 8, 16, 2))).astype(np.int64), 255)
    return pack(x, l, tag, ef, w, mid(rng, start(x, l, w, tag)[2]))
def check_inputs(d):
    bad = []
    for k, hi in (("x", 255), ("nb", V - 1), ("tag", 255), ("ef", 255), ("w", 255), ("th", 4080)):
        v = np.asarray(d[k]).astype(np.float32)
        if not (np.all(v >= 0) and np.all(v <= hi) and np.all(v == np.floor(v))): bad.append("range of " + k)
    if bad: return bad
    l = np.stack([gentries(a) for a in d["nb"]]).reshape(N, 8, NCL, V)
    if np.any(np.sort(l, axis=-1) != np.arange(V)): bad.append("sites of a class all different")
    b = np.asarray(d["ef"]).astype(np.float32).astype(np.int64).reshape(N, 8, 16, H); e = b & 15; f = b >> 4
    if np.any(np.sort(e, axis=2) != LANE[:, None]) or np.any(np.take_along_axis(f, e, 2) != LANE[:, None]): bad.append("e a permutation, f its inverse")
    t = np.asarray(d["th"]).reshape(N, 8, 16)
    if np.any(t != t[:, :, :1]): bad.append("th alike in a group")
    return bad
def reference(x, nb, tag, ef, w, th):
    whole = lambda a, n: a.astype(np.float32).astype(np.int64).reshape(N, 8, 16, n)
    xs, tg, pf, ws = whole(x, V), whole(tag, H), whole(ef, H), whole(w, 2)
    lim = th.astype(np.int64).reshape(N, 8, 16)[:, :, :1]
    l = np.stack([gentries(a) for a in nb]).astype(np.int64).reshape(N, 8, NCL, V)
    cl = [r % NCL for r in range(N)]
    for t in range(ST):
        sig, home, miss = [], [], []
        for r in range(N):
            ix = l[r, :, cl[r]]; a, s = look(xs[r], ix)
            h, least, hs = best(s, ws[r], tg[r]); hit = least <= lim[r]
            f = np.take_along_axis(pf[r] >> 4, hs[:, None, :], 2)
            f = np.where(hit[:, None, :], f, LANE[:, None])
            a = np.take_along_axis(a, f.transpose(0, 2, 1)[:, None, :, :], 3).reshape(8, 16, V)
            for g in range(8): xs[r, g][:, ix[g]] = a[g]
            sig.append(s); home.append(h[:, 0]); miss.append(~hit); cl[r] = int(np.sum(least)) & (NCL - 1)
        new = []
        for r in range(N):
            q = (r + 1 + t % (N - 1)) % N
            far = best(sig[r], ws[q], tg[q])[2]; back = np.take_along_axis(pf[q], far[:, None, :], 2)
            for g in range(8):
                i = np.flatnonzero(miss[r][g])[:Q]
                col, first = np.unique(home[r][g, i], return_index=True); i = i[first]
                new.append((r, g, col, sig[r][g][:, i], back[g][:, i]))
        for r, g, col, s, b in new:
            tg[r, g][:, col] = s; pf[r, g][:, col] = (b >> 4) + 16 * (b & 15)
    return {"y": xs.reshape(N, 128, V).astype(np.float32).astype(BF)}

@@ -1,0 +1,546 @@
+from concourse.mybir import AluOpType as ALU, ActivationFunctionType as ACT
+
+NR, ST, H = 4, 5, 4096
+MAGIC = 12582912.0
+F32, BF, I32, U16 = "float32", "bfloat16", "int32", "uint16"
+
+
+def _sb(n, d):
+    return ("sbuf", [128, n], d)
+
+
+SCRATCH = {
+    "X": _sb(2048, BF), "A": _sb(2048, BF), "A2": _sb(2048, BF), "MX": _sb(2048, BF), "MN": _sb(2048, BF),
+    "NB": _sb(1024, I32), "NB0": _sb(128, I32), "TAG": _sb(H + 64, BF), "EF": _sb(H + 64, BF),
+    "S8": _sb(1024, BF), "D": _sb(2048, BF), "N2": _sb(2048, BF), "TG": _sb(1024, BF), "AB": _sb(1024, BF),
+    "TG2": _sb(512, BF), "AB2": _sb(512, BF),
+    "WB": _sb(8, BF), "THI": _sb(4, I32), "PC1": _sb(4, I32), "PI": _sb(4, I32), "CF": _sb(24, F32),
+    "I144": _sb(144, F32), "I8": _sb(128, BF), "I16": _sb(128, BF), "KC": _sb(128, BF), "KC2": _sb(16, BF),
+    "BASE": _sb(128, F32), "Z": _sb(144, BF), "ZW1": _sb(144, BF), "ZW2": _sb(144, BF),
+    "WE": _sb(512, BF), "WN": _sb(512, BF), "WF": _sb(256, BF), "IDN": _sb(128, BF), "NEG": _sb(128, BF),
+    "N4K": _sb(128, BF), "CM": _sb(128, BF), "YF": _sb(128, F32), "QB": _sb(128, BF), "U2S": _sb(64, F32),
+    "BR": _sb(2048, BF), "DK": _sb(16, F32), "OB": _sb(128, BF), "LT": _sb(128, BF), "ONES": _sb(128, BF),
+    "MK1": _sb(768, BF), "MK2": _sb(768, BF), "RK": _sb(64, BF), "RK2": _sb(32, BF),
+    "IOT": _sb(16, F32), "IOT0": _sb(16, U16), "SJO": _sb(8, U16), "Q32": _sb(32, U16),
+    "CN": _sb(8, BF), "JK": _sb(256, BF), "AC": _sb(2, F32), "SIG": _sb(8, F32),
+    "DD": _sb(68, F32), "DT": _sb(68, F32), "LL0": _sb(256, U16), "LL1": _sb(256, U16),
+    "UI": _sb(128, I32), "UA": _sb(128, I32), "PR": _sb(64, I32), "FF": _sb(64, I32), "HH": _sb(128, I32),
+    "HA": _sb(128, I32), "HT": _sb(128, U16),
+    "CI": _sb(16, I32), "CA": _sb(16, I32), "CP": _sb(8, I32), "CG": _sb(8, I32),
+    "CI2": _sb(8, I32), "CA2": _sb(8, I32), "CP2": _sb(4, I32), "CG2": _sb(4, I32),
+    "KS": _sb(128, F32), "KEY": _sb(8, I32), "K1": _sb(8, I32), "K2": _sb(8, I32), "K3": _sb(8, I32),
+    "K4": _sb(8, I32), "K5": _sb(8, I32), "K6": _sb(8, U16), "U9": _sb(16, BF),
+    "J2": _sb(4, I32), "J3": _sb(4, I32), "J4": _sb(4, I32), "J6": _sb(2, U16), "KS2": _sb(32, F32),
+    "EV": _sb(128, F32), "IDX": _sb(128, U16),
+    "L7": _sb(8, I32), "L7B": _sb(8, BF), "O1": _sb(16, I32), "O2": _sb(16, I32), "O3": _sb(16, U16),
+    "SJ": _sb(144, BF), "DST": _sb(2, U16),
+    "HS": _sb(64, I32), "HSU": _sb(32, U16), "S16": _sb(512, BF), "T4": _sb(4, I32), "KY2": _sb(4, I32),
+    "G1": _sb(32, I32), "E": _sb(68, F32), "ES": _sb(68, F32), "DU": _sb(2, U16),
+}
+for _t in range(ST - 1):
+    SCRATCH["SQ%d" % _t] = _sb(64, BF)
+    SCRATCH["RP%d" % _t] = _sb(32, I32)
+    SCRATCH["RL%d" % _t] = _sb(32, I32)
+for _n in ("PU", "PA", "PK0", "PK1", "PC", "PD0", "PD1", "PL"):
+    SCRATCH[_n] = ("psum", [128, 512], F32)
+
+SEMAPHORES = (["qv", "qs", "qp", "qg", "d_nb0", "d_w", "d_x", "d_tag", "d_ef", "d_nb", "d_th", "d_y"]
+              + ["req%d" % t for t in range(ST - 1)] + ["rep%d" % t for t in range(ST - 1)]
+              + ["lq%d" % t for t in range(ST - 1)] + ["lp%d" % t for t in range(ST - 1)])
+
+CFG = {
+    "ach": [0, 640, 1280, 1792, 2048],
+    "av": (3,),
+    "av0": (0,),
+    "xch": [0, 256, 640, 1024, 1408, 1728, 2048],
+    "xl": [0, 128, 512, 1280, 2048],
+    "sp": [0, 7],
+    "vp": [(0, 0, 8, 1), (0, 8, 16, 1), (1, 7, 13, 1), (1, 13, 16, 0)],
+    "neng": 8,
+    "cy": 1.04, "g": 1.56, "sc": 3.8, "pe": 0.52, "lat": 90.0, "rem": 3500.0, "win": 40.0, "beta": 1.0,
+    "head": {"learn": 4000.0, "shash": 5000.0, "spre": 2000.0, "sbest": 1000.0, "first": 1000.0, "cls": 1500.0,
+             "cost": -500.0},
+}
+
+
+def issue_order(ops, C):
+    n = len(ops)
+    succ = [[] for _ in range(n)]
+    left = [0] * n
+    for i, o in enumerate(ops):
+        edges = [(d, ops[d]["done"] + C["lat"]) for d in o["deps"] | o["after"]] + [(d, 0.0) for d in o["order"]]
+        left[i] = len(edges)
+        for d, lt in edges:
+            succ[d].append((i, lt))
+    prio = [0.0] * n
+    for i in range(n - 1, -1, -1):
+        prio[i] = ops[i]["c"] + max([lt + prio[j] for j, lt in succ[i]] + [0.0])
+    prio = [prio[i] + C["head"].get(ops[i]["part"], 0.0) for i in range(n)]
+    free, cand = {}, {}
+    rdy = [0.0] * n
+    for i in range(n):
+        free[ops[i]["eng"]] = 0.0
+        cand.setdefault(ops[i]["eng"], [])
+        if left[i] == 0:
+            cand[ops[i]["eng"]].append(i)
+    seq = []
+    while len(seq) < n:
+        t0, e = min((max(free[e], min(rdy[i] for i in cand[e])), e) for e in cand if cand[e])
+        i = max((j for j in cand[e] if rdy[j] <= t0 + C["win"]), key=lambda j: (prio[j], -j))
+        end = t0 + ops[i]["c"]
+        for j in cand[e]:
+            if rdy[j] > t0 + C["win"] and prio[j] > prio[i] and (rdy[j] - t0) * C["beta"] < end - rdy[j]:
+                i = j
+        cand[e].remove(i)
+        free[e] = max(t0, rdy[i]) + ops[i]["c"]
+        seq.append(i)
+        for j, lt in succ[i]:
+            rdy[j] = max(rdy[j], free[e] + lt)
+            left[j] -= 1
+            if left[j] == 0:
+                cand[ops[j]["eng"]].append(j)
+    return seq
+
+
+def rank_program(g, core, T, topo):
+    rank = T.rank_of(core)
+    if rank is None:
+        return
+    C = CFG
+    ACH, NENG, CY = C["ach"], C["neng"], C["cy"]
+    Q = {"v": g.vector, "s": g.scalar, "p": g.tensor, "g": g, "y": g.sync}
+    ops = []
+    last_w, readers, sent = {}, {}, {}
+    part = ["setup"]
+
+    def op(eng, fn, r=(), w=(), sem=None, ext=(), c=64 * CY, done=0.0):
+        me = len(ops)
+        deps = set()
+        for x in r:
+            if x in last_w:
+                deps.add(last_w[x])
+            if x[:2] == "P_":
+                deps.update(q for q in readers.get(x, ()) if ops[q]["eng"] != eng)
+        for x in w:
+            if x in last_w:
+                deps.add(last_w[x])
+            deps.update(readers.get(x, ()))
+        order = set(d for d in deps if eng == "p" and ops[d]["eng"] == "p")
+        after = set(sent[name] for name, _ in ext)
+        ops.append({"eng": eng, "fn": fn, "deps": deps - order, "order": order, "after": after, "sem": sem,
+                    "ext": list(ext), "need": False, "part": part[0], "c": c, "done": done})
+        for x in r:
+            readers.setdefault(x, []).append(me)
+        for x in w:
+            last_w[x] = me
+            readers[x] = []
+        return me
+
+    V, S, P = g.vector, g.scalar, g.tensor
+    cyc = lambda n: max(64, n) * CY
+    gat = lambda n: 55 + n * C["g"] * CY
+    sca = lambda n: 50 + n * C["sc"] * CY
+
+    def ts(out, in0, s1, s2, o0, o1, r, w, c=cyc(64)):
+        if o1 is None:
+            return op("v", lambda: V.tensor_scalar(out, in0, s1, None, o0), r, w, c=c)
+        return op("v", lambda: V.tensor_scalar(out, in0, s1, s2, o0, o1), r, w, c=c)
+
+    def tt(out, a, b, o, r, w, c=cyc(64)):
+        return op("v", lambda: V.tensor_tensor(out, a, b, o), r, w, c=c)
+
+    def cp(out, a, r, w, c=cyc(64), ext=()):
+        return op("v", lambda: V.tensor_copy(out, a), r, w, ext=ext, c=c)
+
+    def ms(out, v, w, c=cyc(64)):
+        return op("v", lambda: V.memset(out, v), (), w, c=c)
+
+    def scan(out, d0, d1, o0, o1, r, w, c=cyc(64)):
+        return op("v", lambda: V.tensor_tensor_scan(out, d0, d1, 0.0, o0, o1), r, w, c=c)
+
+    def act(out, a, f, r, w, c=cyc(64), ext=(), **kw):
+        return op("s", lambda: S.activation(out, a, f, **kw), r, w, ext=ext, c=c)
+
+    def mm(out, l, rhs, st, sp, r, w, n=64, ext=()):
+        return op("p", lambda: P.matmul(out, l, rhs, st, sp), r, w, ext=ext, c=n * C["pe"])
+
+    def iota(out, pat, base, cm, w, n, flag=True):
+        if flag:
+            op("g", lambda: g.iota(out, pat, base, cm, allow_small_or_imprecise_dtypes=True), (), w, c=130 + 2 * n * CY)
+        else:
+            op("g", lambda: g.iota(out, pat, base, cm), (), w, c=130 + 2 * n * CY)
+
+    def dma(eng, out, a, sem, r, w, done, **kw):
+        op(eng, lambda: Q[eng].dma_start(out, a, **kw), r, list(w) + ["Q" + eng], sem=(sem, 16, True), c=100.0, done=done)
+        o = ops[-1]
+        prev = set(d for d in o["deps"] if ops[d]["eng"] == eng and ops[d]["sem"] is not None)
+        o["deps"] = o["deps"] - prev
+        o["order"] = prev
+
+    def send(dst_rank, out, a, rsem, lsem, r):
+        dst = T.cores[dst_rank]
+        rid, pid = topo.addr(dst)[0], topo.addr(dst)[1]
+        m = 0
+        for e in topo.engines(core, dst)[:NENG]:
+            m |= 1 << e
+        sent[rsem] = op("g", lambda: g.remote_dma(out, a, T.sem[rsem], T.sem[lsem], pid, rid, m), r, (),
+                        sem=(lsem, NENG, False), c=500.0, done=C["rem"])
+
+    AND, SHR, ADD, SUB, MUL, MAX, MIN = (ALU.bitwise_and, ALU.logical_shift_right, ALU.add, ALU.subtract, ALU.mult,
+                                         ALU.max, ALU.min)
+    EQ, GE, GT = ALU.is_equal, ALU.is_ge, ALU.is_gt
+    CF = T.CF
+    col = lambda j: CF[:, j:j + 1]
+    cK, cG, cK8, cE, cP, cIQ, c64K, c17K, c2K1, cC0, cC1, cG2, cG21, cZ, cW1, cW2, cV1, cV2, cTH, cM = range(20)
+
+    c0 = rank % 8
+    dma("y", T.X[:], T.x[:], "d_x", (), ["X"], 4200.0)
+    dma("s", T.NB0[:], T.nb[:, c0 * 128:c0 * 128 + 128], "d_nb0", (), ["NB0"], 2400.0)
+    dma("s", T.WB[:, 0:2], T.w[:], "d_w", (), ["WB"], 2400.0)
+    dma("y", T.TAG[:, 0:H], T.tag[:], "d_tag", (), ["TAG"], 8500.0)
+    dma("y", T.EF[:, 0:H], T.ef[:], "d_ef", (), ["EF"], 12500.0)
+    dma("y", T.NB[:], T.nb[:], "d_nb", (), ["NB"], 14500.0)
+
+    iota(T.PC1[:, 0:1], [[0, 1]], 0, 1, ["PC1"], 1, False)
+    iota(T.I144[:], [[1, 144]], 0, 0, ["I144"], 144)
+    iota(T.I8[:], [[1, 16], [0, 8]], 0, 0, ["I8"], 128)
+    iota(T.I16[:], [[1, 8], [0, 16]], 0, 0, ["I16"], 128)
+    iota(T.KC[:], [[16, 2], [0, 8], [2, 8]], 1, 0, ["KC"], 128)
+    iota(T.BASE[:], [[256, 8], [2048, 16]], 0, 0, ["BASE"], 128)
+    dma("g", T.THI[:, 0:1], T.th[:], "d_th", ["BASE"], ["THI"], 4000.0, allow_slow_non_contiguous=True)
+
+    ms(T.MK1[:], 1.0, ["MK1"], cyc(384))
+    ms(T.MK2[:], 0.0, ["MK2"], cyc(384))
+    ms(T.MK1[:, 0:768:16], 0.0, ["MK1"])
+    ms(T.MK2[:, 0:768:16], 256.0, ["MK2"])
+    ts(T.PI[:, 0:1], T.PC1[:, 0:1], 15, None, AND, None, ["PC1"], ["PI0"])
+    ts(T.PI[:, 1:2], T.PC1[:, 0:1], 4, None, SHR, None, ["PC1"], ["PI1"])
+    ts(T.PI[:, 2:3], T.PC1[:, 0:1], 7, None, AND, None, ["PC1"], ["PI2"])
+    ts(T.PI[:, 3:4], T.PC1[:, 0:1], 3, 1, SHR, AND, ["PC1"], ["PI3"])
+    cp(CF[:, 0:4], T.PI[:, 0:4], ["PI0", "PI1", "PI2", "PI3"], ["CF"])
+    cp(col(cP), T.PC1[:, 0:1], ["PC1"], ["cP"])
+    ts(col(cIQ), col(cK8), 16.0, col(cE), MUL, ADD, ["CF"], ["cIQ"])
+    ts(T.IOT[:, 8:16], T.I144[:, 0:128:16], col(cK), None, ADD, None, ["I144", "CF"], ["IOTb"])
+    ts(T.IOT[:, 0:8], T.I144[:, 0:16:2], col(cIQ), None, ADD, None, ["I144", "cIQ"], ["IOTa"])
+    for j, src, sc, bi in ((cG2, cG, 2.0, 0.0), (cG21, cG, 2.0, 1.0), (cZ, cG, 16.0, 15.0), (cC0, cK8, 2.0, 1.0),
+                           (cC1, cK8, 2.0, 17.0), (c64K, cK, 64.0, 0.0), (c17K, cK, 17.0, 0.0), (c2K1, cK, 2.0, 1.0)):
+        act(col(j), col(src), ACT.Identity, ["CF"], ["c%d" % j], scale=sc, bias=bi)
+    cp(T.IOT0[:], T.IOT[:], ["IOTa", "IOTb"], ["IOT0"])
+    cp(T.LL0[:], T.NB0[:, 0:128].indirect(T.IOT0[:, 0:16]), ["NB0", "IOT0"], ["LL0"], gat(256))
+
+    cp(CF[:, cW1:cW1 + 2], T.WB[:, 0:2], ["WB"], ["cW"])
+    ts(CF[:, cV1:cV1 + 2], T.WB[:, 0:2], 1.0 / 32, None, MUL, None, ["WB"], ["cV"])
+    ts(T.Z[:], T.I144[:], col(cZ), 32.0, EQ, MUL, ["I144", "c%d" % cZ], ["Z"], cyc(144))
+    for u in range(2):
+        for e in range(2):
+            j = 2 * u + e
+            ts(T.WE[:, 128 * j:128 * j + 128], T.I8[:], col(cG2 + e), col(cW1 + u), EQ, MUL,
+               ["I8", "c%d" % (cG2 + e), "cW"], ["WE%d" % j])
+        act(T.WN[:, 256 * u:256 * u + 256], T.WE[:, 256 * u:256 * u + 256], ACT.Copy,
+            ["WE%d" % (2 * u), "WE%d" % (2 * u + 1)], ["WN%d" % u], cyc(256), scale=-1.0)
+        ts(T.WF[:, 128 * u:128 * u + 128], T.I16[:], col(cG), col(cW1 + u), EQ, MUL, ["I16", "CF", "cW"], ["WF%d" % u])
+    act(T.ZW1[:], T.Z[:], ACT.Copy, ["Z", "cV"], ["ZW0"], cyc(144), scale=col(cV1))
+    act(T.ZW2[:], T.Z[:], ACT.Copy, ["Z", "cV"], ["ZW1"], cyc(144), scale=col(cV2))
+    ts(T.IDN[:], T.I144[:, 0:128], col(cP), None, EQ, None, ["I144", "cP"], ["IDN"], cyc(128))
+    act(T.NEG[:], T.IDN[:], ACT.Copy, ["IDN"], ["NEG"], cyc(128), scale=-1.0)
+    ms(T.RK[:], 0.0, ["RK"])
+    ms(T.RK[:, 0:64:8], 262144.0, ["RK"])
+    ms(T.RK2[:], 0.0, ["RK2"])
+    ms(T.RK2[:, 0:32:16], 262144.0, ["RK2"])
+    ts(T.DK[:], T.I144[:, 0:16], col(cK), 4096.0, EQ, MUL, ["I144", "CF"], ["DK"])
+    ts(T.OB[:], T.I16[:], col(cG), 1.0 / 4096, EQ, MUL, ["I16", "CF"], ["OB"])
+    op("g", lambda: g.affine_select(T.LT[:], T.OB[:], [[1, 128]], GE, 0.0, 0, -1), ["OB"], ["LT"], c=450.0)
+    ms(T.ONES[:], 128.0, ["ONES"])
+    for a in range(16):
+        act(T.BR[:, 128 * a:128 * a + 128], T.OB[:], ACT.Copy, ["OB", "DK"], ["BR%d" % a], cyc(128),
+            scale=T.DK[:, a:a + 1])
+    ts(T.SJO[:], T.I144[:, 0:64:8], col(c64K), None, ADD, None, ["I144", "c%d" % c64K], ["SJO"])
+    act(T.EF[:, H:H + 64], T.I144[:, 0:64], ACT.Identity, ["I144", "c%d" % c17K], ["EFt"], scale=0.0, bias=col(c17K))
+    ms(T.U9[:], 0.0, ["U9"])
+    ms(T.SJ[:, 128:144], 0.0, ["SJt"])
+    ts(col(cTH), T.THI[:, 0:1], 32.0, 31.0, MUL, ADD, ["THI"], ["cTH"])
+    act(T.SIG[:, 0:2], T.I144[:, 0:32:16], ACT.Identity, ["I144", "CF"], ["SIG"], bias=col(cK))
+    for j, v in ((1, 1.0), (2, 4097.0), (3, 0.5)):
+        act(T.SIG[:, 2 * j:2 * j + 2], T.SIG[:, 0:2], ACT.Identity, ["SIG"], ["SIG%d" % j], bias=v)
+    act(T.KC2[:], T.I144[:, 1:32:2], ACT.Copy, ["I144"], ["KC2"])
+    cp(T.Q32[:], T.I144[:, 0:32], ["I144"], ["Q32"])
+    act(T.N4K[:], T.IDN[:], ACT.Copy, ["IDN"], ["N4K"], cyc(128), scale=-4096.0)
+    ts(col(cM), col(cP), 0.0, -16.0, EQ, MUL, ["cP"], ["cM"])
+    ts(col(cM + 1), col(cP), 1.0, 1.0 / 256, EQ, MUL, ["cP"], ["cM1"])
+    act(T.CM[:], T.IDN[:], ACT.Identity, ["IDN", "cM"], ["CM"], cyc(128), scale=0.0, bias=col(cM))
+    ts(T.CM[:], T.CM[:], col(cM + 1), None, ADD, None, ["CM", "cM1"], ["CM"])
+    ms(T.T4[:, 2:4], 1, ["T4b"])
+    for s in range(2):
+        ts(T.DT[:, 34 * s:34 * s + 34], T.I144[:, 0:34], T.SIG[:, 2 + s:3 + s], T.SIG[:, 4 + s:5 + s], EQ, MUL,
+           ["I144", "SIG1", "SIG2"], ["DT%d" % s])
+    ms(T.TAG[:, H:H + 64], 0.0, ["TAGt"])
+    act(T.DD[:], T.DT[:], ACT.Identity, ["DT0", "DT1"], ["DD"], bias=1.0)
+    ms(T.DD[:, 0:68:34], 0.0, ["DD"])
+
+    sel = lambda buf, a: buf[:, 15 - a:143 - a]
+    AN = ["A%d" % i for i in range(len(ACH) - 1)]
+    MXN = ["MX%d" % i for i in range(len(ACH) - 1)]
+    MNN = ["MN%d" % i for i in range(len(ACH) - 1)]
+    S8N = ["s8_%d" % k for k in range(8)]
+    W = T.TAG[:, 0:H]
+
+    def compact(rhs_of, n, r, sfx, ext=()):
+        CI, CA, CP, CG = T["CI" + sfx], T["CA" + sfx], T["CP" + sfx], T["CG" + sfx]
+        for u, buf in enumerate((T.ZW1, T.ZW2)):
+            for a in range(16):
+                mm(T.PC[:, u * n:u * n + n], sel(buf, a), rhs_of(a), a == 0, a == 15, r + ["ZW%d" % u], ["P_C"], 64, ext)
+        cp(CI[:], T.PC[:, 0:2 * n], ["P_C"], ["CI" + sfx])
+        ts(CA[:], CI[:], H - 1, None, AND, None, ["CI" + sfx], ["CA" + sfx])
+        tt(CP[:], CA[:, 0:n], CA[:, n:2 * n], MUL, ["CA" + sfx], ["CP" + sfx])
+        ts(CG[:], CP[:], 5, H - 1, SHR, AND, ["CP" + sfx], ["CG" + sfx])
+
+    def serve(t):
+        SQ, RP = T["SQ%d" % t], T["RP%d" % t]
+        arr = [("req%d" % t, NENG)]
+        own = "SQo%d" % t
+        part[0] = "shash"
+        for bank, bn in ((T.PU, "P_U"), (T.PL, "P_L")):
+            if bn == "P_U":
+                mm(bank[:, 0:128], T.ONES[:], T.CM[:], True, False, ["ONES", "CM"], [bn], 128)
+            else:
+                mm(bank[:, 0:128], T.N4K[:], T.QB[:], True, False, ["N4K", "QB"], [bn], 128)
+            for u in range(2):
+                mm(bank[:, 64 * u:64 * u + 64], T.WF[:, 128 * u:128 * u + 128], SQ[:, 0:64], False, u == 1,
+                   [own, "WF%d" % u], [bn], 64, arr)
+            if bn == "P_U":
+                act(T.YF[:], T.PU[:, 0:128], ACT.Identity, ["P_U"], ["YF"], cyc(128), scale=1.0 / 4096, bias=MAGIC)
+                act(T.QB[:], T.YF[:], ACT.Identity, ["YF"], ["QB"], cyc(128), bias=-MAGIC)
+        act(T.U2S[:], T.PL[:, 64:128], ACT.Copy, ["P_L"], ["U2S"])
+        tt(T.PR[:], T.PL[:, 0:64], T.U2S[:], MUL, ["P_L", "U2S"], ["PR"])
+        act(T.PA[:, 0:32], T.U2S[:, 0:32], ACT.Copy, ["U2S", "c%d" % c2K1], ["P_A"], scale=col(c2K1))
+        z = act(T.PA[:, 32:64], T.U2S[:, 32:64], ACT.Copy, ["U2S"], ["P_A"])
+        y = act(T.S16[:], SQ[:, 0:32].indirect(T.Q32[:, 0:32]), ACT.Copy, ["Q32"], ["S16"], gat(512), arr)
+        ops[y]["order"] = {z}
+        mm(T.PD0[:, 0:512], T.NEG[:], T.S16[:], True, False, ["NEG", "S16"], ["P_D0"], 512)
+        ts(T.FF[:], T.PR[:], 5, H - 1, SHR, AND, ["PR"], ["FF"])
+        tt(T.HH[:, 0:64], T.FF[:], T.PA[:, 0:64], ADD, ["FF", "P_A"], ["HH0"])
+        ts(T.HS[:], T.HH[:, 0:64], H - 1, None, AND, None, ["HH0"], ["HS"])
+        cp(T.HSU[:], T.HS[:, 0:32], ["HS"], ["HSU"])
+        act(T.TG2[:], W.indirect(T.HSU[:, 0:32]), ACT.Copy, ["TAG", "HSU"], ["TGs"], gat(512))
+        mm(T.PD0[:, 0:512], T.IDN[:], T.TG2[:], False, True, ["IDN", "TGs"], ["P_D0"], 512)
+        act(T.AB2[:], T.PD0[:, 0:512], ACT.Abs, ["P_D0"], ["ABs"], cyc(512))
+        for b in range(2):
+            o = T.PK0[:, 16 * b:16 * b + 16]
+            mm(o, T.IDN[:], T.KC2[:], True, False, ["IDN", "KC2"], ["P_K0"])
+            for a in range(16):
+                j = 16 * (16 * b + a)
+                mm(o, sel(T.Z, a), T.AB2[:, j:j + 16], False, a == 15, ["Z", "ABs"], ["P_K0"])
+        part[0] = "spre"
+        compact(lambda a: SQ[:, a:64:16], 4, [own], "2", arr)
+        part[0] = "sbest"
+        scan(T.KS2[:], T.RK2[:], T.PK0[:, 0:32], ADD, MIN, ["RK2", "P_K0"], ["KS2"])
+        cp(T.KY2[:, 0:2], T.KS2[:, 15:32:16], ["KS2"], ["KY2"])
+        ts(T.T4[:, 0:2], T.KY2[:, 0:2], 31, None, AND, None, ["KY2"], ["T4a"])
+        tt(T.J2[:], T.T4[:], T.CA2[:, 4:8], MUL, ["T4a", "T4b", "CA2"], ["J2"])
+        tt(T.J3[:], T.J2[:], T.CG2[:], ADD, ["J2", "CG2"], ["J3"])
+        ts(T.J4[:], T.J3[:], H - 1, None, AND, None, ["J3"], ["J4"])
+        cp(T.J6[:], T.J4[:, 0:2], ["J4"], ["J6"])
+        ts(T.G1[:], T.EF[:, 0:H].indirect(T.J6[:, 0:2]), 257.0, None, MUL, None, ["EF", "J6"], ["G1"], gat(32))
+        ts(RP[:], T.G1[:], 4, 255, SHR, AND, ["G1"], ["RP%d" % t])
+        send((rank - 1 - t % (NR - 1)) % NR, T["RL%d" % t][:], RP[:], "rep%d" % t, "lp%d" % t, ["RP%d" % t])
+        part[0] = "first"
+        ts(T.E[:, 33:68:34], T.J4[:, 2:4], 1.0, None, ADD, None, ["J4"], ["Eh"])
+        for s in range(2):
+            ts(T.E[:, 34 * s + 1:34 * s + 33], T.HS[:, 32:64], T.E[:, 34 * s + 33:34 * s + 34], -1.0, SUB, EQ,
+               ["HS", "Eh"], ["Ee%d" % s])
+        scan(T.ES[:], T.DD[:], T.E[:], MUL, MAX, ["DD", "Ee0", "Ee1", "Eh", "Ei"], ["ES"], cyc(68))
+        ts(T.DU[:], T.ES[:, 33:68:34], -1.0, None, ADD, None, ["ES"], ["DU"])
+        cp(T.TAG[:, 0:H + 64].indirect(T.DU[:, 0:2]), SQ[:, 32:64], ["DU", own], ["TAG", "TAGt"], sca(32))
+        part[0] = "efw"
+        cp(T.EF[:, 0:H + 64].indirect(T.DU[:, 0:2]), T["RL%d" % t][:], ["DU"], ["EF", "EFt"], sca(32),
+           [("rep%d" % t, NENG)])
+
+    def kmm(h, buf, off, a0, a1, name, stop):
+        for a in range(a0, a1):
+            j = 64 * a + off
+            mm(T["PK%d" % h][:, 0:64], sel(T.Z, a), buf[:, j:j + 64], False, stop and a == a1 - 1, ["Z", name],
+               ["P_K%d" % h])
+
+    def spiece(i, a0, a1):
+        x, y = 64 * a0, 64 * a1
+        PD, pn = T["PD%d" % (i % 2)], "P_D%d" % (i % 2)
+        mm(PD[:, 0:y - x], T.NEG[:], T.S8[:, x:y], True, False, ["NEG"] + S8N, [pn], y - x)
+        act(T.TG[:, x:y], W.indirect(T.HT[:, 64 + 4 * a0:64 + 4 * a1]), ACT.Copy, ["TAG", "HT1"], ["TG%d" % i],
+            gat(y - x))
+        mm(PD[:, 0:y - x], T.IDN[:], T.TG[:, x:y], False, True, ["IDN", "TG%d" % i], [pn], y - x)
+        act(T.AB[:, x:y], PD[:, 0:y - x], ACT.Abs, [pn], ["AB%d" % i], cyc(y - x))
+
+    def vpiece(i, before, h, a0, a1, on_scalar):
+        x, y = 64 * a0 + 1024 * h, 64 * a1 + 1024 * h
+        z = tt(T.D[:, x:y], W.indirect(T.HT[:, 64 * h + 4 * a0:64 * h + 4 * a1]), T.S8[:, 64 * a0:64 * a1], SUB,
+               ["TAG", "HT%d" % h] + S8N, ["D%d" % i], gat(y - x))
+        ops[z]["order"] = set(before)
+        if on_scalar:
+            act(T.N2[:, x:y], T.D[:, x:y], ACT.Abs, ["D%d" % i], ["N%d" % i], cyc(y - x))
+            return z
+        return ts(T.N2[:, x:y], T.D[:, x:y], 0.0, -2.0, MIN, MUL, ["D%d" % i], ["N%d" % i], cyc((y - x) // 2))
+
+    for t in range(ST):
+        last = t == ST - 1
+        LL, ln = T["LL%d" % (t % 2)], "LL%d" % (t % 2)
+        LN, lnn = T["LL%d" % ((t + 1) % 2)], "LL%d" % ((t + 1) % 2)
+        part[0] = "sig"
+        for i in range(len(ACH) - 1):
+            a, b = ACH[i], ACH[i + 1]
+            src = T.X[:, 0:2048].indirect(LL[:, a // 16:b // 16])
+            if i in (C["av0"] if t == 0 else C["av"]):
+                cp(T.A[:, a:b], src, ["X", ln], [AN[i]], gat(b - a))
+            else:
+                act(T.A[:, a:b], src, ACT.Copy, ["X", ln], [AN[i]], gat(b - a))
+            scan(T.MX[:, a:b], T.MK1[:, 0:b - a], T.A[:, a:b], MUL, MAX, ["MK1", AN[i]], [MXN[i]], cyc((b - a) // 2))
+            scan(T.MN[:, a:b], T.MK2[:, 0:b - a], T.A[:, a:b], ADD, MIN, ["MK2", AN[i]], [MNN[i]], cyc((b - a) // 2))
+            mm(T.PD1[:, a // 16:b // 16], T.IDN[:], T.MX[:, a + 15:b:16], True, False, ["IDN", MXN[i]], ["P_D1"])
+            mm(T.PD1[:, a // 16:b // 16], T.NEG[:], T.MN[:, a + 15:b:16], False, True, ["NEG", MNN[i]], ["P_D1"])
+        part[0] = "hash"
+        for u in range(2):
+            for z, (wb, xb, rn) in enumerate(((T.WE, T.MX, MXN), (T.WN, T.MN, MNN))):
+                for e in range(2):
+                    j = 2 * u + e
+                    mm(T.PU[:, 64 * u:64 * u + 64], wb[:, 128 * j:128 * j + 128], xb[:, 16 * e + 15:2048:32],
+                       z + e == 0, z + e == 2, rn + ["WE%d" % j, "WN%d" % u], ["P_U"])
+        for k in range(8):
+            act(T.S8[:, k:1024:8], T.PD1[:, 0:128], ACT.Copy, ["P_D1"], ["s8_%d" % k], cyc(128))
+        cp(T.UI[:], T.PU[:, 0:128], ["P_U"], ["UI"], cyc(128))
+        ts(T.UA[:], T.UI[:], H - 1, None, AND, None, ["UI"], ["UA"], cyc(128))
+        tt(T.PR[:], T.UA[:, 0:64], T.UA[:, 64:128], MUL, ["UA"], ["PR"], cyc(128))
+        for h in range(2):
+            ts(T.PA[:, 64 * h:64 * h + 64], T.UA[:, 64:128], col(cC0 + h), None, MUL, None, ["UA", "c%d" % (cC0 + h)],
+               ["VA%d" % h] + ["P_A"][:1 - h])
+        ts(T.FF[:], T.PR[:], 5, H - 1, SHR, AND, ["PR"], ["FF"])
+        for h in (1, 0):
+            tt(T.HH[:, 64 * h:64 * h + 64], T.FF[:], T.PA[:, 64 * h:64 * h + 64], ADD, ["FF", "VA%d" % h, "P_A"],
+               ["HH%d" % h])
+            ts(T.HA[:, 64 * h:64 * h + 64], T.HH[:, 64 * h:64 * h + 64], H - 1, None, AND, None, ["HH%d" % h],
+               ["HA%d" % h])
+            cp(T.HT[:, 64 * h:64 * h + 64], T.HA[:, 64 * h:64 * h + 64], ["HA%d" % h], ["HT%d" % h])
+        part[0] = "pre"
+        compact(lambda a: T.S8[:, 64 * a:64 * a + 64:8], 8, ["s8_0"], "")
+        part[0] = "cost"
+        for h in range(2):
+            mm(T["PK%d" % h][:, 0:64], T.IDN[:], T.KC[:, 64 * h:64 * h + 64], True, False, ["IDN", "KC"], ["P_K%d" % h])
+        SP, VP = C["sp"], C["vp"]
+        for i in range(len(SP) - 1):
+            spiece(i, SP[i], SP[i + 1])
+        before = []
+        for i, z in enumerate(VP):
+            before = [vpiece(i, before, *z)]
+        for h in range(2):
+            todo = [(T.AB, 0, SP[i], SP[i + 1], "AB%d" % i) for i in range(len(SP) - 1) if h == 1]
+            for i, (hh, a0, a1, on_scalar) in enumerate(VP):
+                if hh == h:
+                    todo += [(T.D, 1024 * h, a0, a1, "D%d" % i)][:1 - on_scalar] + [(T.N2, 1024 * h, a0, a1, "N%d" % i)]
+            for i, z in enumerate(todo):
+                kmm(h, z[0], z[1], z[2], z[3], z[4], i == len(todo) - 1)
+        if not last:
+            act(T.SJ[:, 0:128], T.S8[:, 0:1024].indirect(T.SJO[:, 0:8]), ACT.Copy, S8N + ["SJO"], ["SJ"], gat(128))
+        scan(T.KS[:, 0:64], T.RK[:], T.PK0[:, 0:64], ADD, MIN, ["RK", "P_K0"], ["KS0"])
+        scan(T.KS[:, 64:128], T.RK[:], T.PK1[:, 0:64], ADD, MIN, ["RK", "P_K1"], ["KS1"])
+        tt(T.KEY[:], T.KS[:, 7:64:8], T.KS[:, 71:128:8], MIN, ["KS0", "KS1"], ["KEY"])
+        part[0] = "best"
+        ts(T.K1[:], T.KEY[:], 31, None, AND, None, ["KEY"], ["K1"])
+        ts(T.U9[:, 8:16], T.KEY[:], col(cTH), 4096.0, GT, MUL, ["KEY", "cTH"], ["U9"])
+        tt(T.K2[:], T.K1[:], T.CA[:, 8:16], MUL, ["K1", "CA"], ["K2"])
+        tt(T.K3[:], T.K2[:], T.CG[:], ADD, ["K2", "CG"], ["K3"])
+        ts(T.K4[:], T.K3[:], H - 1, None, AND, None, ["K3"], ["K4"])
+        tt(T.K5[:], T.K4[:], T.U9[:, 8:16], MAX, ["K4", "U9"], ["K5"])
+        cp(T.K6[:], T.K5[:], ["K5"], ["K6"])
+        tt(T.EV[:], T.EF[:, 0:H + 16].indirect(T.K6[:, 0:8]), T.BASE[:], ADD, ["EF", "EFt", "K6", "BASE"], ["EV"],
+           gat(128))
+        ts(T.IDX[:], T.EV[:], 1.0 / 16, -15.0 / 32, MUL, ADD, ["EV"], ["IDX"], cyc(128))
+        part[0] = "move"
+        XCH = C["xl"] if last else C["xch"]
+        for i in range(len(XCH) - 1):
+            a, b = XCH[i], XCH[i + 1]
+            act(T.A2[:, a:b], T.A[:, 0:2048].indirect(T.IDX[:, a // 16:b // 16]), ACT.Copy, AN + ["IDX", "X0"],
+                ["B%d" % i], gat(b - a))
+            cp(T.X[:, 0:2048].indirect(LL[:, 128 + a // 16:128 + b // 16]), T.A2[:, a:b], [ln, "B%d" % i], ["X"],
+               sca(b - a))
+        last_w["X0"] = last_w["X"]
+        if last:
+            break
+        part[0] = "learn"
+        mm(T.PL[:, 0:8], T.LT[:], T.U9[:, 8:16], True, False, ["LT", "U9"], ["P_L"])
+        for d in range(1, 8):
+            mm(T.PL[:, 0:8], T.OB[:], T.U9[:, 8 - d:16 - d], False, d == 7, ["OB", "U9"], ["P_L"])
+        act(T.CN[:], T.PL[:, 0:8], ACT.Copy, ["P_L"], ["CN"])
+        for a in range(16):
+            mm(T.PL[:, 128 + 8 * a:136 + 8 * a], T.BR[:, 128 * a:128 * a + 128], T.CN[:], True, True,
+               ["BR%d" % a, "CN"], ["P_L"])
+        for sl in range(2):
+            act(T.JK[:, 128 * sl:128 * sl + 128], T.PL[:, 128:256], ACT.Sign, ["P_L", "SIG3"], ["AC%d" % sl],
+                cyc(128) + 20, scale=-1.0, bias=T.SIG[:, 6 + sl:7 + sl], accum_out=T.AC[:, sl:sl + 1])
+        ts(T.DST[:], T.AC[:], 0.5, 64.0, MUL, ADD, ["AC0", "AC1"], ["DST"])
+        SQ = T["SQ%d" % t]
+        act(SQ[:, 32:64], T.SJ[:, 0:144].indirect(T.DST[:, 0:2]), ACT.Copy, ["DST", "SJ", "SJt"], ["SQo%d" % t], gat(32))
+        send((rank + 1 + t % (NR - 1)) % NR, SQ[:, 0:32], SQ[:, 32:64], "req%d" % t, "lq%d" % t, ["SQo%d" % t])
+        ts(T.E[:, 0:68:34], T.AC[:], 128.0, None, GE, None, ["AC0", "AC1"], ["Ei"])
+        part[0] = "cls"
+        ts(T.L7[:], T.KEY[:], 5, 7, SHR, AND, ["KEY"], ["L7"])
+        cp(T.L7B[:], T.L7[:], ["L7"], ["L7B"])
+        for b in range(8):
+            mm(T.PC[:, 0:1], T.ONES[:], T.L7B[:, b:b + 1], b == 0, b == 7, ["ONES", "L7B"], ["P_C"])
+        ts(T.O1[:], T.IOT[:], T.PC[:, 0:1], None, ADD, None, ["IOTa", "IOTb", "P_C"], ["O1"])
+        ts(T.O2[:], T.O1[:], 1023, None, AND, None, ["O1"], ["O2"])
+        cp(T.O3[:], T.O2[:], ["O2"], ["O3"])
+        cp(LN[:], T.NB[:, 0:1024].indirect(T.O3[:, 0:16]), ["NB", "O3"], [lnn], gat(256))
+        serve(t)
+    dma("y", T.y[:], T.X[:], "d_y", ["X"], (), 3000.0)
+
+    seq = issue_order(ops, C)
+    pos = {}
+    for i in seq:
+        o = ops[i]
+        if o["sem"] is None:
+            pos[o["eng"]] = pos.get(o["eng"], 0) + 1
+            o["pos"] = pos[o["eng"]]
+    at = {i: k for k, i in enumerate(seq)}
+    know = {e: {} for e in Q}
+    for i in seq:
+        o = ops[i]
+        k = know[o["eng"]]
+        waits = []
+        for d in sorted(o["deps"], key=lambda z: -at[z]):
+            x = ops[d]
+            key, val = (x["eng"], x["pos"]) if x["sem"] is None else (x["sem"][0], 1)
+            if k.get(key, 0) >= val:
+                continue
+            waits.append(d)
+            x["need"] = True
+            k[key] = val
+            for kk, vv in x["know"].items():
+                if k.get(kk, 0) < vv:
+                    k[kk] = vv
+        ex = []
+        for name, c in o["ext"]:
+            if k.get(name, 0) < 1:
+                ex.append((name, c))
+                k[name] = 1
+        o["waits"], o["ex"], o["know"] = waits, ex, dict(k)
+    cnt = {}
+    for i in seq:
+        o = ops[i]
+        q = Q[o["eng"]]
+        for d in o["waits"]:
+            x = ops[d]
+            if x["sem"] is None:
+                q.wait_ge(T.sem["q" + x["eng"]], x["cnt"])
+            else:
+                q.wait_ge(T.sem[x["sem"][0]], x["sem"][1])
+        for name, c in o["ex"]:
+            q.wait_ge(T.sem[name], c)
+        ins = o["fn"]()
+        if o["sem"] is None:
+            if o["need"]:
+                cnt[o["eng"]] = cnt.get(o["eng"], 0) + 1
+                o["cnt"] = cnt[o["eng"]]
+                ins.then_inc(T.sem["q" + o["eng"]], 1)
+        elif o["sem"][2]:
+            ins.then_inc(T.sem[o["sem"][0]], 16)
+    for o in ops:
+        if o["sem"] is not None and not o["need"]:
+            Q[o["eng"]].wait_ge(T.sem[o["sem"][0]], o["sem"][1])

@@ -1,8 +1,10 @@
-from concourse.mybir import AluOpType as ALU, ActivationFunctionType as ACT
+from concourse.mybir import AluOpType as ALU, ActivationFunctionType as ACT, AxisListType as AX
 
 NR, ST, H = 4, 5, 4096
-MAGIC = 12582912.0
 F32, BF, I32, U16 = "float32", "bfloat16", "int32", "uint16"
+BIG = 524288.0
+UB = 1048576
+M33 = 12884901888.0
 
 
 def _sb(n, d):
@@ -10,38 +12,36 @@ def _sb(n, d):
 
 
 SCRATCH = {
-    "X": _sb(2048, BF), "A": _sb(2048, BF), "A2": _sb(2048, BF), "MX": _sb(2048, BF), "MN": _sb(2048, BF),
+    "X": _sb(2048, BF), "XF": _sb(2048, F32), "A": _sb(2048, BF), "A2": _sb(2048, F32), "A2B": _sb(2048, BF),
+    "MX": _sb(2048, BF), "MN": _sb(2048, BF), "SP": _sb(2048, BF), "S16": _sb(2048, BF),
     "NB": _sb(1024, I32), "NB0": _sb(128, I32), "TAG": _sb(H + 64, BF), "EF": _sb(H + 64, BF),
-    "S8": _sb(1024, BF), "D": _sb(2048, BF), "N2": _sb(2048, BF), "TG": _sb(1024, BF), "AB": _sb(1024, BF),
-    "TG2": _sb(512, BF), "AB2": _sb(512, BF),
+    "D": _sb(2048, BF), "N2": _sb(2048, BF), "TG2": _sb(512, BF), "M2": _sb(512, BF), "SJ": _sb(128, BF),
     "WB": _sb(8, BF), "THI": _sb(4, I32), "PC1": _sb(4, I32), "PI": _sb(4, I32), "CF": _sb(24, F32),
-    "I144": _sb(144, F32), "I8": _sb(128, BF), "I16": _sb(128, BF), "KC": _sb(128, BF), "KC2": _sb(16, BF),
-    "BASE": _sb(128, F32), "Z": _sb(144, BF), "ZW1": _sb(144, BF), "ZW2": _sb(144, BF),
-    "WE": _sb(512, BF), "WN": _sb(512, BF), "WF": _sb(256, BF), "IDN": _sb(128, BF), "NEG": _sb(128, BF),
-    "N4K": _sb(128, BF), "CM": _sb(128, BF), "YF": _sb(128, F32), "QB": _sb(128, BF), "U2S": _sb(64, F32),
-    "BR": _sb(2048, BF), "DK": _sb(16, F32), "OB": _sb(128, BF), "LT": _sb(128, BF), "ONES": _sb(128, BF),
-    "MK1": _sb(768, BF), "MK2": _sb(768, BF), "RK": _sb(64, BF), "RK2": _sb(32, BF),
-    "IOT": _sb(16, F32), "IOT0": _sb(16, U16), "SJO": _sb(8, U16), "Q32": _sb(32, U16),
-    "CN": _sb(8, BF), "JK": _sb(256, BF), "AC": _sb(2, F32), "SIG": _sb(8, F32),
+    "I144": _sb(144, F32), "I16": _sb(128, BF), "IM": _sb(128, BF), "PR0": _sb(128, BF), "PR1": _sb(128, BF),
+    "PR2": _sb(128, F32), "BASE": _sb(128, F32), "Z": _sb(144, BF), "Z2": _sb(144, BF), "ZN": _sb(144, BF),
+    "ZW1": _sb(144, BF), "ZW2": _sb(144, BF), "WF": _sb(256, BF), "WN": _sb(256, BF), "IDN": _sb(128, BF),
+    "NEG": _sb(128, BF), "N256": _sb(128, BF), "ZR": _sb(128, BF), "OB": _sb(128, BF), "LT": _sb(128, BF),
+    "FOUR": _sb(128, F32), "MK1": _sb(1024, BF), "MK2": _sb(1024, BF), "RK": _sb(128, BF), "RT": _sb(128, BF),
+    "IOT": _sb(16, F32), "IOT0": _sb(16, U16), "CIC": _sb(8, F32), "SIG": _sb(8, F32),
     "DD": _sb(68, F32), "DT": _sb(68, F32), "LL0": _sb(256, U16), "LL1": _sb(256, U16),
-    "UI": _sb(128, I32), "UA": _sb(128, I32), "PR": _sb(64, I32), "FF": _sb(64, I32), "HH": _sb(128, I32),
-    "HA": _sb(128, I32), "HT": _sb(128, U16),
-    "CI": _sb(16, I32), "CA": _sb(16, I32), "CP": _sb(8, I32), "CG": _sb(8, I32),
-    "CI2": _sb(8, I32), "CA2": _sb(8, I32), "CP2": _sb(4, I32), "CG2": _sb(4, I32),
-    "KS": _sb(128, F32), "KEY": _sb(8, I32), "K1": _sb(8, I32), "K2": _sb(8, I32), "K3": _sb(8, I32),
-    "K4": _sb(8, I32), "K5": _sb(8, I32), "K6": _sb(8, U16), "U9": _sb(16, BF),
-    "J2": _sb(4, I32), "J3": _sb(4, I32), "J4": _sb(4, I32), "J6": _sb(2, U16), "KS2": _sb(32, F32),
-    "EV": _sb(128, F32), "IDX": _sb(128, U16),
-    "L7": _sb(8, I32), "L7B": _sb(8, BF), "O1": _sb(16, I32), "O2": _sb(16, I32), "O3": _sb(16, U16),
-    "SJ": _sb(144, BF), "DST": _sb(2, U16),
-    "HS": _sb(64, I32), "HSU": _sb(32, U16), "S16": _sb(512, BF), "T4": _sb(4, I32), "KY2": _sb(4, I32),
+    "UI": _sb(256, I32), "UA": _sb(256, I32), "PR": _sb(128, F32), "P2": _sb(128, I32), "HA": _sb(128, I32),
+    "HT": _sb(128, U16),
+    "VI": _sb(128, I32), "VA": _sb(128, I32), "VR": _sb(64, F32), "V2": _sb(64, I32), "HS": _sb(64, I32),
+    "HSU": _sb(32, U16),
+    "CI": _sb(16, I32), "CA": _sb(16, I32), "CP": _sb(8, I32), "CG": _sb(8, I32), "CH": _sb(8, I32),
+    "CI2": _sb(8, I32), "CA2": _sb(8, I32), "CP2": _sb(4, I32), "CG2": _sb(4, I32), "CH2": _sb(4, I32),
+    "KS": _sb(144, F32), "KT": _sb(128, F32), "K1": _sb(8, F32), "K2": _sb(8, I32), "K3": _sb(8, I32),
+    "K4": _sb(8, I32), "FU": _sb(8, I32), "K6": _sb(16, U16), "U9": _sb(16, BF),
+    "JS": _sb(32, F32), "JT": _sb(32, F32), "J1": _sb(2, F32), "J2": _sb(2, I32), "J3": _sb(2, I32), "J4": _sb(2, I32),
+    "J6": _sb(2, U16), "H0": _sb(2, I32), "EV": _sb(128, F32), "IDX": _sb(128, U16),
+    "RS": _sb(4, F32), "O3": _sb(16, U16), "POI": _sb(8, F32), "POS": _sb(8, U16),
     "G1": _sb(32, I32), "E": _sb(68, F32), "ES": _sb(68, F32), "DU": _sb(2, U16),
 }
 for _t in range(ST - 1):
-    SCRATCH["SQ%d" % _t] = _sb(64, BF)
+    SCRATCH["SQ%d" % _t] = _sb(288, BF)
     SCRATCH["RP%d" % _t] = _sb(32, I32)
     SCRATCH["RL%d" % _t] = _sb(32, I32)
-for _n in ("PU", "PA", "PK0", "PK1", "PC", "PD0", "PD1", "PL"):
+for _n in ("PU0", "PU1", "PK0", "PK1", "PC", "PD0", "PD1", "PS"):
     SCRATCH[_n] = ("psum", [128, 512], F32)
 
 SEMAPHORES = (["qv", "qs", "qp", "qg", "d_nb0", "d_w", "d_x", "d_tag", "d_ef", "d_nb", "d_th", "d_y"]
@@ -49,17 +49,17 @@ SEMAPHORES = (["qv", "qs", "qp", "qg", "d_nb0", "d_w", "d_x", "d_tag", "d_ef", "
               + ["lq%d" % t for t in range(ST - 1)] + ["lp%d" % t for t in range(ST - 1)])
 
 CFG = {
-    "ach": [0, 640, 1280, 1792, 2048],
-    "av": (3,),
-    "av0": (0,),
-    "xch": [0, 256, 640, 1024, 1408, 1728, 2048],
-    "xl": [0, 128, 512, 1280, 2048],
-    "sp": [0, 7],
-    "vp": [(0, 0, 8, 1), (0, 8, 16, 1), (1, 7, 13, 1), (1, 13, 16, 0)],
-    "neng": 8,
-    "cy": 1.04, "g": 1.56, "sc": 3.8, "pe": 0.52, "lat": 90.0, "rem": 3500.0, "win": 40.0, "beta": 1.0,
-    "head": {"learn": 4000.0, "shash": 5000.0, "spre": 2000.0, "sbest": 1000.0, "first": 1000.0, "cls": 1500.0,
-             "cost": -500.0},
+    "parts": [0, 3, 8],
+    "ach": [[("v", 64), ("s", 192), ("s", 256), ("s", 256)], [("s", 448), ("s", 512), ("s", 320)]],
+    "cost": [[("s", 10), ("v", 6)], [("s", 6), ("s", 6), ("v", 2), ("v", 2)]],
+    "kord": {0: [0, 2, 1], 1: [5, 2, 4, 3, 0, 1]},
+    "move": [[256, 192, 320], [448, 832]],
+    "movel": [[256, 512], [1280]],
+    "neng": 16,
+    "cy": 0.95, "g": 1.56, "sc": 3.8, "lat": 150.0, "rem": 3000.0, "win": 40.0, "beta": 1.0,
+    "head": {"move0": -200.0, "cls": -900.0, "spre": 2200.0, "hash1": -200.0, "count": 1500.0, "move1": -3800.0,
+             "learn": 100.0, "scost": 1200.0, "best0": 3000.0, "sig0": 2000.0, "cost0": -500.0, "shash": 2400.0,
+             "first": 1100.0, "sbest": -500.0, "cost1": -1500.0, "pre": -400.0, "efw": -200.0},
 }
 
 
@@ -74,7 +74,7 @@ def issue_order(ops, C):
             succ[d].append((i, lt))
     prio = [0.0] * n
     for i in range(n - 1, -1, -1):
-        prio[i] = ops[i]["c"] + max([lt + prio[j] for j, lt in succ[i]] + [0.0])
+        prio[i] = ops[i]["c"] + max([lt + prio[j] for j, lt in succ[i]] + [ops[i]["done"]])
     prio = [prio[i] + C["head"].get(ops[i]["part"], 0.0) for i in range(n)]
     free, cand = {}, {}
     rdy = [0.0] * n
@@ -107,7 +107,8 @@ def rank_program(g, core, T, topo):
     if rank is None:
         return
     C = CFG
-    ACH, NENG, CY = C["ach"], C["neng"], C["cy"]
+    PARTS, NENG, CY = C["parts"], C["neng"], C["cy"]
+    NP = len(PARTS) - 1
     Q = {"v": g.vector, "s": g.scalar, "p": g.tensor, "g": g, "y": g.sync}
     ops = []
     last_w, readers, sent = {}, {}, {}
@@ -138,8 +139,9 @@ def rank_program(g, core, T, topo):
 
     V, S, P = g.vector, g.scalar, g.tensor
     cyc = lambda n: max(64, n) * CY
-    gat = lambda n: 55 + n * C["g"] * CY
-    sca = lambda n: 50 + n * C["sc"] * CY
+    gat = lambda n: (65 + n * C["g"]) * CY
+    sca = lambda n: (65 + n * C["sc"]) * CY
+    blk = lambda name, a, b, k=64: ["%s.%d" % (name, j) for j in range(a // k, (b + k - 1) // k)]
 
     def ts(out, in0, s1, s2, o0, o1, r, w, c=cyc(64)):
         if o1 is None:
@@ -158,11 +160,11 @@ def rank_program(g, core, T, topo):
     def scan(out, d0, d1, o0, o1, r, w, c=cyc(64)):
         return op("v", lambda: V.tensor_tensor_scan(out, d0, d1, 0.0, o0, o1), r, w, c=c)
 
-    def act(out, a, f, r, w, c=cyc(64), ext=(), **kw):
-        return op("s", lambda: S.activation(out, a, f, **kw), r, w, ext=ext, c=c)
+    def act(out, a, f, r, w, c=cyc(64), **kw):
+        return op("s", lambda: S.activation(out, a, f, **kw), r, w, c=c)
 
     def mm(out, l, rhs, st, sp, r, w, n=64, ext=()):
-        return op("p", lambda: P.matmul(out, l, rhs, st, sp), r, w, ext=ext, c=n * C["pe"])
+        return op("p", lambda: P.matmul(out, l, rhs, st, sp), r, w, ext=ext, c=max(64, n) * 0.5 * CY)
 
     def iota(out, pat, base, cm, w, n, flag=True):
         if flag:
@@ -186,12 +188,17 @@ def rank_program(g, core, T, topo):
         sent[rsem] = op("g", lambda: g.remote_dma(out, a, T.sem[rsem], T.sem[lsem], pid, rid, m), r, (),
                         sem=(lsem, NENG, False), c=500.0, done=C["rem"])
 
-    AND, SHR, ADD, SUB, MUL, MAX, MIN = (ALU.bitwise_and, ALU.logical_shift_right, ALU.add, ALU.subtract, ALU.mult,
-                                         ALU.max, ALU.min)
+    def moved(eng, out, src, add, r, w, n):
+        if eng == "s":
+            return act(out, src, ACT.Identity, r, w, gat(n), bias=add)
+        return ts(out, src, add, None, ADD, None, r, w, gat(n))
+
+    AND, SHR, ASR, ADD, SUB, MUL, MAX, MIN = (ALU.bitwise_and, ALU.logical_shift_right, ALU.arith_shift_right, ALU.add,
+                                              ALU.subtract, ALU.mult, ALU.max, ALU.min)
     EQ, GE, GT = ALU.is_equal, ALU.is_ge, ALU.is_gt
     CF = T.CF
     col = lambda j: CF[:, j:j + 1]
-    cK, cG, cK8, cE, cP, cIQ, c64K, c17K, c2K1, cC0, cC1, cG2, cG21, cZ, cW1, cW2, cV1, cV2, cTH, cM = range(20)
+    cK, cG, cP, c17K, cM, cZ, cW1, cW2, cV1, cV2, cTH = range(11)
 
     c0 = rank % 8
     dma("y", T.X[:], T.x[:], "d_x", (), ["X"], 4200.0)
@@ -203,27 +210,32 @@ def rank_program(g, core, T, topo):
 
     iota(T.PC1[:, 0:1], [[0, 1]], 0, 1, ["PC1"], 1, False)
     iota(T.I144[:], [[1, 144]], 0, 0, ["I144"], 144)
-    iota(T.I8[:], [[1, 16], [0, 8]], 0, 0, ["I8"], 128)
+    iota(T.IM[:], [[0, 8], [1, 16]], 0, 0, ["IM"], 128)
+    for q in range(NP):
+        b0, b1 = PARTS[q], PARTS[q + 1]
+        iota(T.PR0[:, 16 * b0:16 * b1], [[1, 16], [16, b1 - b0]], 16 * b0, 0, ["PR0%d" % q], 16 * (b1 - b0))
     iota(T.I16[:], [[1, 8], [0, 16]], 0, 0, ["I16"], 128)
-    iota(T.KC[:], [[16, 2], [0, 8], [2, 8]], 1, 0, ["KC"], 128)
-    iota(T.BASE[:], [[256, 8], [2048, 16]], 0, 0, ["BASE"], 128)
-    dma("g", T.THI[:, 0:1], T.th[:], "d_th", ["BASE"], ["THI"], 4000.0, allow_slow_non_contiguous=True)
+    dma("g", T.THI[:, 0:1], T.th[:], "d_th", ["I16"], ["THI"], 4000.0, allow_slow_non_contiguous=True)
+    for q in range(NP):
+        b0, b1 = PARTS[q], PARTS[q + 1]
+        iota(T.BASE[:, 16 * b0:16 * b1], [[256, b1 - b0], [256 * (b1 - b0), 16]], 0, 0, ["BASE%d" % q], 16 * (b1 - b0))
 
-    ms(T.MK1[:], 1.0, ["MK1"], cyc(384))
-    ms(T.MK2[:], 0.0, ["MK2"], cyc(384))
-    ms(T.MK1[:, 0:768:16], 0.0, ["MK1"])
-    ms(T.MK2[:, 0:768:16], 256.0, ["MK2"])
+    ms(T.MK1[:], 1.0, ["MK1"], cyc(512))
+    ms(T.MK2[:], 0.0, ["MK2"], cyc(512))
+    ms(T.MK1[:, 0:1024:16], 0.0, ["MK1"])
+    ms(T.MK2[:, 0:1024:16], 512.0, ["MK2"])
+    ms(T.SP[:], 0.0, blk("SP", 0, 128, 16), cyc(1024))
+    act(T.XF[:], T.SP[:], ACT.Silu, blk("SP", 0, 128, 16), ["XF"], cyc(2048) + 1300)
     ts(T.PI[:, 0:1], T.PC1[:, 0:1], 15, None, AND, None, ["PC1"], ["PI0"])
     ts(T.PI[:, 1:2], T.PC1[:, 0:1], 4, None, SHR, None, ["PC1"], ["PI1"])
-    ts(T.PI[:, 2:3], T.PC1[:, 0:1], 7, None, AND, None, ["PC1"], ["PI2"])
-    ts(T.PI[:, 3:4], T.PC1[:, 0:1], 3, 1, SHR, AND, ["PC1"], ["PI3"])
-    cp(CF[:, 0:4], T.PI[:, 0:4], ["PI0", "PI1", "PI2", "PI3"], ["CF"])
+    cp(CF[:, 0:2], T.PI[:, 0:2], ["PI0", "PI1"], ["CF"])
     cp(col(cP), T.PC1[:, 0:1], ["PC1"], ["cP"])
-    ts(col(cIQ), col(cK8), 16.0, col(cE), MUL, ADD, ["CF"], ["cIQ"])
+    ts(T.PR1[:], T.IM[:], col(cK), None, EQ, None, ["IM", "CF"], ["PR1"])
+    tt(T.PR2[:], T.PR1[:], T.PR0[:], MUL, ["PR1"] + ["PR0%d" % q for q in range(NP)], ["PR2"], cyc(256))
+    scan(T.EV[:], T.MK1[:, 0:128], T.PR2[:], MUL, ADD, ["MK1", "PR2"], blk("EV", 0, 128, 16), cyc(128))
+    cp(T.IOT[:, 0:8], T.EV[:, 15:128:16], blk("EV", 0, 128, 16), ["IOTa"])
     ts(T.IOT[:, 8:16], T.I144[:, 0:128:16], col(cK), None, ADD, None, ["I144", "CF"], ["IOTb"])
-    ts(T.IOT[:, 0:8], T.I144[:, 0:16:2], col(cIQ), None, ADD, None, ["I144", "cIQ"], ["IOTa"])
-    for j, src, sc, bi in ((cG2, cG, 2.0, 0.0), (cG21, cG, 2.0, 1.0), (cZ, cG, 16.0, 15.0), (cC0, cK8, 2.0, 1.0),
-                           (cC1, cK8, 2.0, 17.0), (c64K, cK, 64.0, 0.0), (c17K, cK, 17.0, 0.0), (c2K1, cK, 2.0, 1.0)):
+    for j, src, sc, bi in ((cZ, cG, 16.0, 15.0), (c17K, cK, 17.0, 0.0), (cM, cK, -64.0, 992.0)):
         act(col(j), col(src), ACT.Identity, ["CF"], ["c%d" % j], scale=sc, bias=bi)
     cp(T.IOT0[:], T.IOT[:], ["IOTa", "IOTb"], ["IOT0"])
     cp(T.LL0[:], T.NB0[:, 0:128].indirect(T.IOT0[:, 0:16]), ["NB0", "IOT0"], ["LL0"], gat(256))
@@ -232,122 +244,107 @@ def rank_program(g, core, T, topo):
     ts(CF[:, cV1:cV1 + 2], T.WB[:, 0:2], 1.0 / 32, None, MUL, None, ["WB"], ["cV"])
     ts(T.Z[:], T.I144[:], col(cZ), 32.0, EQ, MUL, ["I144", "c%d" % cZ], ["Z"], cyc(144))
     for u in range(2):
-        for e in range(2):
-            j = 2 * u + e
-            ts(T.WE[:, 128 * j:128 * j + 128], T.I8[:], col(cG2 + e), col(cW1 + u), EQ, MUL,
-               ["I8", "c%d" % (cG2 + e), "cW"], ["WE%d" % j])
-        act(T.WN[:, 256 * u:256 * u + 256], T.WE[:, 256 * u:256 * u + 256], ACT.Copy,
-            ["WE%d" % (2 * u), "WE%d" % (2 * u + 1)], ["WN%d" % u], cyc(256), scale=-1.0)
         ts(T.WF[:, 128 * u:128 * u + 128], T.I16[:], col(cG), col(cW1 + u), EQ, MUL, ["I16", "CF", "cW"], ["WF%d" % u])
+    act(T.WN[:], T.WF[:], ACT.Copy, ["WF0", "WF1"], ["WN"], cyc(256), scale=-1.0)
     act(T.ZW1[:], T.Z[:], ACT.Copy, ["Z", "cV"], ["ZW0"], cyc(144), scale=col(cV1))
     act(T.ZW2[:], T.Z[:], ACT.Copy, ["Z", "cV"], ["ZW1"], cyc(144), scale=col(cV2))
+    act(T.Z2[:], T.Z[:], ACT.Copy, ["Z"], ["Z2"], cyc(144), scale=2.0)
+    act(T.ZN[:], T.Z[:], ACT.Copy, ["Z"], ["ZN"], cyc(144), scale=-1.0)
     ts(T.IDN[:], T.I144[:, 0:128], col(cP), None, EQ, None, ["I144", "cP"], ["IDN"], cyc(128))
     act(T.NEG[:], T.IDN[:], ACT.Copy, ["IDN"], ["NEG"], cyc(128), scale=-1.0)
-    ms(T.RK[:], 0.0, ["RK"])
-    ms(T.RK[:, 0:64:8], 262144.0, ["RK"])
-    ms(T.RK2[:], 0.0, ["RK2"])
-    ms(T.RK2[:, 0:32:16], 262144.0, ["RK2"])
-    ts(T.DK[:], T.I144[:, 0:16], col(cK), 4096.0, EQ, MUL, ["I144", "CF"], ["DK"])
-    ts(T.OB[:], T.I16[:], col(cG), 1.0 / 4096, EQ, MUL, ["I16", "CF"], ["OB"])
+    act(T.N256[:], T.IDN[:], ACT.Copy, ["IDN"], ["N256"], cyc(128), scale=-256.0 / UB)
+    act(T.ZR[:], T.IDN[:], ACT.Copy, ["IDN"], ["ZR"], cyc(128), scale=0.0)
+    act(T.FOUR[:], T.IDN[:], ACT.Identity, ["IDN"], ["FOUR"], cyc(128), scale=0.0, bias=4.0)
+    act(T.RK[:], T.MK1[:, 0:128], ACT.Identity, ["MK1"], ["RK"], cyc(128), scale=-BIG, bias=BIG)
+    act(T.RT[:], T.RK[:], ACT.Identity, ["RK"], ["RT"], cyc(128), bias=2.0)
+    ts(T.OB[:], T.I16[:], col(cG), 1.0 / UB, EQ, MUL, ["I16", "CF"], ["OB"])
     op("g", lambda: g.affine_select(T.LT[:], T.OB[:], [[1, 128]], GE, 0.0, 0, -1), ["OB"], ["LT"], c=450.0)
-    ms(T.ONES[:], 128.0, ["ONES"])
-    for a in range(16):
-        act(T.BR[:, 128 * a:128 * a + 128], T.OB[:], ACT.Copy, ["OB", "DK"], ["BR%d" % a], cyc(128),
-            scale=T.DK[:, a:a + 1])
-    ts(T.SJO[:], T.I144[:, 0:64:8], col(c64K), None, ADD, None, ["I144", "c%d" % c64K], ["SJO"])
+    for t in range(ST - 1):
+        iota(T["SQ%d" % t][:, 32:288], [[0, 256]], 0, 0, ["SQo%d" % t], 256)
     act(T.EF[:, H:H + 64], T.I144[:, 0:64], ACT.Identity, ["I144", "c%d" % c17K], ["EFt"], scale=0.0, bias=col(c17K))
-    ms(T.U9[:], 0.0, ["U9"])
-    ms(T.SJ[:, 128:144], 0.0, ["SJt"])
-    ts(col(cTH), T.THI[:, 0:1], 32.0, 31.0, MUL, ADD, ["THI"], ["cTH"])
+    act(T.TAG[:, H:H + 64], T.I144[:, 0:64], ACT.Copy, ["I144"], ["TAGt"], scale=0.0)
+    act(T.U9[:, 0:8], T.I144[:, 0:8], ACT.Copy, ["I144"], ["U0"], scale=0.0)
+    act(T.KS[:, 143:144], T.IDN[:, 0:1], ACT.Copy, ["IDN"], ["KSc"], scale=-112.0)
+    ts(col(cTH), T.THI[:, 0:1], 32.0, None, MUL, None, ["THI"], ["cTH"])
+    act(T.CIC[:], T.IOT[:, 8:16], ACT.Identity, ["IOTb"], ["CIC"], bias=-127.0)
     act(T.SIG[:, 0:2], T.I144[:, 0:32:16], ACT.Identity, ["I144", "CF"], ["SIG"], bias=col(cK))
-    for j, v in ((1, 1.0), (2, 4097.0), (3, 0.5)):
+    for j, v in ((1, 1.0), (2, 4097.0)):
         act(T.SIG[:, 2 * j:2 * j + 2], T.SIG[:, 0:2], ACT.Identity, ["SIG"], ["SIG%d" % j], bias=v)
-    act(T.KC2[:], T.I144[:, 1:32:2], ACT.Copy, ["I144"], ["KC2"])
-    cp(T.Q32[:], T.I144[:, 0:32], ["I144"], ["Q32"])
-    act(T.N4K[:], T.IDN[:], ACT.Copy, ["IDN"], ["N4K"], cyc(128), scale=-4096.0)
-    ts(col(cM), col(cP), 0.0, -16.0, EQ, MUL, ["cP"], ["cM"])
-    ts(col(cM + 1), col(cP), 1.0, 1.0 / 256, EQ, MUL, ["cP"], ["cM1"])
-    act(T.CM[:], T.IDN[:], ACT.Identity, ["IDN", "cM"], ["CM"], cyc(128), scale=0.0, bias=col(cM))
-    ts(T.CM[:], T.CM[:], col(cM + 1), None, ADD, None, ["CM", "cM1"], ["CM"])
-    ms(T.T4[:, 2:4], 1, ["T4b"])
     for s in range(2):
         ts(T.DT[:, 34 * s:34 * s + 34], T.I144[:, 0:34], T.SIG[:, 2 + s:3 + s], T.SIG[:, 4 + s:5 + s], EQ, MUL,
            ["I144", "SIG1", "SIG2"], ["DT%d" % s])
-    ms(T.TAG[:, H:H + 64], 0.0, ["TAGt"])
     act(T.DD[:], T.DT[:], ACT.Identity, ["DT0", "DT1"], ["DD"], bias=1.0)
-    ms(T.DD[:, 0:68:34], 0.0, ["DD"])
+    act(T.DD[:, 0:68:34], T.I144[:, 0:2], ACT.Copy, ["I144"], ["DD"], scale=0.0)
 
     sel = lambda buf, a: buf[:, 15 - a:143 - a]
-    AN = ["A%d" % i for i in range(len(ACH) - 1)]
-    MXN = ["MX%d" % i for i in range(len(ACH) - 1)]
-    MNN = ["MN%d" % i for i in range(len(ACH) - 1)]
-    S8N = ["s8_%d" % k for k in range(8)]
     W = T.TAG[:, 0:H]
+    bank = [0]
 
-    def compact(rhs_of, n, r, sfx, ext=()):
-        CI, CA, CP, CG = T["CI" + sfx], T["CA" + sfx], T["CP" + sfx], T["CG" + sfx]
+    def compact(src, n, r, sfx, ext=()):
+        CI, CA, CP, CG, CH = T["CI" + sfx], T["CA" + sfx], T["CP" + sfx], T["CG" + sfx], T["CH" + sfx]
         for u, buf in enumerate((T.ZW1, T.ZW2)):
             for a in range(16):
-                mm(T.PC[:, u * n:u * n + n], sel(buf, a), rhs_of(a), a == 0, a == 15, r + ["ZW%d" % u], ["P_C"], 64, ext)
+                mm(T.PC[:, u * n:u * n + n], sel(buf, a), src[:, a:16 * n:16], a == 0, a == 15, r + ["ZW%d" % u], ["P_C"],
+                   64, ext)
         cp(CI[:], T.PC[:, 0:2 * n], ["P_C"], ["CI" + sfx])
         ts(CA[:], CI[:], H - 1, None, AND, None, ["CI" + sfx], ["CA" + sfx])
         tt(CP[:], CA[:, 0:n], CA[:, n:2 * n], MUL, ["CA" + sfx], ["CP" + sfx])
         ts(CG[:], CP[:], 5, H - 1, SHR, AND, ["CP" + sfx], ["CG" + sfx])
+        tt(CH[:], CG[:], CA[:, n:2 * n], ADD, ["CG" + sfx, "CA" + sfx], ["CH" + sfx])
+
+    def hashes(PU, pn, n, UI, UA, PR, P2, HA, sfx, cs):
+        cp(UI, PU[:, 0:2 * n], [pn], ["UI" + sfx], cyc(2 * n))
+        ts(UA(0, 2 * n), UI, H - 1, None, AND, None, ["UI" + sfx], ["UA" + sfx], cyc(2 * n))
+        tt(PR, UA(0, n), UA(n, 2 * n), MUL, ["UA" + sfx], ["PR" + sfx], cyc(2 * n))
+        for j, (a, b, c) in enumerate(cs):
+            ts(PU[:, 2 * n + a:2 * n + b], UA(n + a, n + b), -4096.0, c, ADD, MUL, ["UA" + sfx, "c%d" % cM, pn],
+               ["PA%d" % j + sfx], cyc(b - a))
+        tt(P2, PR, PU[:, 2 * n:3 * n], ADD, ["PR" + sfx, pn] + ["PA%d" % j + sfx for j in range(len(cs))], ["P2" + sfx],
+           cyc(n))
+        ts(HA, P2, 5, H - 1, ASR, AND, ["P2" + sfx], ["HA" + sfx], cyc(n))
 
     def serve(t):
         SQ, RP = T["SQ%d" % t], T["RP%d" % t]
         arr = [("req%d" % t, NENG)]
         own = "SQo%d" % t
         part[0] = "shash"
-        for bank, bn in ((T.PU, "P_U"), (T.PL, "P_L")):
-            if bn == "P_U":
-                mm(bank[:, 0:128], T.ONES[:], T.CM[:], True, False, ["ONES", "CM"], [bn], 128)
-            else:
-                mm(bank[:, 0:128], T.N4K[:], T.QB[:], True, False, ["N4K", "QB"], [bn], 128)
-            for u in range(2):
-                mm(bank[:, 64 * u:64 * u + 64], T.WF[:, 128 * u:128 * u + 128], SQ[:, 0:64], False, u == 1,
-                   [own, "WF%d" % u], [bn], 64, arr)
-            if bn == "P_U":
-                act(T.YF[:], T.PU[:, 0:128], ACT.Identity, ["P_U"], ["YF"], cyc(128), scale=1.0 / 4096, bias=MAGIC)
-                act(T.QB[:], T.YF[:], ACT.Identity, ["YF"], ["QB"], cyc(128), bias=-MAGIC)
-        act(T.U2S[:], T.PL[:, 64:128], ACT.Copy, ["P_L"], ["U2S"])
-        tt(T.PR[:], T.PL[:, 0:64], T.U2S[:], MUL, ["P_L", "U2S"], ["PR"])
-        act(T.PA[:, 0:32], T.U2S[:, 0:32], ACT.Copy, ["U2S", "c%d" % c2K1], ["P_A"], scale=col(c2K1))
-        z = act(T.PA[:, 32:64], T.U2S[:, 32:64], ACT.Copy, ["U2S"], ["P_A"])
-        y = act(T.S16[:], SQ[:, 0:32].indirect(T.Q32[:, 0:32]), ACT.Copy, ["Q32"], ["S16"], gat(512), arr)
-        ops[y]["order"] = {z}
-        mm(T.PD0[:, 0:512], T.NEG[:], T.S16[:], True, False, ["NEG", "S16"], ["P_D0"], 512)
-        ts(T.FF[:], T.PR[:], 5, H - 1, SHR, AND, ["PR"], ["FF"])
-        tt(T.HH[:, 0:64], T.FF[:], T.PA[:, 0:64], ADD, ["FF", "P_A"], ["HH0"])
-        ts(T.HS[:], T.HH[:, 0:64], H - 1, None, AND, None, ["HH0"], ["HS"])
-        cp(T.HSU[:], T.HS[:, 0:32], ["HS"], ["HSU"])
-        act(T.TG2[:], W.indirect(T.HSU[:, 0:32]), ACT.Copy, ["TAG", "HSU"], ["TGs"], gat(512))
-        mm(T.PD0[:, 0:512], T.IDN[:], T.TG2[:], False, True, ["IDN", "TGs"], ["P_D0"], 512)
-        act(T.AB2[:], T.PD0[:, 0:512], ACT.Abs, ["P_D0"], ["ABs"], cyc(512))
-        for b in range(2):
-            o = T.PK0[:, 16 * b:16 * b + 16]
-            mm(o, T.IDN[:], T.KC2[:], True, False, ["IDN", "KC2"], ["P_K0"])
-            for a in range(16):
-                j = 16 * (16 * b + a)
-                mm(o, sel(T.Z, a), T.AB2[:, j:j + 16], False, a == 15, ["Z", "ABs"], ["P_K0"])
+        for u in range(2):
+            wf = T.WF[:, 128 * u:128 * u + 128]
+            for s in range(2):
+                mm(T.PU0[:, 64 * u + s:64 * u + 32:2], wf, SQ[:, 16 * s:16 * s + 16], True, True, ["WF%d" % u], ["P_U0"],
+                   64, arr)
+            mm(T.PU0[:, 64 * u + 32:64 * u + 64], wf, SQ[:, 32:64], True, True, [own, "WF%d" % u], ["P_U0"])
+        hashes(T.PU0, "P_U0", 64, T.VI[:], lambda a, b: T.VA[:, a:b], T.VR[:], T.V2[:], T.HS[:], "s",
+               [(0, 32, col(cM)), (32, 64, 32.0)])
+        cp(T.HSU[:], T.HS[:, 0:32], ["HAs"], ["HSU"])
         part[0] = "spre"
-        compact(lambda a: SQ[:, a:64:16], 4, [own], "2", arr)
+        compact(SQ, 4, [own], "2", arr)
+        part[0] = "scost"
+        for s in range(2):
+            for m in range(16):
+                mm(T.PS[:, 16 * s + m:512:32], T.IDN[:], SQ[:, 16 * s:16 * s + 16], True, True, ["IDN"], ["P_S"], 64, arr)
+        cp(T.TG2[:], W.indirect(T.HSU[:, 0:32]), ["TAG", "HSU"], ["TG2"], gat(512))
+        tt(T.M2[:], T.TG2[:], T.PS[:, 0:512], MAX, ["TG2", "P_S"], ["M2"], cyc(512))
+        for j, (z, buf, nm) in enumerate(((T.ZN, T.TG2, ["ZN", "TG2"]), (T.Z2, T.M2, ["Z2", "M2"]))):
+            for a in range(16):
+                mm(T.PK1[:, 0:32], sel(z, a), buf[:, 32 * a:32 * a + 32], j + a == 0, j + a == 16, nm, ["P_K1"])
         part[0] = "sbest"
-        scan(T.KS2[:], T.RK2[:], T.PK0[:, 0:32], ADD, MIN, ["RK2", "P_K0"], ["KS2"])
-        cp(T.KY2[:, 0:2], T.KS2[:, 15:32:16], ["KS2"], ["KY2"])
-        ts(T.T4[:, 0:2], T.KY2[:, 0:2], 31, None, AND, None, ["KY2"], ["T4a"])
-        tt(T.J2[:], T.T4[:], T.CA2[:, 4:8], MUL, ["T4a", "T4b", "CA2"], ["J2"])
-        tt(T.J3[:], T.J2[:], T.CG2[:], ADD, ["J2", "CG2"], ["J3"])
+        scan(T.JS[:], T.RK[:, 0:32], T.PK1[:, 0:32], ADD, MIN, ["RK", "P_K1"], ["JS"])
+        scan(T.JT[:], T.RT[:, 0:32], T.PK1[:, 0:32], ADD, MIN, ["RT", "P_K1"], ["JT"])
+        tt(T.J1[:], T.JT[:, 15:32:16], T.JS[:, 15:32:16], SUB, ["JS", "JT"], ["J1"])
+        tt(T.J2[:], T.J1[:], T.CA2[:, 4:6], MUL, ["J1", "CA2"], ["J2"])
+        tt(T.J3[:], T.J2[:], T.CH2[:, 0:2], ADD, ["J2", "CH2"], ["J3"])
         ts(T.J4[:], T.J3[:], H - 1, None, AND, None, ["J3"], ["J4"])
-        cp(T.J6[:], T.J4[:, 0:2], ["J4"], ["J6"])
+        cp(T.J6[:], T.J4[:], ["J4"], ["J6"])
         ts(T.G1[:], T.EF[:, 0:H].indirect(T.J6[:, 0:2]), 257.0, None, MUL, None, ["EF", "J6"], ["G1"], gat(32))
         ts(RP[:], T.G1[:], 4, 255, SHR, AND, ["G1"], ["RP%d" % t])
         send((rank - 1 - t % (NR - 1)) % NR, T["RL%d" % t][:], RP[:], "rep%d" % t, "lp%d" % t, ["RP%d" % t])
         part[0] = "first"
-        ts(T.E[:, 33:68:34], T.J4[:, 2:4], 1.0, None, ADD, None, ["J4"], ["Eh"])
+        ts(T.H0[:], T.CH2[:, 2:4], H - 1, None, AND, None, ["CH2"], ["H0"])
+        ts(T.E[:, 33:68:34], T.H0[:], 1.0, None, ADD, None, ["H0"], ["Eh"])
         for s in range(2):
             ts(T.E[:, 34 * s + 1:34 * s + 33], T.HS[:, 32:64], T.E[:, 34 * s + 33:34 * s + 34], -1.0, SUB, EQ,
-               ["HS", "Eh"], ["Ee%d" % s])
+               ["HAs", "Eh"], ["Ee%d" % s])
         scan(T.ES[:], T.DD[:], T.E[:], MUL, MAX, ["DD", "Ee0", "Ee1", "Eh", "Ei"], ["ES"], cyc(68))
         ts(T.DU[:], T.ES[:, 33:68:34], -1.0, None, ADD, None, ["ES"], ["DU"])
         cp(T.TAG[:, 0:H + 64].indirect(T.DU[:, 0:2]), SQ[:, 32:64], ["DU", own], ["TAG", "TAGt"], sca(32))
@@ -355,138 +352,138 @@ def rank_program(g, core, T, topo):
         cp(T.EF[:, 0:H + 64].indirect(T.DU[:, 0:2]), T["RL%d" % t][:], ["DU"], ["EF", "EFt"], sca(32),
            [("rep%d" % t, NENG)])
 
-    def kmm(h, buf, off, a0, a1, name, stop):
-        for a in range(a0, a1):
-            j = 64 * a + off
-            mm(T["PK%d" % h][:, 0:64], sel(T.Z, a), buf[:, j:j + 64], False, stop and a == a1 - 1, ["Z", name],
-               ["P_K%d" % h])
-
-    def spiece(i, a0, a1):
-        x, y = 64 * a0, 64 * a1
-        PD, pn = T["PD%d" % (i % 2)], "P_D%d" % (i % 2)
-        mm(PD[:, 0:y - x], T.NEG[:], T.S8[:, x:y], True, False, ["NEG"] + S8N, [pn], y - x)
-        act(T.TG[:, x:y], W.indirect(T.HT[:, 64 + 4 * a0:64 + 4 * a1]), ACT.Copy, ["TAG", "HT1"], ["TG%d" % i],
-            gat(y - x))
-        mm(PD[:, 0:y - x], T.IDN[:], T.TG[:, x:y], False, True, ["IDN", "TG%d" % i], [pn], y - x)
-        act(T.AB[:, x:y], PD[:, 0:y - x], ACT.Abs, [pn], ["AB%d" % i], cyc(y - x))
-
-    def vpiece(i, before, h, a0, a1, on_scalar):
-        x, y = 64 * a0 + 1024 * h, 64 * a1 + 1024 * h
-        z = tt(T.D[:, x:y], W.indirect(T.HT[:, 64 * h + 4 * a0:64 * h + 4 * a1]), T.S8[:, 64 * a0:64 * a1], SUB,
-               ["TAG", "HT%d" % h] + S8N, ["D%d" % i], gat(y - x))
-        ops[z]["order"] = set(before)
-        if on_scalar:
-            act(T.N2[:, x:y], T.D[:, x:y], ACT.Abs, ["D%d" % i], ["N%d" % i], cyc(y - x))
-            return z
-        return ts(T.N2[:, x:y], T.D[:, x:y], 0.0, -2.0, MIN, MUL, ["D%d" % i], ["N%d" % i], cyc((y - x) // 2))
-
     for t in range(ST):
         last = t == ST - 1
         LL, ln = T["LL%d" % (t % 2)], "LL%d" % (t % 2)
         LN, lnn = T["LL%d" % ((t + 1) % 2)], "LL%d" % ((t + 1) % 2)
-        part[0] = "sig"
-        for i in range(len(ACH) - 1):
-            a, b = ACH[i], ACH[i + 1]
-            src = T.X[:, 0:2048].indirect(LL[:, a // 16:b // 16])
-            if i in (C["av0"] if t == 0 else C["av"]):
-                cp(T.A[:, a:b], src, ["X", ln], [AN[i]], gat(b - a))
-            else:
-                act(T.A[:, a:b], src, ACT.Copy, ["X", ln], [AN[i]], gat(b - a))
-            scan(T.MX[:, a:b], T.MK1[:, 0:b - a], T.A[:, a:b], MUL, MAX, ["MK1", AN[i]], [MXN[i]], cyc((b - a) // 2))
-            scan(T.MN[:, a:b], T.MK2[:, 0:b - a], T.A[:, a:b], ADD, MIN, ["MK2", AN[i]], [MNN[i]], cyc((b - a) // 2))
-            mm(T.PD1[:, a // 16:b // 16], T.IDN[:], T.MX[:, a + 15:b:16], True, False, ["IDN", MXN[i]], ["P_D1"])
-            mm(T.PD1[:, a // 16:b // 16], T.NEG[:], T.MN[:, a + 15:b:16], False, True, ["NEG", MNN[i]], ["P_D1"])
-        part[0] = "hash"
-        for u in range(2):
-            for z, (wb, xb, rn) in enumerate(((T.WE, T.MX, MXN), (T.WN, T.MN, MNN))):
-                for e in range(2):
-                    j = 2 * u + e
-                    mm(T.PU[:, 64 * u:64 * u + 64], wb[:, 128 * j:128 * j + 128], xb[:, 16 * e + 15:2048:32],
-                       z + e == 0, z + e == 2, rn + ["WE%d" % j, "WN%d" % u], ["P_U"])
-        for k in range(8):
-            act(T.S8[:, k:1024:8], T.PD1[:, 0:128], ACT.Copy, ["P_D1"], ["s8_%d" % k], cyc(128))
-        cp(T.UI[:], T.PU[:, 0:128], ["P_U"], ["UI"], cyc(128))
-        ts(T.UA[:], T.UI[:], H - 1, None, AND, None, ["UI"], ["UA"], cyc(128))
-        tt(T.PR[:], T.UA[:, 0:64], T.UA[:, 64:128], MUL, ["UA"], ["PR"], cyc(128))
-        for h in range(2):
-            ts(T.PA[:, 64 * h:64 * h + 64], T.UA[:, 64:128], col(cC0 + h), None, MUL, None, ["UA", "c%d" % (cC0 + h)],
-               ["VA%d" % h] + ["P_A"][:1 - h])
-        ts(T.FF[:], T.PR[:], 5, H - 1, SHR, AND, ["PR"], ["FF"])
-        for h in (1, 0):
-            tt(T.HH[:, 64 * h:64 * h + 64], T.FF[:], T.PA[:, 64 * h:64 * h + 64], ADD, ["FF", "VA%d" % h, "P_A"],
-               ["HH%d" % h])
-            ts(T.HA[:, 64 * h:64 * h + 64], T.HH[:, 64 * h:64 * h + 64], H - 1, None, AND, None, ["HH%d" % h],
-               ["HA%d" % h])
-            cp(T.HT[:, 64 * h:64 * h + 64], T.HA[:, 64 * h:64 * h + 64], ["HA%d" % h], ["HT%d" % h])
+        XS, xn, off = (T.X, "X", 0.0) if t == 0 else (T.XF, "XF", -32.0)
+        for q in range(NP):
+            b0, b1 = PARTS[q], PARTS[q + 1]
+            n, p0, p1 = 16 * (b1 - b0), 16 * b0, 16 * b1
+            sq = str(q)
+            PU, pu = T["PU%d" % (q % 2)], "P_U%d" % (q % 2)
+            part[0] = "sig" + sq
+            a = 16 * p0
+            for eng, k in C["ach"][q]:
+                b = a + k
+                moved(eng, T.A[:, a:b], XS[:, 0:2048].indirect(LL[:, a // 16:b // 16]), off, [xn, ln], blk("A", a, b), k)
+                scan(T.MX[:, a:b], T.MK1[:, 0:k], T.A[:, a:b], MUL, MAX, ["MK1"] + blk("A", a, b), blk("MX", a, b),
+                     cyc(k // 2))
+                scan(T.MN[:, a:b], T.MK2[:, 0:k], T.A[:, a:b], ADD, MIN, ["MK2"] + blk("A", a, b), blk("MN", a, b),
+                     cyc(k // 2))
+                a = b
+            a, b = 16 * p0, 16 * p1
+            mxn, mnn, spn = blk("MX", a, b), blk("MN", a, b), blk("SP", p0, p1, 16)
+            part[0] = "hash" + sq
+            for u in range(2):
+                mm(PU[:, n * u:n * u + n], T.WF[:, 128 * u:128 * u + 128], T.MX[:, a + 15:b:16], True, False,
+                   mxn + ["WF%d" % u], [pu], n)
+                mm(PU[:, n * u:n * u + n], T.WN[:, 128 * u:128 * u + 128], T.MN[:, a + 15:b:16], False, True,
+                   mnn + ["WN"], [pu], n)
+            tt(T.SP[:, a:b:16], T.MX[:, a + 15:b:16], T.MN[:, a + 15:b:16], SUB, mxn + mnn, spn, cyc(2 * n))
+            hashes(PU, pu, n, T.UI[:, 2 * p0:2 * p1], lambda x, y, o=2 * p0: T.UA[:, o + x:o + y], T.PR[:, p0:p1],
+                   T.P2[:, p0:p1], T.HA[:, p0:p1], sq, [(0, n, col(cM))])
+            cp(T.HT[:, p0:p1], T.HA[:, p0:p1], ["HA" + sq], ["HT" + sq], cyc(n))
+            part[0] = "sj"
+            for j in range(b1 - b0):
+                mm(T.PC[:, p0 + 16 * j:p0 + 16 * j + 16], T.IDN[:], T.SP[:, a + 16 * j:b:n], True, True, ["IDN"] + spn,
+                   ["P_C"])
+            act(T.SJ[:, p0:p1], T.PC[:, p0:p1], ACT.Copy, ["P_C"], ["SJ" + sq], cyc(n))
+        sjn = ["SJ%d" % q for q in range(NP)]
         part[0] = "pre"
-        compact(lambda a: T.S8[:, 64 * a:64 * a + 64:8], 8, ["s8_0"], "")
-        part[0] = "cost"
-        for h in range(2):
-            mm(T["PK%d" % h][:, 0:64], T.IDN[:], T.KC[:, 64 * h:64 * h + 64], True, False, ["IDN", "KC"], ["P_K%d" % h])
-        SP, VP = C["sp"], C["vp"]
-        for i in range(len(SP) - 1):
-            spiece(i, SP[i], SP[i + 1])
-        before = []
-        for i, z in enumerate(VP):
-            before = [vpiece(i, before, *z)]
-        for h in range(2):
-            todo = [(T.AB, 0, SP[i], SP[i + 1], "AB%d" % i) for i in range(len(SP) - 1) if h == 1]
-            for i, (hh, a0, a1, on_scalar) in enumerate(VP):
-                if hh == h:
-                    todo += [(T.D, 1024 * h, a0, a1, "D%d" % i)][:1 - on_scalar] + [(T.N2, 1024 * h, a0, a1, "N%d" % i)]
-            for i, z in enumerate(todo):
-                kmm(h, z[0], z[1], z[2], z[3], z[4], i == len(todo) - 1)
-        if not last:
-            act(T.SJ[:, 0:128], T.S8[:, 0:1024].indirect(T.SJO[:, 0:8]), ACT.Copy, S8N + ["SJO"], ["SJ"], gat(128))
-        scan(T.KS[:, 0:64], T.RK[:], T.PK0[:, 0:64], ADD, MIN, ["RK", "P_K0"], ["KS0"])
-        scan(T.KS[:, 64:128], T.RK[:], T.PK1[:, 0:64], ADD, MIN, ["RK", "P_K1"], ["KS1"])
-        tt(T.KEY[:], T.KS[:, 7:64:8], T.KS[:, 71:128:8], MIN, ["KS0", "KS1"], ["KEY"])
-        part[0] = "best"
-        ts(T.K1[:], T.KEY[:], 31, None, AND, None, ["KEY"], ["K1"])
-        ts(T.U9[:, 8:16], T.KEY[:], col(cTH), 4096.0, GT, MUL, ["KEY", "cTH"], ["U9"])
-        tt(T.K2[:], T.K1[:], T.CA[:, 8:16], MUL, ["K1", "CA"], ["K2"])
-        tt(T.K3[:], T.K2[:], T.CG[:], ADD, ["K2", "CG"], ["K3"])
-        ts(T.K4[:], T.K3[:], H - 1, None, AND, None, ["K3"], ["K4"])
-        tt(T.K5[:], T.K4[:], T.U9[:, 8:16], MAX, ["K4", "U9"], ["K5"])
-        cp(T.K6[:], T.K5[:], ["K5"], ["K6"])
-        tt(T.EV[:], T.EF[:, 0:H + 16].indirect(T.K6[:, 0:8]), T.BASE[:], ADD, ["EF", "EFt", "K6", "BASE"], ["EV"],
-           gat(128))
-        ts(T.IDX[:], T.EV[:], 1.0 / 16, -15.0 / 32, MUL, ADD, ["EV"], ["IDX"], cyc(128))
-        part[0] = "move"
-        XCH = C["xl"] if last else C["xch"]
-        for i in range(len(XCH) - 1):
-            a, b = XCH[i], XCH[i + 1]
-            act(T.A2[:, a:b], T.A[:, 0:2048].indirect(T.IDX[:, a // 16:b // 16]), ACT.Copy, AN + ["IDX", "X0"],
-                ["B%d" % i], gat(b - a))
-            cp(T.X[:, 0:2048].indirect(LL[:, 128 + a // 16:128 + b // 16]), T.A2[:, a:b], [ln, "B%d" % i], ["X"],
-               sca(b - a))
-        last_w["X0"] = last_w["X"]
+        compact(T.SJ, 8, sjn, "")
+        for q in range(NP):
+            b0, b1 = PARTS[q], PARTS[q + 1]
+            n, p0, p1 = 16 * (b1 - b0), 16 * b0, 16 * b1
+            sq = str(q)
+            PK, pk = T["PK%d" % (q % 2)], "P_K%d" % (q % 2)
+            spn = blk("SP", p0, p1, 16)
+            part[0] = "cost" + sq
+            todo = []
+            a0 = 0
+            for kind, k in C["cost"][q]:
+                x, y = 16 * p0 + n * a0, 16 * p0 + n * (a0 + k)
+                tags = W.indirect(T.HT[:, x // 16:y // 16])
+                dn, nn = blk("D", x, y, 16), blk("N", x, y, 16)
+                if kind == "s":
+                    PD, pd = T["PD%d" % bank[0]], "P_D%d" % bank[0]
+                    bank[0] = 1 - bank[0]
+                    mm(PD[:, 0:y - x], T.ZR[:], T.MK1[:, 0:y - x], True, False, ["ZR", "MK1"], [pd], y - x)
+                    for m in range(16):
+                        mm(PD[:, m:y - x:16], T.NEG[:], T.SP[:, x:y:16], False, False, ["NEG"] + spn, [pd])
+                    act(T.D[:, x:y], tags, ACT.Copy, ["TAG", "HT" + sq], dn, gat(y - x))
+                    mm(PD[:, 0:y - x], T.IDN[:], T.D[:, x:y], False, True, ["IDN"] + dn, [pd], y - x)
+                    act(T.N2[:, x:y], PD[:, 0:y - x], ACT.Abs, [pd], nn, cyc(y - x))
+                else:
+                    sn = blk("S16", x, y, 16)
+                    scan(T.S16[:, x:y], T.MK1[:, 0:y - x], T.SP[:, x:y], MUL, ADD, ["MK1"] + spn, sn, cyc((y - x) // 2))
+                    tt(T.D[:, x:y], tags, T.S16[:, x:y], SUB, ["TAG", "HT" + sq] + sn, dn, gat(y - x))
+                    if kind == "w":
+                        act(T.N2[:, x:y], T.D[:, x:y], ACT.Abs, dn, nn, cyc(y - x))
+                    else:
+                        ts(T.N2[:, x:y], T.D[:, x:y], 0.0, -2.0, MIN, MUL, dn, nn, cyc((y - x) // 2))
+                        todo.append((T.D, a0, k, dn))
+                todo.append((T.N2, a0, k, nn))
+                a0 += k
+            order = C.get("kord", {}).get(q) or range(len(todo))
+            for i, z in enumerate(order):
+                buf, a0, k, nm = todo[z]
+                for a in range(a0, a0 + k):
+                    j = 16 * p0 + n * a
+                    mm(PK[:, 0:n], sel(T.Z, a), buf[:, j:j + n], i == 0 and a == a0,
+                       i == len(todo) - 1 and a == a0 + k - 1, ["Z"] + nm, [pk], n)
+            part[0] = "best" + sq
+            scan(T.KS[:, p0:p1], T.RK[:, 0:n], PK[:, 0:n], ADD, MIN, ["RK", pk], ["KS" + sq], cyc(n))
+            scan(T.KT[:, p0:p1], T.RT[:, 0:n], PK[:, 0:n], ADD, MIN, ["RT", pk], ["KT" + sq], cyc(n))
+            tt(T.K1[:, b0:b1], T.KT[:, p0 + 15:p1:16], T.KS[:, p0 + 15:p1:16], SUB, ["KS" + sq, "KT" + sq], ["K1" + sq])
+            ts(T.U9[:, 8 + b0:8 + b1], T.KS[:, p0 + 15:p1:16], col(cTH), float(UB), GT, MUL, ["KS" + sq, "cTH"], ["U" + sq])
+            tt(T.K2[:, b0:b1], T.K1[:, b0:b1], T.CA[:, 8 + b0:8 + b1], MUL, ["K1" + sq, "CA"], ["K2" + sq])
+            tt(T.FU[:, b0:b1], T.U9[:, 8 + b0:8 + b1], T.CH[:, b0:b1], ADD, ["U" + sq, "CH"], ["FU" + sq])
+            tt(T.K3[:, b0:b1], T.K2[:, b0:b1], T.FU[:, b0:b1], ADD, ["K2" + sq, "FU" + sq], ["K3" + sq])
+            ts(T.K4[:, b0:b1], T.K3[:, b0:b1], UB + H - 1, None, AND, None, ["K3" + sq], ["K4" + sq])
+            K6 = T.K6[:, 2 * b0:b0 + b1]
+            ts(K6, T.K4[:, b0:b1], float(H), None, MIN, None, ["K4" + sq], ["K6" + sq])
+            evn = blk("EV", p0, p1, 16)
+            tt(T.EV[:, p0:p1], T.EF[:, 0:H + 16].indirect(K6), T.BASE[:, p0:p1], ADD,
+               ["EF", "EFt", "K6" + sq, "BASE" + sq], evn, gat(n))
+            ts(T.IDX[:, p0:p1], T.EV[:, p0:p1], 1.0 / 16, -15.0 / 32, MUL, ADD, evn, ["IDX" + sq], cyc(n))
+            part[0] = "move" + sq
+            a = 16 * p0
+            for k in C["movel" if last else "move"][q]:
+                b = a + k
+                src = T.A[:, 16 * p0:16 * p1].indirect(T.IDX[:, a // 16:b // 16])
+                r = blk("A", 16 * p0, 16 * p1) + ["IDX" + sq]
+                to = LL[:, 128 + a // 16:128 + b // 16]
+                if last:
+                    moved("s", T.A2B[:, a:b], src, -1.0, r, blk("B", a, b), k)
+                    cp(T.X[:, 0:2048].indirect(to), T.A2B[:, a:b], [ln] + blk("B", a, b), ["X"], sca(k))
+                else:
+                    moved("v", T.A2[:, a:b], src, 33.0 if t == 0 else 32.0, r, blk("B", a, b), k)
+                    act(T.XF[:, 0:2048].indirect(to), T.A2[:, a:b], ACT.Silu, [ln] + blk("B", a, b), ["XF"], sca(k))
+                a = b
         if last:
             break
+        un, ksn = ["U%d" % q for q in range(NP)], ["KS%d" % q for q in range(NP)]
         part[0] = "learn"
-        mm(T.PL[:, 0:8], T.LT[:], T.U9[:, 8:16], True, False, ["LT", "U9"], ["P_L"])
+        mm(T.PC[:, 0:8], T.LT[:], T.U9[:, 8:16], True, False, ["LT"] + un, ["P_C"])
+        mm(T.PC[:, 0:8], T.N256[:], T.U9[:, 8:16], False, False, ["N256"] + un, ["P_C"])
         for d in range(1, 8):
-            mm(T.PL[:, 0:8], T.OB[:], T.U9[:, 8 - d:16 - d], False, d == 7, ["OB", "U9"], ["P_L"])
-        act(T.CN[:], T.PL[:, 0:8], ACT.Copy, ["P_L"], ["CN"])
-        for a in range(16):
-            mm(T.PL[:, 128 + 8 * a:136 + 8 * a], T.BR[:, 128 * a:128 * a + 128], T.CN[:], True, True,
-               ["BR%d" % a, "CN"], ["P_L"])
-        for sl in range(2):
-            act(T.JK[:, 128 * sl:128 * sl + 128], T.PL[:, 128:256], ACT.Sign, ["P_L", "SIG3"], ["AC%d" % sl],
-                cyc(128) + 20, scale=-1.0, bias=T.SIG[:, 6 + sl:7 + sl], accum_out=T.AC[:, sl:sl + 1])
-        ts(T.DST[:], T.AC[:], 0.5, 64.0, MUL, ADD, ["AC0", "AC1"], ["DST"])
+            mm(T.PC[:, 0:8], T.OB[:], T.U9[:, 8 - d:16 - d], False, d == 7, ["OB", "U0"] + un, ["P_C"])
+        tt(T.POI[:], T.PC[:, 0:8], T.CIC[:], MIN, ["P_C", "CIC"], ["POI"])
+        ts(T.POS[:], T.POI[:], 255.0, None, ADD, None, ["POI"], ["POS"])
         SQ = T["SQ%d" % t]
-        act(SQ[:, 32:64], T.SJ[:, 0:144].indirect(T.DST[:, 0:2]), ACT.Copy, ["DST", "SJ", "SJt"], ["SQo%d" % t], gat(32))
+        cp(SQ[:, 32:288].indirect(T.POS[:, 0:8]), T.SJ[:], ["POS"] + sjn, ["SQo%d" % t], sca(128))
         send((rank + 1 + t % (NR - 1)) % NR, SQ[:, 0:32], SQ[:, 32:64], "req%d" % t, "lq%d" % t, ["SQo%d" % t])
-        ts(T.E[:, 0:68:34], T.AC[:], 128.0, None, GE, None, ["AC0", "AC1"], ["Ei"])
-        part[0] = "cls"
-        ts(T.L7[:], T.KEY[:], 5, 7, SHR, AND, ["KEY"], ["L7"])
-        cp(T.L7B[:], T.L7[:], ["L7"], ["L7B"])
+        part[0] = "count"
         for b in range(8):
-            mm(T.PC[:, 0:1], T.ONES[:], T.L7B[:, b:b + 1], b == 0, b == 7, ["ONES", "L7B"], ["P_C"])
-        ts(T.O1[:], T.IOT[:], T.PC[:, 0:1], None, ADD, None, ["IOTa", "IOTb", "P_C"], ["O1"])
-        ts(T.O2[:], T.O1[:], 1023, None, AND, None, ["O1"], ["O2"])
-        cp(T.O3[:], T.O2[:], ["O2"], ["O3"])
+            mm(T.PD0[:, 0:1], T.OB[:], T.U9[:, 8 + b:9 + b], b == 0, b == 7, ["OB"] + un, ["P_D0"])
+        ts(T.E[:, 0:68:34], T.SIG[:, 0:2], T.PD0[:, 0:1], None, GE, None, ["SIG", "P_D0"], ["Ei"])
+        part[0] = "cls"
+        op("v", lambda: V.tensor_reduce(T.RS[:, 0:1], T.KS[:, 15:144:16], AX.X, ADD), ksn + ["KSc"], ["RS0"])
+        mm(T.PS[:, 0:1], T.FOUR[:], T.RS[:, 0:1], True, True, ["FOUR", "RS0"], ["P_S"], 256)
+        ts(T.RS[:, 1:2], T.PS[:, 0:1], M33, M33, ADD, SUB, ["P_S"], ["RS1"])
+        ts(T.RS[:, 2:3], T.PS[:, 0:1], T.RS[:, 1:2], None, SUB, None, ["P_S", "RS1"], ["RS2"])
+        ts(T.O3[:], T.IOT[:], T.RS[:, 2:3], 448.0, ADD, ADD, ["IOTa", "IOTb", "RS2"], ["O3"])
         cp(LN[:], T.NB[:, 0:1024].indirect(T.O3[:, 0:16]), ["NB", "O3"], [lnn], gat(256))
         serve(t)
     dma("y", T.y[:], T.X[:], "d_y", ["X"], (), 3000.0)

@@ -1,6 +1,7 @@
 from concourse.mybir import AluOpType as ALU, ActivationFunctionType as ACT, AxisListType as AX
 
 NR, ST, H = 4, 5, 4096
+MKW = 768
 F32, BF, I32, U16 = "float32", "bfloat16", "int32", "uint16"
 BIG = 524288.0
 UB = 1048576
@@ -12,27 +13,28 @@ def _sb(n, d):
 
 
 SCRATCH = {
-    "X": _sb(2048, BF), "XF": _sb(2048, F32), "A": _sb(2048, BF), "A2": _sb(2048, F32), "A2B": _sb(2048, BF),
+    "X": _sb(2048, BF), "GB": _sb(2048, BF), "A": _sb(2048, BF), "A2B": _sb(2048, BF),
     "MX": _sb(2048, BF), "MN": _sb(2048, BF), "SP": _sb(2048, BF), "S16": _sb(2048, BF),
     "NB": _sb(1024, I32), "NB0": _sb(128, I32), "TAG": _sb(H + 64, BF), "EF": _sb(H + 64, BF),
     "D": _sb(2048, BF), "N2": _sb(2048, BF), "TG2": _sb(512, BF), "M2": _sb(512, BF), "SJ": _sb(128, BF),
     "WB": _sb(8, BF), "THI": _sb(4, I32), "PC1": _sb(4, I32), "PI": _sb(4, I32), "CF": _sb(24, F32),
     "I144": _sb(144, F32), "I16": _sb(128, BF), "IM": _sb(128, BF), "PR0": _sb(128, BF), "PR1": _sb(128, BF),
-    "PR2": _sb(128, F32), "BASE": _sb(128, F32), "Z": _sb(144, BF), "Z2": _sb(144, BF), "ZN": _sb(144, BF),
+    "BASE": _sb(128, F32), "Z": _sb(144, BF), "Z2": _sb(144, BF), "ZN": _sb(144, BF),
     "ZW1": _sb(144, BF), "ZW2": _sb(144, BF), "WF": _sb(256, BF), "WN": _sb(256, BF), "IDN": _sb(128, BF),
     "NEG": _sb(128, BF), "N256": _sb(128, BF), "ZR": _sb(128, BF), "OB": _sb(128, BF), "LT": _sb(128, BF),
-    "FOUR": _sb(128, F32), "MK1": _sb(1024, BF), "MK2": _sb(1024, BF), "RK": _sb(128, BF), "RT": _sb(128, BF),
+    "IW": _sb(2048, F32), "J33": _sb(2048, F32), "ZB": _sb(144, BF), "GL": _sb(128, U16), "HB": _sb(16, F32),
+    "FOUR": _sb(128, F32), "MK1": _sb(MKW, BF), "MK2": _sb(MKW, BF), "RK": _sb(128, BF), "RT": _sb(128, BF),
     "IOT": _sb(16, F32), "IOT0": _sb(16, U16), "CIC": _sb(8, F32), "SIG": _sb(8, F32),
     "DD": _sb(68, F32), "DT": _sb(68, F32), "LL0": _sb(256, U16), "LL1": _sb(256, U16),
     "UI": _sb(256, I32), "UA": _sb(256, I32), "PR": _sb(128, F32), "P2": _sb(128, I32), "HA": _sb(128, I32),
     "HT": _sb(128, U16),
     "VI": _sb(128, I32), "VA": _sb(128, I32), "VR": _sb(64, F32), "V2": _sb(64, I32), "HS": _sb(64, I32),
     "HSU": _sb(32, U16),
-    "CI": _sb(16, I32), "CA": _sb(16, I32), "CP": _sb(8, I32), "CG": _sb(8, I32), "CH": _sb(8, I32),
-    "CI2": _sb(8, I32), "CA2": _sb(8, I32), "CP2": _sb(4, I32), "CG2": _sb(4, I32), "CH2": _sb(4, I32),
-    "KS": _sb(144, F32), "KT": _sb(128, F32), "K1": _sb(8, F32), "K2": _sb(8, I32), "K3": _sb(8, I32),
-    "K4": _sb(8, I32), "FU": _sb(8, I32), "K6": _sb(16, U16), "U9": _sb(16, BF),
-    "JS": _sb(32, F32), "JT": _sb(32, F32), "J1": _sb(2, F32), "J2": _sb(2, I32), "J3": _sb(2, I32), "J4": _sb(2, I32),
+    "CI": _sb(16, I32), "CA": _sb(16, I32), "CP": _sb(8, I32), "CG": _sb(8, I32),
+    "CI2": _sb(8, I32), "CA2": _sb(8, I32), "CP2": _sb(4, I32), "CG2": _sb(4, I32), "CH2": _sb(2, I32),
+    "KB": _sb(448, F32), "KD": _sb(24, F32), "K1": _sb(24, F32), "K3": _sb(8, I32),
+    "K4": _sb(8, I32), "K6": _sb(16, U16), "U9": _sb(16, BF),
+    "JB": _sb(128, F32), "JD": _sb(6, F32), "J1": _sb(6, F32), "J3": _sb(2, I32), "J4": _sb(2, I32),
     "J6": _sb(2, U16), "H0": _sb(2, I32), "EV": _sb(128, F32), "IDX": _sb(128, U16),
     "RS": _sb(4, F32), "O3": _sb(16, U16), "POI": _sb(8, F32), "POS": _sb(8, U16),
     "G1": _sb(32, I32), "E": _sb(68, F32), "ES": _sb(68, F32), "DU": _sb(2, U16),
@@ -44,7 +46,8 @@ for _t in range(ST - 1):
 for _n in ("PU0", "PU1", "PK0", "PK1", "PC", "PD0", "PD1", "PS"):
     SCRATCH[_n] = ("psum", [128, 512], F32)
 
-SEMAPHORES = (["qv", "qs", "qp", "qg", "d_nb0", "d_w", "d_x", "d_tag", "d_ef", "d_nb", "d_th", "d_y"]
+SEMAPHORES = (["qv", "qs", "qp", "qg", "d_nb0", "d_w", "d_x", "d_tag", "d_ef", "d_nb", "d_th"]
+              + ["d_y%d" % i for i in range(8)]
               + ["req%d" % t for t in range(ST - 1)] + ["rep%d" % t for t in range(ST - 1)]
               + ["lq%d" % t for t in range(ST - 1)] + ["lp%d" % t for t in range(ST - 1)])
 
@@ -53,29 +56,109 @@ CFG = {
     "ach": [[("v", 64), ("s", 192), ("s", 256), ("s", 256)], [("s", 448), ("s", 512), ("s", 320)]],
     "cost": [[("s", 10), ("v", 6)], [("s", 6), ("s", 6), ("v", 2), ("v", 2)]],
     "kord": {0: [0, 2, 1], 1: [5, 2, 4, 3, 0, 1]},
-    "move": [[256, 192, 320], [448, 832]],
-    "movel": [[256, 512], [1280]],
+    "move": [[("v", 256), ("v", 192), ("v", 320)], [("v", 448), ("v", 832)]],
+    "movei": [[("s", 768)], [("s", 640), ("v", 640)]],
+    "invs": [0, 4],
+    "inv": [[512, 512, 512, 512], [512, 512]],
+    "invv": [256, 256, 256, 256],
+    "home": [[("s", 1024), ("v", 1024)], [("s", 512), ("v", 512), ("s", 512), ("v", 512)]],
+    "hend": [1, 2],
+    "spv": [1, 1],
+    "tg2": [("v", 16)],
     "neng": 16,
-    "cy": 0.95, "g": 1.56, "sc": 3.8, "lat": 150.0, "rem": 3000.0, "win": 40.0, "beta": 1.0,
+    "guess": [(0.9, 1.56, 3.8, 160.0, 2700.0), (1.1, 1.9, 2.2, 160.0, 3500.0), (1.1, 1.25, 5.3, 160.0, 2500.0)],
+    "win": 40.0, "beta": 1.0, "moves": 2000, "slack": 0.002,
     "head": {"move0": -200.0, "cls": -900.0, "spre": 2200.0, "hash1": -200.0, "count": 1500.0, "move1": -3800.0,
              "learn": 100.0, "scost": 1200.0, "best0": 3000.0, "sig0": 2000.0, "cost0": -500.0, "shash": 2400.0,
              "first": 1100.0, "sbest": -500.0, "cost1": -1500.0, "pre": -400.0, "efw": -200.0},
 }
+CFG.update(dict(parts=[0, 8], hend=[1], dbank=["U1", "K1"], guess=[(0.95, 1.56, 3.8, 150.0, 2700.0)], moves=0))
+CFG.update({'ach':[[('v',576),('s',448),('s',512),('v',192),('s',320)]],'cost':[[('s',4),('v',4),('s',4),('v',4)]],'kord':{0:[1,4,2,0,5,3]},'move':[[('s',960),('v',1088)]],'inv':[('s',448),('s',512),('s',448),('v',64),('s',576)],'home':[('s',448),('v',448),('v',448),('s',128),('s',576)],'spv':[0],'tg2':[('s',4),('v',12)],'win':0.0,'beta':2.5,'gg':[('s',960),('v',576),('s',384),('s',128)],'achF':[[('v',448),('s',512),('v',512),('s',576)]],'achL':[[('v',512),('s',384),('s',512),('v',192),('s',128),('s',320)]],'costF':[[('v',5),('v',5),('s',4),('v',2)]],'costL':[[('s',3),('v',6),('s',4),('v',3)]],'kordF':{},'kordL':{},'moveF':[[('s',1024),('v',1024)]],'moveL':[[('s',896),('v',1152)]],'invF':[('s',384),('s',384),('s',448),('v',128),('s',704)],'invL':[('s',384),('s',768),('s',128),('v',192),('s',192),('s',384)],'ggF':[('s',1088),('v',640),('s',320)],'ggL':[('s',1728),('v',192),('s',128)],'head':{'sp0':1000,'count':-2200,'cls':6200,'home':1700,'shash':11300,'best0':-700,'scost':1800,'pre':-4700,'spre':2900,'sbest':1800,'sig0':600,'learn':300,'move0':6900,'clsn':-1600,'setup':4700,'diag':3900,'efw':-700,'sj':1900,'gg':1500,'hash0':3900,'inv':-2700,'cost0':-900,'first':-1000,'j33':8200,'late':-4500,'diagF':4500,'hash0F':2400,'sig0F':6700,'sjF':3700,'efwF':-8900,'homeF':500,'ggF':-500,'countF':-2800,'cost0F':6100,'clsnF':-600,'invF':2200,'clsF':-400,'learnF':-2700,'sbestF':800,'preF':3000,'move0F':3800,'sp0F':-700,'spreF':-1900,'shashF':2000,'best0F':-1500,'firstF':400,'best0L':-800,'sp0L':3600,'invL':1800,'move0L':-1500,'preL':3100,'diagL':-1100,'hash0L':2000,'homeL':-2300,'sig0L':100,'ggL':-2100,'cost0L':-700,'sjL':5700}})
+
+
+ORDER = {}
+
+
+def lengths(ops, guess):
+    cy, gather, scatter, wake, remote = guess
+    cost = [(o["c"][0] + o["c"][1] * gather + o["c"][2] * scatter) * cy for o in ops]
+    done = [remote if o["done"] is None else o["done"] for o in ops]
+    pred = [[(d, done[d] + wake) for d in o["deps"] | o["after"]] + [(d, 0.0) for d in o["order"]] for o in ops]
+    return cost, done, pred
+
+
+def improve(ops, seq, C):
+    n = len(ops)
+    eng = [o["eng"] for o in ops]
+    guesses = [lengths(ops, z) for z in C["guess"]]
+    before = [[d for d, _ in p] for p in guesses[0][2]]
+
+    def run(seq, k):
+        cost, done, pred = guesses[k]
+        end, by, last = [0.0] * n, [-1] * n, {}
+        for i in seq:
+            j = last.get(eng[i], -1)
+            t = end[j] if j >= 0 else 0.0
+            for d, lt in pred[i]:
+                if end[d] + lt > t:
+                    t, j = end[d] + lt, d
+            end[i], by[i], last[eng[i]] = t + cost[i], j, i
+        i = max(range(n), key=lambda z: end[z] + done[z])
+        return end[i] + done[i], i, by
+
+    runs = [run(seq, k) for k in range(len(guesses))]
+    unit = [z[0] for z in runs]
+    now = best = float(len(runs))
+    kept, seed = seq, 1
+    for move in range(C["moves"]):
+        seed = (seed * 1103515245 + 12345) % 2147483648
+        _, i, by = runs[(seed >> 8) % len(runs)]
+        links = []
+        while by[i] >= 0:
+            if eng[by[i]] == eng[i] and by[i] not in before[i]:
+                links.append((by[i], i))
+            i = by[i]
+        if not links:
+            continue
+        u, v = links[(seed >> 12) % len(links)]
+        a, b = seq.index(u), seq.index(v)
+        if seed >> 27 & 1:
+            mark = {v}
+            for i in seq[b:a - 1 if a else None:-1]:
+                if i in mark:
+                    mark.update(before[i])
+            if u in mark:
+                continue
+            new = seq[:a] + [i for i in seq[a:b + 1] if i in mark] + [i for i in seq[a:b + 1] if i not in mark] + seq[b + 1:]
+        else:
+            mark = {u}
+            for i in seq[a + 1:b + 1]:
+                if any(d in mark for d in before[i]):
+                    mark.add(i)
+            if v in mark:
+                continue
+            new = seq[:a] + [i for i in seq[a:b + 1] if i not in mark] + [i for i in seq[a:b + 1] if i in mark] + seq[b + 1:]
+        tried = [run(new, k) for k in range(len(guesses))]
+        value = sum(z[0] / w for z, w in zip(tried, unit))
+        if value <= now + C["slack"] * (1.0 - move / C["moves"]) * ((seed >> 4) % 16) / 16:
+            seq, runs, now = new, tried, value
+            if now < best:
+                kept, best = seq, now
+    return kept
 
 
 def issue_order(ops, C):
     n = len(ops)
+    cost, done, pred = lengths(ops, C["guess"][0])
     succ = [[] for _ in range(n)]
-    left = [0] * n
-    for i, o in enumerate(ops):
-        edges = [(d, ops[d]["done"] + C["lat"]) for d in o["deps"] | o["after"]] + [(d, 0.0) for d in o["order"]]
-        left[i] = len(edges)
-        for d, lt in edges:
+    left = [len(p) for p in pred]
+    for i in range(n):
+        for d, lt in pred[i]:
             succ[d].append((i, lt))
     prio = [0.0] * n
     for i in range(n - 1, -1, -1):
-        prio[i] = ops[i]["c"] + max([lt + prio[j] for j, lt in succ[i]] + [ops[i]["done"]])
-    prio = [prio[i] + C["head"].get(ops[i]["part"], 0.0) for i in range(n)]
+        prio[i] = cost[i] + max([lt + prio[j] for j, lt in succ[i]] + [done[i]])
+    prio = [prio[i] + C["head"].get(ops[i]["part"], 0.0) + C["head"].get(ops[i]["step"], 0.0) for i in range(n)]
     free, cand = {}, {}
     rdy = [0.0] * n
     for i in range(n):
@@ -87,12 +170,12 @@ def issue_order(ops, C):
     while len(seq) < n:
         t0, e = min((max(free[e], min(rdy[i] for i in cand[e])), e) for e in cand if cand[e])
         i = max((j for j in cand[e] if rdy[j] <= t0 + C["win"]), key=lambda j: (prio[j], -j))
-        end = t0 + ops[i]["c"]
+        end = t0 + cost[i]
         for j in cand[e]:
             if rdy[j] > t0 + C["win"] and prio[j] > prio[i] and (rdy[j] - t0) * C["beta"] < end - rdy[j]:
                 i = j
         cand[e].remove(i)
-        free[e] = max(t0, rdy[i]) + ops[i]["c"]
+        free[e] = max(t0, rdy[i]) + cost[i]
         seq.append(i)
         for j, lt in succ[i]:
             rdy[j] = max(rdy[j], free[e] + lt)
@@ -107,14 +190,14 @@ def rank_program(g, core, T, topo):
     if rank is None:
         return
     C = CFG
-    PARTS, NENG, CY = C["parts"], C["neng"], C["cy"]
+    PARTS, NENG = C["parts"], C["neng"]
     NP = len(PARTS) - 1
     Q = {"v": g.vector, "s": g.scalar, "p": g.tensor, "g": g, "y": g.sync}
     ops = []
     last_w, readers, sent = {}, {}, {}
-    part = ["setup"]
+    part = ["setup", "-"]
 
-    def op(eng, fn, r=(), w=(), sem=None, ext=(), c=64 * CY, done=0.0):
+    def op(eng, fn, r=(), w=(), sem=None, ext=(), c=(64, 0, 0), done=0.0):
         me = len(ops)
         deps = set()
         for x in r:
@@ -129,7 +212,8 @@ def rank_program(g, core, T, topo):
         order = set(d for d in deps if eng == "p" and ops[d]["eng"] == "p")
         after = set(sent[name] for name, _ in ext)
         ops.append({"eng": eng, "fn": fn, "deps": deps - order, "order": order, "after": after, "sem": sem,
-                    "ext": list(ext), "need": False, "part": part[0], "c": c, "done": done})
+                    "ext": list(ext), "need": False, "part": part[0], "step": part[0] + part[1], "c": c, "done": done,
+                    "more": []})
         for x in r:
             readers.setdefault(x, []).append(me)
         for x in w:
@@ -138,9 +222,9 @@ def rank_program(g, core, T, topo):
         return me
 
     V, S, P = g.vector, g.scalar, g.tensor
-    cyc = lambda n: max(64, n) * CY
-    gat = lambda n: (65 + n * C["g"]) * CY
-    sca = lambda n: (65 + n * C["sc"]) * CY
+    cyc = lambda n: (max(64, n), 0, 0)
+    gat = lambda n: (70, n, 0)
+    sca = lambda n: (70, 0, n)
     blk = lambda name, a, b, k=64: ["%s.%d" % (name, j) for j in range(a // k, (b + k - 1) // k)]
 
     def ts(out, in0, s1, s2, o0, o1, r, w, c=cyc(64)):
@@ -164,16 +248,24 @@ def rank_program(g, core, T, topo):
         return op("s", lambda: S.activation(out, a, f, **kw), r, w, c=c)
 
     def mm(out, l, rhs, st, sp, r, w, n=64, ext=()):
-        return op("p", lambda: P.matmul(out, l, rhs, st, sp), r, w, ext=ext, c=max(64, n) * 0.5 * CY)
+        one = lambda: P.matmul(out, l, rhs, st, sp)
+        o = ops[-1]
+        if o.get("row") == (r, w, ext) and o["c"][0] + max(64, n) // 2 <= 256:
+            o["more"].append(one)
+            o["c"] = (o["c"][0] + max(64, n) // 2, 0, 0)
+        else:
+            op("p", one, r, w, ext=ext, c=(max(64, n) // 2, 0, 0))
+            ops[-1]["row"] = (r, w, ext)
 
     def iota(out, pat, base, cm, w, n, flag=True):
         if flag:
-            op("g", lambda: g.iota(out, pat, base, cm, allow_small_or_imprecise_dtypes=True), (), w, c=130 + 2 * n * CY)
+            op("g", lambda: g.iota(out, pat, base, cm, allow_small_or_imprecise_dtypes=True), (), w, c=cyc(157 + 2 * n))
         else:
-            op("g", lambda: g.iota(out, pat, base, cm), (), w, c=130 + 2 * n * CY)
+            op("g", lambda: g.iota(out, pat, base, cm), (), w, c=cyc(157 + 2 * n))
 
     def dma(eng, out, a, sem, r, w, done, **kw):
-        op(eng, lambda: Q[eng].dma_start(out, a, **kw), r, list(w) + ["Q" + eng], sem=(sem, 16, True), c=100.0, done=done)
+        op(eng, lambda: Q[eng].dma_start(out, a, **kw), r, list(w) + ["Q" + eng], sem=(sem, 16, True),
+           c=cyc(500 if eng == "g" else 64), done=done)
         o = ops[-1]
         prev = set(d for d in o["deps"] if ops[d]["eng"] == eng and ops[d]["sem"] is not None)
         o["deps"] = o["deps"] - prev
@@ -186,7 +278,7 @@ def rank_program(g, core, T, topo):
         for e in topo.engines(core, dst)[:NENG]:
             m |= 1 << e
         sent[rsem] = op("g", lambda: g.remote_dma(out, a, T.sem[rsem], T.sem[lsem], pid, rid, m), r, (),
-                        sem=(lsem, NENG, False), c=500.0, done=C["rem"])
+                        sem=(lsem, NENG, False), c=cyc(550), done=None)
 
     def moved(eng, out, src, add, r, w, n):
         if eng == "s":
@@ -198,15 +290,15 @@ def rank_program(g, core, T, topo):
     EQ, GE, GT = ALU.is_equal, ALU.is_ge, ALU.is_gt
     CF = T.CF
     col = lambda j: CF[:, j:j + 1]
-    cK, cG, cP, c17K, cM, cZ, cW1, cW2, cV1, cV2, cTH = range(11)
+    cK, cG, cO, cP, c17K, cM, cZ, cW1, cW2, cV1, cV2, cTH, cE, cB = range(14)
 
     c0 = rank % 8
-    dma("y", T.X[:], T.x[:], "d_x", (), ["X"], 4200.0)
+    dma("y", T.X[:], T.x[:], "d_x", (), blk("X", 0, 2048), 4200.0)
     dma("s", T.NB0[:], T.nb[:, c0 * 128:c0 * 128 + 128], "d_nb0", (), ["NB0"], 2400.0)
     dma("s", T.WB[:, 0:2], T.w[:], "d_w", (), ["WB"], 2400.0)
     dma("y", T.TAG[:, 0:H], T.tag[:], "d_tag", (), ["TAG"], 8500.0)
-    dma("y", T.EF[:, 0:H], T.ef[:], "d_ef", (), ["EF"], 12500.0)
-    dma("y", T.NB[:], T.nb[:], "d_nb", (), ["NB"], 14500.0)
+    dma("y", T.NB[:], T.nb[:], "d_nb", (), ["NB"], 10800.0)
+    dma("y", T.EF[:, 0:H], T.ef[:], "d_ef", (), ["EF"], 15000.0)
 
     iota(T.PC1[:, 0:1], [[0, 1]], 0, 1, ["PC1"], 1, False)
     iota(T.I144[:], [[1, 144]], 0, 0, ["I144"], 144)
@@ -220,25 +312,25 @@ def rank_program(g, core, T, topo):
         b0, b1 = PARTS[q], PARTS[q + 1]
         iota(T.BASE[:, 16 * b0:16 * b1], [[256, b1 - b0], [256 * (b1 - b0), 16]], 0, 0, ["BASE%d" % q], 16 * (b1 - b0))
 
-    ms(T.MK1[:], 1.0, ["MK1"], cyc(512))
-    ms(T.MK2[:], 0.0, ["MK2"], cyc(512))
-    ms(T.MK1[:, 0:1024:16], 0.0, ["MK1"])
-    ms(T.MK2[:, 0:1024:16], 512.0, ["MK2"])
+    ms(T.MK1[:], 1.0, ["MK1"], cyc(MKW // 2))
+    ms(T.MK2[:], 0.0, ["MK2"], cyc(MKW // 2))
+    ms(T.MK1[:, 0:MKW:16], 0.0, ["MK1"])
+    ms(T.MK2[:, 0:MKW:16], 512.0, ["MK2"])
     ms(T.SP[:], 0.0, blk("SP", 0, 128, 16), cyc(1024))
-    act(T.XF[:], T.SP[:], ACT.Silu, blk("SP", 0, 128, 16), ["XF"], cyc(2048) + 1300)
     ts(T.PI[:, 0:1], T.PC1[:, 0:1], 15, None, AND, None, ["PC1"], ["PI0"])
     ts(T.PI[:, 1:2], T.PC1[:, 0:1], 4, None, SHR, None, ["PC1"], ["PI1"])
-    cp(CF[:, 0:2], T.PI[:, 0:2], ["PI0", "PI1"], ["CF"])
+    ts(T.PI[:, 2:3], T.PC1[:, 0:1], 1, None, AND, None, ["PC1"], ["PI2"])
+    cp(CF[:, 0:3], T.PI[:, 0:3], ["PI0", "PI1", "PI2"], ["CF"])
     cp(col(cP), T.PC1[:, 0:1], ["PC1"], ["cP"])
     ts(T.PR1[:], T.IM[:], col(cK), None, EQ, None, ["IM", "CF"], ["PR1"])
-    tt(T.PR2[:], T.PR1[:], T.PR0[:], MUL, ["PR1"] + ["PR0%d" % q for q in range(NP)], ["PR2"], cyc(256))
-    scan(T.EV[:], T.MK1[:, 0:128], T.PR2[:], MUL, ADD, ["MK1", "PR2"], blk("EV", 0, 128, 16), cyc(128))
+    tt(T.PR1[:], T.PR1[:], T.PR0[:], MUL, ["PR1"] + ["PR0%d" % q for q in range(NP)], ["PR1"], cyc(256))
+    scan(T.EV[:], T.MK1[:, 0:128], T.PR1[:], MUL, ADD, ["MK1", "PR1"], blk("EV", 0, 128, 16), cyc(128))
     cp(T.IOT[:, 0:8], T.EV[:, 15:128:16], blk("EV", 0, 128, 16), ["IOTa"])
     ts(T.IOT[:, 8:16], T.I144[:, 0:128:16], col(cK), None, ADD, None, ["I144", "CF"], ["IOTb"])
     for j, src, sc, bi in ((cZ, cG, 16.0, 15.0), (c17K, cK, 17.0, 0.0), (cM, cK, -64.0, 992.0)):
         act(col(j), col(src), ACT.Identity, ["CF"], ["c%d" % j], scale=sc, bias=bi)
     cp(T.IOT0[:], T.IOT[:], ["IOTa", "IOTb"], ["IOT0"])
-    cp(T.LL0[:], T.NB0[:, 0:128].indirect(T.IOT0[:, 0:16]), ["NB0", "IOT0"], ["LL0"], gat(256))
+    cp(T.LL0[:], T.NB0[:, 0:128].indirect(T.IOT0[:, 0:16]), ["NB0", "IOT0"], ["LL0", "LL0n"], gat(256))
 
     cp(CF[:, cW1:cW1 + 2], T.WB[:, 0:2], ["WB"], ["cW"])
     ts(CF[:, cV1:cV1 + 2], T.WB[:, 0:2], 1.0 / 32, None, MUL, None, ["WB"], ["cV"])
@@ -248,24 +340,35 @@ def rank_program(g, core, T, topo):
     act(T.WN[:], T.WF[:], ACT.Copy, ["WF0", "WF1"], ["WN"], cyc(256), scale=-1.0)
     act(T.ZW1[:], T.Z[:], ACT.Copy, ["Z", "cV"], ["ZW0"], cyc(144), scale=col(cV1))
     act(T.ZW2[:], T.Z[:], ACT.Copy, ["Z", "cV"], ["ZW1"], cyc(144), scale=col(cV2))
-    act(T.Z2[:], T.Z[:], ACT.Copy, ["Z"], ["Z2"], cyc(144), scale=2.0)
-    act(T.ZN[:], T.Z[:], ACT.Copy, ["Z"], ["ZN"], cyc(144), scale=-1.0)
     ts(T.IDN[:], T.I144[:, 0:128], col(cP), None, EQ, None, ["I144", "cP"], ["IDN"], cyc(128))
     act(T.NEG[:], T.IDN[:], ACT.Copy, ["IDN"], ["NEG"], cyc(128), scale=-1.0)
-    act(T.N256[:], T.IDN[:], ACT.Copy, ["IDN"], ["N256"], cyc(128), scale=-256.0 / UB)
-    act(T.ZR[:], T.IDN[:], ACT.Copy, ["IDN"], ["ZR"], cyc(128), scale=0.0)
-    act(T.FOUR[:], T.IDN[:], ACT.Identity, ["IDN"], ["FOUR"], cyc(128), scale=0.0, bias=4.0)
+    iota(T.ZR[:], [[0, 128]], 0, 0, ["ZR"], 128)
     act(T.RK[:], T.MK1[:, 0:128], ACT.Identity, ["MK1"], ["RK"], cyc(128), scale=-BIG, bias=BIG)
     act(T.RT[:], T.RK[:], ACT.Identity, ["RK"], ["RT"], cyc(128), bias=2.0)
     ts(T.OB[:], T.I16[:], col(cG), 1.0 / UB, EQ, MUL, ["I16", "CF"], ["OB"])
-    op("g", lambda: g.affine_select(T.LT[:], T.OB[:], [[1, 128]], GE, 0.0, 0, -1), ["OB"], ["LT"], c=450.0)
+    ts(col(cTH), T.THI[:, 0:1], 32.0, None, MUL, None, ["THI"], ["cTH"])
+    part[0] = "j33"
+    act(col(cE), col(cO), ACT.Identity, ["CF"], ["cE"], scale=-1.0, bias=1.0)
+    act(T.HB[:], T.I144[:, 0:16], ACT.Identity, ["I144", "CF"], ["HB"], scale=col(cO), bias=33.0)
+    for j in range(16):
+        act(T.J33[:, 128 * j:128 * j + 128], T.I144[:, 0:128], ACT.Identity if j else ACT.Silu, ["I144", "cE", "HB"],
+            ["J33.%d" % j], cyc(128 if j else 1700), scale=col(cE), bias=T.HB[:, j:j + 1])
+    part[0] = "late"
+    act(col(cB), col(cO), ACT.Identity, ["CF"], ["cB"], scale=127.0 / 256, bias=1.0 / 256)
+    act(T.ZB[:], T.Z[:], ACT.Copy, ["Z", "cB"], ["ZB"], cyc(144), scale=col(cB))
+    act(T.Z2[:], T.Z[:], ACT.Copy, ["Z"], ["Z2"], cyc(144), scale=2.0)
+    act(T.ZN[:], T.Z[:], ACT.Copy, ["Z"], ["ZN"], cyc(144), scale=-1.0)
+    act(T.N256[:], T.IDN[:], ACT.Copy, ["IDN"], ["N256"], cyc(128), scale=-256.0 / UB)
+    iota(T.KD[:], [[0, 8], [-1, 3]], 0, 0, ["KDa", "KD"], 24)
+    iota(T.JD[:], [[0, 2], [-1, 3]], 0, 0, ["JDa", "KD2"], 6)
+    iota(T.U9[:, 0:8], [[0, 8]], 0, 0, ["U0"], 8)
+    iota(T.FOUR[:], [[0, 128]], 4, 0, ["FOUR"], 128)
+    op("g", lambda: g.affine_select(T.LT[:], T.OB[:], [[1, 128]], GE, 0.0, 0, -1), ["OB"], ["LT"], c=cyc(460))
+    iota(T.TAG[:, H:H + 64], [[0, 64]], 0, 0, ["TAGt"], 64)
     for t in range(ST - 1):
         iota(T["SQ%d" % t][:, 32:288], [[0, 256]], 0, 0, ["SQo%d" % t], 256)
     act(T.EF[:, H:H + 64], T.I144[:, 0:64], ACT.Identity, ["I144", "c%d" % c17K], ["EFt"], scale=0.0, bias=col(c17K))
-    act(T.TAG[:, H:H + 64], T.I144[:, 0:64], ACT.Copy, ["I144"], ["TAGt"], scale=0.0)
-    act(T.U9[:, 0:8], T.I144[:, 0:8], ACT.Copy, ["I144"], ["U0"], scale=0.0)
-    act(T.KS[:, 143:144], T.IDN[:, 0:1], ACT.Copy, ["IDN"], ["KSc"], scale=-112.0)
-    ts(col(cTH), T.THI[:, 0:1], 32.0, None, MUL, None, ["THI"], ["cTH"])
+    act(T.KB[:, 445:446], T.IDN[:, 0:1], ACT.Copy, ["IDN"], ["KSc"], scale=-112.0)
     act(T.CIC[:], T.IOT[:, 8:16], ACT.Identity, ["IOTb"], ["CIC"], bias=-127.0)
     act(T.SIG[:, 0:2], T.I144[:, 0:32:16], ACT.Identity, ["I144", "CF"], ["SIG"], bias=col(cK))
     for j, v in ((1, 1.0), (2, 4097.0)):
@@ -280,8 +383,8 @@ def rank_program(g, core, T, topo):
     W = T.TAG[:, 0:H]
     bank = [0]
 
-    def compact(src, n, r, sfx, ext=()):
-        CI, CA, CP, CG, CH = T["CI" + sfx], T["CA" + sfx], T["CP" + sfx], T["CG" + sfx], T["CH" + sfx]
+    def compact(src, n, k, KB, KD, r, sfx, ext=()):
+        CI, CA, CP, CG = T["CI" + sfx], T["CA" + sfx], T["CP" + sfx], T["CG" + sfx]
         for u, buf in enumerate((T.ZW1, T.ZW2)):
             for a in range(16):
                 mm(T.PC[:, u * n:u * n + n], sel(buf, a), src[:, a:16 * n:16], a == 0, a == 15, r + ["ZW%d" % u], ["P_C"],
@@ -290,7 +393,15 @@ def rank_program(g, core, T, topo):
         ts(CA[:], CI[:], H - 1, None, AND, None, ["CI" + sfx], ["CA" + sfx])
         tt(CP[:], CA[:, 0:n], CA[:, n:2 * n], MUL, ["CA" + sfx], ["CP" + sfx])
         ts(CG[:], CP[:], 5, H - 1, SHR, AND, ["CP" + sfx], ["CG" + sfx])
-        tt(CH[:], CG[:], CA[:, n:2 * n], ADD, ["CG" + sfx, "CA" + sfx], ["CH" + sfx])
+        ts(KD[:, 2:3 * k:3], CA[:, n:n + k], -1.0, None, MUL, None, ["CA" + sfx], ["KD" + sfx])
+        tt(KB[:, 77:30 + 48 * k:48], CG[:, 0:k], CA[:, n:n + k], ADD, ["CG" + sfx, "CA" + sfx], ["CH" + sfx])
+
+    def least(KB, KD, K1, PK, pk, b0, b1, sfx, c):
+        n = 16 * (b1 - b0)
+        scan(KB[:, 48 * b0 + 16:48 * b1 + 16:3], T.RK[:, 0:n], PK[:, 0:n], ADD, MIN, ["RK", pk], ["KS" + sfx], cyc(n))
+        scan(KB[:, 48 * b0:48 * b1:3], T.RT[:, 0:n], PK[:, 0:n], ADD, MIN, ["RT", pk], ["KT" + sfx], cyc(n))
+        scan(K1[:, 3 * b0:3 * b1], KD[:, 3 * b0:3 * b1], KB[:, 48 * b0 + 45:48 * b1 + 30:16], MUL, ADD,
+             ["KS" + sfx, "KT" + sfx, "KD" + c, "CH" + c, "KDa", "JDa"], ["K1" + sfx])
 
     def hashes(PU, pn, n, UI, UA, PR, P2, HA, sfx, cs):
         cp(UI, PU[:, 0:2 * n], [pn], ["UI" + sfx], cyc(2 * n))
@@ -318,29 +429,35 @@ def rank_program(g, core, T, topo):
                [(0, 32, col(cM)), (32, 64, 32.0)])
         cp(T.HSU[:], T.HS[:, 0:32], ["HAs"], ["HSU"])
         part[0] = "spre"
-        compact(SQ, 4, [own], "2", arr)
+        compact(SQ, 4, 2, T.JB, T.JD, [own], "2", arr)
         part[0] = "scost"
         for s in range(2):
             for m in range(16):
                 mm(T.PS[:, 16 * s + m:512:32], T.IDN[:], SQ[:, 16 * s:16 * s + 16], True, True, ["IDN"], ["P_S"], 64, arr)
-        cp(T.TG2[:], W.indirect(T.HSU[:, 0:32]), ["TAG", "HSU"], ["TG2"], gat(512))
-        tt(T.M2[:], T.TG2[:], T.PS[:, 0:512], MAX, ["TG2", "P_S"], ["M2"], cyc(512))
-        for j, (z, buf, nm) in enumerate(((T.ZN, T.TG2, ["ZN", "TG2"]), (T.Z2, T.M2, ["Z2", "M2"]))):
-            for a in range(16):
-                mm(T.PK1[:, 0:32], sel(z, a), buf[:, 32 * a:32 * a + 32], j + a == 0, j + a == 16, nm, ["P_K1"])
+        a0 = 0
+        for eng, k in C["tg2"]:
+            x, y, nm = 32 * a0, 32 * (a0 + k), str(a0)
+            tags = W.indirect(T.HSU[:, x // 16:y // 16])
+            if eng == "s":
+                act(T.TG2[:, x:y], tags, ACT.Copy, ["TAG", "HSU"], ["TG2" + nm], gat(y - x))
+            else:
+                cp(T.TG2[:, x:y], tags, ["TAG", "HSU"], ["TG2" + nm], gat(y - x))
+            tt(T.M2[:, x:y], T.TG2[:, x:y], T.PS[:, x:y], MAX, ["TG2" + nm, "P_S"], ["M2" + nm], cyc(y - x))
+            for j, (z, buf, r) in enumerate(((T.ZN, T.TG2, ["ZN", "TG2" + nm]), (T.Z2, T.M2, ["Z2", "M2" + nm]))):
+                for a in range(a0, a0 + k):
+                    mm(T.PK1[:, 0:32], sel(z, a), buf[:, 32 * a:32 * a + 32], j + a == 0, j + a == 16, r, ["P_K1"])
+            a0 += k
         part[0] = "sbest"
-        scan(T.JS[:], T.RK[:, 0:32], T.PK1[:, 0:32], ADD, MIN, ["RK", "P_K1"], ["JS"])
-        scan(T.JT[:], T.RT[:, 0:32], T.PK1[:, 0:32], ADD, MIN, ["RT", "P_K1"], ["JT"])
-        tt(T.J1[:], T.JT[:, 15:32:16], T.JS[:, 15:32:16], SUB, ["JS", "JT"], ["J1"])
-        tt(T.J2[:], T.J1[:], T.CA2[:, 4:6], MUL, ["J1", "CA2"], ["J2"])
-        tt(T.J3[:], T.J2[:], T.CH2[:, 0:2], ADD, ["J2", "CH2"], ["J3"])
+        least(T.JB, T.JD, T.J1, T.PK1, "P_K1", 0, 2, "s", "2")
+        cp(T.J3[:], T.J1[:, 2:6:3], ["K1s"], ["J3"])
         ts(T.J4[:], T.J3[:], H - 1, None, AND, None, ["J3"], ["J4"])
         cp(T.J6[:], T.J4[:], ["J4"], ["J6"])
         ts(T.G1[:], T.EF[:, 0:H].indirect(T.J6[:, 0:2]), 257.0, None, MUL, None, ["EF", "J6"], ["G1"], gat(32))
         ts(RP[:], T.G1[:], 4, 255, SHR, AND, ["G1"], ["RP%d" % t])
         send((rank - 1 - t % (NR - 1)) % NR, T["RL%d" % t][:], RP[:], "rep%d" % t, "lp%d" % t, ["RP%d" % t])
         part[0] = "first"
-        ts(T.H0[:], T.CH2[:, 2:4], H - 1, None, AND, None, ["CH2"], ["H0"])
+        tt(T.CH2[:], T.CG2[:, 2:4], T.CA2[:, 6:8], ADD, ["CG2", "CA2"], ["CHo"])
+        ts(T.H0[:], T.CH2[:], H - 1, None, AND, None, ["CHo"], ["H0"])
         ts(T.E[:, 33:68:34], T.H0[:], 1.0, None, ADD, None, ["H0"], ["Eh"])
         for s in range(2):
             ts(T.E[:, 34 * s + 1:34 * s + 33], T.HS[:, 32:64], T.E[:, 34 * s + 33:34 * s + 34], -1.0, SUB, EQ,
@@ -352,21 +469,46 @@ def rank_program(g, core, T, topo):
         cp(T.EF[:, 0:H + 64].indirect(T.DU[:, 0:2]), T["RL%d" % t][:], ["DU"], ["EF", "EFt"], sca(32),
            [("rep%d" % t, NENG)])
 
+    def slots(LN, lnn, sfx):
+        part[0] = "gg"
+        a = 0
+        for eng, k in C["gg" + sfx]:
+            b = a + k
+            if LN is not None:
+                moved(eng, T.GB[:, a:b], T.IW[:, 0:2048].indirect(LN[:, a // 16:b // 16]), -32.0, ["IW", lnn],
+                      blk("GB", a, b), k)
+            elif eng == "s":
+                act(T.GB[:, a:b], T.IW[:, a:b], ACT.Identity, ["IW"], blk("GB", a, b), cyc(k), bias=-32.0)
+            else:
+                ts(T.GB[:, a:b], T.IW[:, a:b], -32.0, None, ADD, None, ["IW"], blk("GB", a, b), cyc(k))
+            a = b
+        part[0] = "diag"
+        for h, nm in enumerate(C["dbank"]):
+            PI, pi, a = T["P" + nm], "P_" + nm, 1024 * h
+            for k in range(16):
+                mm(PI[:, 0:64], sel(T.ZB, k), T.GB[:, a + k:a + 1024:16], k == 0, k == 15, ["ZB"] + blk("GB", a, a + 1024),
+                   [pi])
+            ts(T.GL[:, 64 * h:64 * h + 64], PI[:, 0:64], -129.0, None, ADD, None, [pi], ["GL.%d" % h])
+
     for t in range(ST):
         last = t == ST - 1
         LL, ln = T["LL%d" % (t % 2)], "LL%d" % (t % 2)
         LN, lnn = T["LL%d" % ((t + 1) % 2)], "LL%d" % ((t + 1) % 2)
-        XS, xn, off = (T.X, "X", 0.0) if t == 0 else (T.XF, "XF", -32.0)
+        sfx = "F" if t == 0 else "L" if last else ""
+        part[1] = sfx or "-"
         for q in range(NP):
             b0, b1 = PARTS[q], PARTS[q + 1]
             n, p0, p1 = 16 * (b1 - b0), 16 * b0, 16 * b1
             sq = str(q)
-            PU, pu = T["PU%d" % (q % 2)], "P_U%d" % (q % 2)
             part[0] = "sig" + sq
             a = 16 * p0
-            for eng, k in C["ach"][q]:
+            for eng, k in C["ach" + sfx][q]:
                 b = a + k
-                moved(eng, T.A[:, a:b], XS[:, 0:2048].indirect(LL[:, a // 16:b // 16]), off, [xn, ln], blk("A", a, b), k)
+                if t == 0:
+                    src, r = T.X[:, 0:2048].indirect(LL[:, a // 16:b // 16]), blk("X", 0, 2048) + [ln]
+                else:
+                    src, r = T.A2B[:, 0:2048].indirect(T.GL[:, a // 16:b // 16]), blk("B", 0, 2048) + blk("GL", a // 16, b // 16)
+                moved(eng, T.A[:, a:b], src, 0.0, r, blk("A", a, b), k)
                 scan(T.MX[:, a:b], T.MK1[:, 0:k], T.A[:, a:b], MUL, MAX, ["MK1"] + blk("A", a, b), blk("MX", a, b),
                      cyc(k // 2))
                 scan(T.MN[:, a:b], T.MK2[:, 0:k], T.A[:, a:b], ADD, MIN, ["MK2"] + blk("A", a, b), blk("MN", a, b),
@@ -374,16 +516,26 @@ def rank_program(g, core, T, topo):
                 a = b
             a, b = 16 * p0, 16 * p1
             mxn, mnn, spn = blk("MX", a, b), blk("MN", a, b), blk("SP", p0, p1, 16)
-            part[0] = "hash" + sq
-            for u in range(2):
-                mm(PU[:, n * u:n * u + n], T.WF[:, 128 * u:128 * u + 128], T.MX[:, a + 15:b:16], True, False,
-                   mxn + ["WF%d" % u], [pu], n)
-                mm(PU[:, n * u:n * u + n], T.WN[:, 128 * u:128 * u + 128], T.MN[:, a + 15:b:16], False, True,
-                   mnn + ["WN"], [pu], n)
-            tt(T.SP[:, a:b:16], T.MX[:, a + 15:b:16], T.MN[:, a + 15:b:16], SUB, mxn + mnn, spn, cyc(2 * n))
-            hashes(PU, pu, n, T.UI[:, 2 * p0:2 * p1], lambda x, y, o=2 * p0: T.UA[:, o + x:o + y], T.PR[:, p0:p1],
-                   T.P2[:, p0:p1], T.HA[:, p0:p1], sq, [(0, n, col(cM))])
-            cp(T.HT[:, p0:p1], T.HA[:, p0:p1], ["HA" + sq], ["HT" + sq], cyc(n))
+            if q + 1 in C["hend"]:
+                part[0] = "hash" + sq
+                k = C["hend"].index(q + 1)
+                h0 = 16 * PARTS[([0] + C["hend"])[k]]
+                PU, pu, hn = T["PU%d" % (k % 2)], "P_U%d" % (k % 2), p1 - h0
+                for u in range(2):
+                    mm(PU[:, hn * u:hn * u + hn], T.WF[:, 128 * u:128 * u + 128], T.MX[:, 16 * h0 + 15:b:16], True, False,
+                       blk("MX", 16 * h0, b) + ["WF%d" % u], [pu], hn)
+                    mm(PU[:, hn * u:hn * u + hn], T.WN[:, 128 * u:128 * u + 128], T.MN[:, 16 * h0 + 15:b:16], False, True,
+                       blk("MN", 16 * h0, b) + ["WN"], [pu], hn)
+                hashes(PU, pu, hn, T.UI[:, 2 * h0:2 * p1], lambda x, y, o=2 * h0: T.UA[:, o + x:o + y], T.PR[:, h0:p1],
+                       T.P2[:, h0:p1], T.HA[:, h0:p1], sq, [(0, hn, col(cM))])
+                cp(T.HT[:, h0:p1], T.HA[:, h0:p1], ["HA" + sq], blk("HT", h0, p1, 16), cyc(hn))
+            part[0] = "sp" + sq
+            if C["spv"][q]:
+                tt(T.SP[:, a:b:16], T.MX[:, a + 15:b:16], T.MN[:, a + 15:b:16], SUB, mxn + mnn, spn, cyc(2 * n))
+            else:
+                mm(T.PC[:, 128:128 + n], T.IDN[:], T.MX[:, a + 15:b:16], True, False, ["IDN"] + mxn, ["P_C"], n)
+                mm(T.PC[:, 128:128 + n], T.NEG[:], T.MN[:, a + 15:b:16], False, True, ["NEG"] + mnn, ["P_C"], n)
+                act(T.SP[:, a:b:16], T.PC[:, 128:128 + n], ACT.Copy, ["P_C"], spn, cyc(n))
             part[0] = "sj"
             for j in range(b1 - b0):
                 mm(T.PC[:, p0 + 16 * j:p0 + 16 * j + 16], T.IDN[:], T.SP[:, a + 16 * j:b:n], True, True, ["IDN"] + spn,
@@ -391,17 +543,17 @@ def rank_program(g, core, T, topo):
             act(T.SJ[:, p0:p1], T.PC[:, p0:p1], ACT.Copy, ["P_C"], ["SJ" + sq], cyc(n))
         sjn = ["SJ%d" % q for q in range(NP)]
         part[0] = "pre"
-        compact(T.SJ, 8, sjn, "")
+        compact(T.SJ, 8, 8, T.KB, T.KD, sjn, "")
         for q in range(NP):
             b0, b1 = PARTS[q], PARTS[q + 1]
             n, p0, p1 = 16 * (b1 - b0), 16 * b0, 16 * b1
             sq = str(q)
             PK, pk = T["PK%d" % (q % 2)], "P_K%d" % (q % 2)
-            spn = blk("SP", p0, p1, 16)
+            spn, htn = blk("SP", p0, p1, 16), blk("HT", p0, p1, 16)
             part[0] = "cost" + sq
             todo = []
             a0 = 0
-            for kind, k in C["cost"][q]:
+            for kind, k in C["cost" + sfx][q]:
                 x, y = 16 * p0 + n * a0, 16 * p0 + n * (a0 + k)
                 tags = W.indirect(T.HT[:, x // 16:y // 16])
                 dn, nn = blk("D", x, y, 16), blk("N", x, y, 16)
@@ -411,21 +563,28 @@ def rank_program(g, core, T, topo):
                     mm(PD[:, 0:y - x], T.ZR[:], T.MK1[:, 0:y - x], True, False, ["ZR", "MK1"], [pd], y - x)
                     for m in range(16):
                         mm(PD[:, m:y - x:16], T.NEG[:], T.SP[:, x:y:16], False, False, ["NEG"] + spn, [pd])
-                    act(T.D[:, x:y], tags, ACT.Copy, ["TAG", "HT" + sq], dn, gat(y - x))
+                    act(T.D[:, x:y], tags, ACT.Copy, ["TAG"] + htn, dn, gat(y - x))
                     mm(PD[:, 0:y - x], T.IDN[:], T.D[:, x:y], False, True, ["IDN"] + dn, [pd], y - x)
                     act(T.N2[:, x:y], PD[:, 0:y - x], ACT.Abs, [pd], nn, cyc(y - x))
                 else:
                     sn = blk("S16", x, y, 16)
-                    scan(T.S16[:, x:y], T.MK1[:, 0:y - x], T.SP[:, x:y], MUL, ADD, ["MK1"] + spn, sn, cyc((y - x) // 2))
-                    tt(T.D[:, x:y], tags, T.S16[:, x:y], SUB, ["TAG", "HT" + sq] + sn, dn, gat(y - x))
-                    if kind == "w":
+                    if kind in "vw":
+                        scan(T.S16[:, x:y], T.MK1[:, 0:y - x], T.SP[:, x:y], MUL, ADD, ["MK1"] + spn, sn, cyc((y - x) // 2))
+                    else:
+                        PD, pd = T["PD%d" % bank[0]], "P_D%d" % bank[0]
+                        bank[0] = 1 - bank[0]
+                        for m in range(16):
+                            mm(PD[:, m:y - x:16], T.IDN[:], T.SP[:, x:y:16], True, True, ["IDN"] + spn, [pd])
+                        act(T.S16[:, x:y], PD[:, 0:y - x], ACT.Copy, [pd], sn, cyc(y - x))
+                    tt(T.D[:, x:y], tags, T.S16[:, x:y], SUB, ["TAG"] + htn + sn, dn, gat(y - x))
+                    if kind in "wy":
                         act(T.N2[:, x:y], T.D[:, x:y], ACT.Abs, dn, nn, cyc(y - x))
                     else:
                         ts(T.N2[:, x:y], T.D[:, x:y], 0.0, -2.0, MIN, MUL, dn, nn, cyc((y - x) // 2))
                         todo.append((T.D, a0, k, dn))
                 todo.append((T.N2, a0, k, nn))
                 a0 += k
-            order = C.get("kord", {}).get(q) or range(len(todo))
+            order = C["kord" + sfx].get(q) or range(len(todo))
             for i, z in enumerate(order):
                 buf, a0, k, nm = todo[z]
                 for a in range(a0, a0 + k):
@@ -433,13 +592,10 @@ def rank_program(g, core, T, topo):
                     mm(PK[:, 0:n], sel(T.Z, a), buf[:, j:j + n], i == 0 and a == a0,
                        i == len(todo) - 1 and a == a0 + k - 1, ["Z"] + nm, [pk], n)
             part[0] = "best" + sq
-            scan(T.KS[:, p0:p1], T.RK[:, 0:n], PK[:, 0:n], ADD, MIN, ["RK", pk], ["KS" + sq], cyc(n))
-            scan(T.KT[:, p0:p1], T.RT[:, 0:n], PK[:, 0:n], ADD, MIN, ["RT", pk], ["KT" + sq], cyc(n))
-            tt(T.K1[:, b0:b1], T.KT[:, p0 + 15:p1:16], T.KS[:, p0 + 15:p1:16], SUB, ["KS" + sq, "KT" + sq], ["K1" + sq])
-            ts(T.U9[:, 8 + b0:8 + b1], T.KS[:, p0 + 15:p1:16], col(cTH), float(UB), GT, MUL, ["KS" + sq, "cTH"], ["U" + sq])
-            tt(T.K2[:, b0:b1], T.K1[:, b0:b1], T.CA[:, 8 + b0:8 + b1], MUL, ["K1" + sq, "CA"], ["K2" + sq])
-            tt(T.FU[:, b0:b1], T.U9[:, 8 + b0:8 + b1], T.CH[:, b0:b1], ADD, ["U" + sq, "CH"], ["FU" + sq])
-            tt(T.K3[:, b0:b1], T.K2[:, b0:b1], T.FU[:, b0:b1], ADD, ["K2" + sq, "FU" + sq], ["K3" + sq])
+            least(T.KB, T.KD, T.K1, PK, pk, b0, b1, sq, "")
+            ts(T.U9[:, 8 + b0:8 + b1], T.KB[:, 48 * b0 + 61:48 * b1 + 14:48], col(cTH), float(UB), GT, MUL,
+               ["KS" + sq, "cTH"], ["U" + sq])
+            tt(T.K3[:, b0:b1], T.K1[:, 3 * b0 + 2:3 * b1:3], T.U9[:, 8 + b0:8 + b1], ADD, ["K1" + sq, "U" + sq], ["K3" + sq])
             ts(T.K4[:, b0:b1], T.K3[:, b0:b1], UB + H - 1, None, AND, None, ["K3" + sq], ["K4" + sq])
             K6 = T.K6[:, 2 * b0:b0 + b1]
             ts(K6, T.K4[:, b0:b1], float(H), None, MIN, None, ["K4" + sq], ["K6" + sq])
@@ -449,19 +605,31 @@ def rank_program(g, core, T, topo):
             ts(T.IDX[:, p0:p1], T.EV[:, p0:p1], 1.0 / 16, -15.0 / 32, MUL, ADD, evn, ["IDX" + sq], cyc(n))
             part[0] = "move" + sq
             a = 16 * p0
-            for k in C["movel" if last else "move"][q]:
+            for eng, k in C["move" + sfx][q]:
                 b = a + k
-                src = T.A[:, 16 * p0:16 * p1].indirect(T.IDX[:, a // 16:b // 16])
-                r = blk("A", 16 * p0, 16 * p1) + ["IDX" + sq]
-                to = LL[:, 128 + a // 16:128 + b // 16]
-                if last:
-                    moved("s", T.A2B[:, a:b], src, -1.0, r, blk("B", a, b), k)
-                    cp(T.X[:, 0:2048].indirect(to), T.A2B[:, a:b], [ln] + blk("B", a, b), ["X"], sca(k))
-                else:
-                    moved("v", T.A2[:, a:b], src, 33.0 if t == 0 else 32.0, r, blk("B", a, b), k)
-                    act(T.XF[:, 0:2048].indirect(to), T.A2[:, a:b], ACT.Silu, [ln] + blk("B", a, b), ["XF"], sca(k))
+                moved(eng, T.A2B[:, a:b], T.A[:, 16 * p0:16 * p1].indirect(T.IDX[:, a // 16:b // 16]), 0.0,
+                      blk("A", 16 * p0, 16 * p1) + ["IDX" + sq], blk("B", a, b), k)
                 a = b
+        part[0] = "inv"
+        a = 0
+        for eng, k in C["inv" + sfx]:
+            to = T.IW[:, 0:2048].indirect(LL[:, 128 + a // 16:128 + (a + k) // 16])
+            r = [ln + "n"] + blk("J33", a, a + k, 128)
+            if eng == "s":
+                act(to, T.J33[:, a:a + k], ACT.Silu, r, ["IW"], sca(k))
+            else:
+                cp(to, T.J33[:, a:a + k], r, ["IW"], sca(k))
+            a += k
         if last:
+            slots(None, None, sfx)
+            part[0] = "home"
+            a = 0
+            for i, (eng, k) in enumerate(C["home"]):
+                b = a + k
+                moved(eng, T.X[:, a:b], T.A2B[:, 0:2048].indirect(T.GL[:, a // 16:b // 16]), 0.0,
+                      blk("GL", a // 16, b // 16) + blk("B", 0, 2048), blk("X", a, b), k)
+                dma("y", T.y[:, a:b], T.X[:, a:b], "d_y%d" % i, blk("X", a, b), (), 2000.0 + 1.3 * k)
+                a = b
             break
         un, ksn = ["U%d" % q for q in range(NP)], ["KS%d" % q for q in range(NP)]
         part[0] = "learn"
@@ -479,16 +647,20 @@ def rank_program(g, core, T, topo):
             mm(T.PD0[:, 0:1], T.OB[:], T.U9[:, 8 + b:9 + b], b == 0, b == 7, ["OB"] + un, ["P_D0"])
         ts(T.E[:, 0:68:34], T.SIG[:, 0:2], T.PD0[:, 0:1], None, GE, None, ["SIG", "P_D0"], ["Ei"])
         part[0] = "cls"
-        op("v", lambda: V.tensor_reduce(T.RS[:, 0:1], T.KS[:, 15:144:16], AX.X, ADD), ksn + ["KSc"], ["RS0"])
+        op("v", lambda: V.tensor_reduce(T.RS[:, 0:1], T.KB[:, 61:446:48], AX.X, ADD), ksn + ["KSc"], ["RS0"])
         mm(T.PS[:, 0:1], T.FOUR[:], T.RS[:, 0:1], True, True, ["FOUR", "RS0"], ["P_S"], 256)
         ts(T.RS[:, 1:2], T.PS[:, 0:1], M33, M33, ADD, SUB, ["P_S"], ["RS1"])
         ts(T.RS[:, 2:3], T.PS[:, 0:1], T.RS[:, 1:2], None, SUB, None, ["P_S", "RS1"], ["RS2"])
         ts(T.O3[:], T.IOT[:], T.RS[:, 2:3], 448.0, ADD, ADD, ["IOTa", "IOTb", "RS2"], ["O3"])
-        cp(LN[:], T.NB[:, 0:1024].indirect(T.O3[:, 0:16]), ["NB", "O3"], [lnn], gat(256))
+        cp(LN[:, 0:128], T.NB[:, 0:1024].indirect(T.O3[:, 0:8]), ["NB", "O3"], [lnn], gat(128))
+        part[0] = "clsn"
+        cp(LN[:, 128:256], T.NB[:, 0:1024].indirect(T.O3[:, 8:16]), ["NB", "O3"], [lnn + "n"], gat(128))
+        slots(LN, lnn, sfx)
         serve(t)
-    dma("y", T.y[:], T.X[:], "d_y", ["X"], (), 3000.0)
 
-    seq = issue_order(ops, C)
+    if C.get("fresh") or "seq" not in ORDER:
+        ORDER["seq"] = improve(ops, issue_order(ops, C), C)
+    seq = ORDER["seq"]
     pos = {}
     for i in seq:
         o = ops[i]
@@ -531,6 +703,8 @@ def rank_program(g, core, T, topo):
         for name, c in o["ex"]:
             q.wait_ge(T.sem[name], c)
         ins = o["fn"]()
+        for fn in o["more"]:
+            ins = fn()
         if o["sem"] is None:
             if o["need"]:
                 cnt[o["eng"]] = cnt.get(o["eng"], 0) + 1

@@ -1,3 +1,5 @@
+import math
+
 from concourse.mybir import AluOpType as ALU, ActivationFunctionType as ACT, AxisListType as AX
 
 NR, ST, H = 4, 5, 4096
@@ -17,36 +19,36 @@ SCRATCH = {
     "MX": _sb(2048, BF), "MN": _sb(2048, BF), "SP": _sb(2048, BF), "S16": _sb(2048, BF),
     "NB": _sb(1024, I32), "NB0": _sb(128, I32), "TAG": _sb(H + 64, BF), "EF": _sb(H + 64, BF),
     "D": _sb(2048, BF), "N2": _sb(2048, BF), "TG2": _sb(512, BF), "M2": _sb(512, BF), "SJ": _sb(128, BF),
-    "WB": _sb(8, BF), "THI": _sb(4, I32), "PC1": _sb(4, I32), "PI": _sb(4, I32), "CF": _sb(24, F32),
-    "I144": _sb(144, F32), "I16": _sb(128, BF), "IM": _sb(128, BF), "PR0": _sb(128, BF), "PR1": _sb(128, BF),
+    "WB": _sb(8, BF), "THI": _sb(4, I32), "PC1": _sb(4, I32), "PI": _sb(8, I32), "CF": _sb(24, F32),
+    "I144": _sb(144, F32), "I16": _sb(128, BF), "IM": _sb(128, BF), "PR0": _sb(128, BF),
     "BASE": _sb(128, F32), "Z": _sb(144, BF), "Z2": _sb(144, BF), "ZN": _sb(144, BF),
     "ZW1": _sb(144, BF), "ZW2": _sb(144, BF), "WF": _sb(256, BF), "WN": _sb(256, BF), "IDN": _sb(128, BF),
-    "NEG": _sb(128, BF), "N256": _sb(128, BF), "ZR": _sb(128, BF), "OB": _sb(128, BF), "LT": _sb(128, BF),
-    "IW": _sb(2048, F32), "J33": _sb(2048, F32), "ZB": _sb(144, BF), "GL": _sb(128, U16), "HB": _sb(16, F32),
+    "NEG": _sb(128, BF), "NL": _sb(512, BF), "ZR": _sb(128, BF), "OB": _sb(128, BF), "LT": _sb(128, BF),
+    "IW": _sb(2048, F32), "J33": _sb(2048, F32), "ZB": _sb(144, BF), "ZF": _sb(144, F32), "GL": _sb(128, U16), "HB": _sb(16, F32), "JR": _sb(256, BF),
     "FOUR": _sb(128, F32), "MK1": _sb(MKW, BF), "MK2": _sb(MKW, BF), "RK": _sb(128, BF), "RT": _sb(128, BF),
-    "IOT": _sb(16, F32), "IOT0": _sb(16, U16), "CIC": _sb(8, F32), "SIG": _sb(8, F32),
-    "DD": _sb(68, F32), "DT": _sb(68, F32), "LL0": _sb(256, U16), "LL1": _sb(256, U16),
+    "IOT": _sb(16, F32), "IOT0": _sb(8, U16), "CIC": _sb(8, BF), "SIG": _sb(8, F32),
+    "DD": _sb(68, F32), "DT": _sb(68, F32), "LL0": _sb(128, U16), "LL1": _sb(128, U16),
     "UI": _sb(256, I32), "UA": _sb(256, I32), "PR": _sb(128, F32), "P2": _sb(128, I32), "HA": _sb(128, I32),
     "HT": _sb(128, U16),
     "VI": _sb(128, I32), "VA": _sb(128, I32), "VR": _sb(64, F32), "V2": _sb(64, I32), "HS": _sb(64, I32),
     "HSU": _sb(32, U16),
     "CI": _sb(16, I32), "CA": _sb(16, I32), "CP": _sb(8, I32), "CG": _sb(8, I32),
-    "CI2": _sb(8, I32), "CA2": _sb(8, I32), "CP2": _sb(4, I32), "CG2": _sb(4, I32), "CH2": _sb(2, I32),
-    "KB": _sb(448, F32), "KD": _sb(24, F32), "K1": _sb(24, F32), "K3": _sb(8, I32),
+    "CI2": _sb(4, I32), "CA2": _sb(4, I32), "CP2": _sb(2, I32),
+    "KB": _sb(544, F32), "KD": _sb(24, F32), "K1": _sb(24, F32), "K3": _sb(8, I32),
     "K4": _sb(8, I32), "K6": _sb(16, U16), "U9": _sb(16, BF),
-    "JB": _sb(128, F32), "JD": _sb(6, F32), "J1": _sb(6, F32), "J3": _sb(2, I32), "J4": _sb(2, I32),
-    "J6": _sb(2, U16), "H0": _sb(2, I32), "EV": _sb(128, F32), "IDX": _sb(128, U16),
-    "RS": _sb(4, F32), "O3": _sb(16, U16), "POI": _sb(8, F32), "POS": _sb(8, U16),
+    "JB": _sb(128, F32), "JD": _sb(12, F32), "J1": _sb(6, F32), "J3": _sb(2, I32), "J4": _sb(2, I32),
+    "J6": _sb(2, U16), "H0": _sb(32, F32), "DK": _sb(32, BF), "TAGS": _sb(H + 64, BF), "EV": _sb(128, F32), "IDX": _sb(128, U16),
+    "RS": _sb(20, F32), "RD": _sb(20, F32), "O3": _sb(8, U16), "POS": _sb(8, U16),
     "G1": _sb(32, I32), "E": _sb(68, F32), "ES": _sb(68, F32), "DU": _sb(2, U16),
 }
 for _t in range(ST - 1):
-    SCRATCH["SQ%d" % _t] = _sb(288, BF)
+    SCRATCH["SQ%d" % _t] = _sb(416, BF)
     SCRATCH["RP%d" % _t] = _sb(32, I32)
     SCRATCH["RL%d" % _t] = _sb(32, I32)
 for _n in ("PU0", "PU1", "PK0", "PK1", "PC", "PD0", "PD1", "PS"):
     SCRATCH[_n] = ("psum", [128, 512], F32)
 
-SEMAPHORES = (["qv", "qs", "qp", "qg", "d_nb0", "d_w", "d_x", "d_tag", "d_ef", "d_nb", "d_th"]
+SEMAPHORES = (["qv", "qs", "qp", "qg", "d_nb0", "d_w", "d_x", "d_tag", "d_ef", "d_nb", "d_th", "d_twin"]
               + ["d_y%d" % i for i in range(8)]
               + ["req%d" % t for t in range(ST - 1)] + ["rep%d" % t for t in range(ST - 1)]
               + ["lq%d" % t for t in range(ST - 1)] + ["lp%d" % t for t in range(ST - 1)])
@@ -72,26 +74,53 @@ CFG = {
              "learn": 100.0, "scost": 1200.0, "best0": 3000.0, "sig0": 2000.0, "cost0": -500.0, "shash": 2400.0,
              "first": 1100.0, "sbest": -500.0, "cost1": -1500.0, "pre": -400.0, "efw": -200.0},
 }
-CFG.update(dict(parts=[0, 8], hend=[1], dbank=["U1", "K1"], guess=[(0.95, 1.56, 3.8, 150.0, 2700.0)], moves=0))
+CFG.update(dict(twin=1, parts=[0, 8], hend=[1], dbank=["U1", "K1"], guess=[(0.95, 1.56, 3.8, 150.0, 2700.0)], moves=0))
 CFG.update({'ach':[[('v',576),('s',448),('s',512),('v',192),('s',320)]],'cost':[[('s',4),('v',4),('s',4),('v',4)]],'kord':{0:[1,4,2,0,5,3]},'move':[[('s',960),('v',1088)]],'inv':[('s',448),('s',512),('s',448),('v',64),('s',576)],'home':[('s',448),('v',448),('v',448),('s',128),('s',576)],'spv':[0],'tg2':[('s',4),('v',12)],'win':0.0,'beta':2.5,'gg':[('s',960),('v',576),('s',384),('s',128)],'achF':[[('v',448),('s',512),('v',512),('s',576)]],'achL':[[('v',512),('s',384),('s',512),('v',192),('s',128),('s',320)]],'costF':[[('v',5),('v',5),('s',4),('v',2)]],'costL':[[('s',3),('v',6),('s',4),('v',3)]],'kordF':{},'kordL':{},'moveF':[[('s',1024),('v',1024)]],'moveL':[[('s',896),('v',1152)]],'invF':[('s',384),('s',384),('s',448),('v',128),('s',704)],'invL':[('s',384),('s',768),('s',128),('v',192),('s',192),('s',384)],'ggF':[('s',1088),('v',640),('s',320)],'ggL':[('s',1728),('v',192),('s',128)],'head':{'sp0':1000,'count':-2200,'cls':6200,'home':1700,'shash':11300,'best0':-700,'scost':1800,'pre':-4700,'spre':2900,'sbest':1800,'sig0':600,'learn':300,'move0':6900,'clsn':-1600,'setup':4700,'diag':3900,'efw':-700,'sj':1900,'gg':1500,'hash0':3900,'inv':-2700,'cost0':-900,'first':-1000,'j33':8200,'late':-4500,'diagF':4500,'hash0F':2400,'sig0F':6700,'sjF':3700,'efwF':-8900,'homeF':500,'ggF':-500,'countF':-2800,'cost0F':6100,'clsnF':-600,'invF':2200,'clsF':-400,'learnF':-2700,'sbestF':800,'preF':3000,'move0F':3800,'sp0F':-700,'spreF':-1900,'shashF':2000,'best0F':-1500,'firstF':400,'best0L':-800,'sp0L':3600,'invL':1800,'move0L':-1500,'preL':3100,'diagL':-1100,'hash0L':2000,'homeL':-2300,'sig0L':100,'ggL':-2100,'cost0L':-700,'sjL':5700}})
 
 
+CFG.update(eng={"req0": (0, 8), "rep0": (8, 16)}, first=2500.0, twin=1, when=None, moves=20000, slack=0.004, seed=1, start=(0.95, 1.56, 3.8, 150.0, 2400.0, 0.55),
+           guess=[(0.88, 1.56, 3.8, 165.0, 2200.0, 0.55), (1.04, 1.56, 3.8, 110.0, 2600.0, 0.7), (1.1, 1.4, 4.6, 160.0, 2600.0, 0.45)])
+CFG['head'].update({'setup':7200,'j33':6800,'late':-5700,'diagF':5800,'hash0F':3300,'sig0F':7200,'sjF':900,'efwF':-11900,'homeF':-5700,'ggF':-1000,'countF':400,'cost0F':2100,'invF':1300,'clsF':300,'learnF':-2700,'sbestF':6100,'preF':5500,'move0F':7500,'sp0F':-3200,'spreF':-3200,'shashF':4200,'best0F':-2500,'firstF':-2000,'ownF':4100,'scostF':-700})
+CFG.update({'ach':[[('v',640),('s',576),('s',384),('v',192),('s',256)]],'cost':[[('s',4),('v',4),('s',4),('v',4)]],'move':[[('s',896),('v',1152)]],'inv':[('s',448),('s',256),('s',704),('v',128),('s',512)],'home':[('s',768),('v',576),('v',320),('s',256),('s',128)],'tg2':[('s',12),('v',4)],'gg':[('s',640),('v',576),('s',832)],'achF':[[('v',448),('s',128),('v',768),('s',704)]],'achL':[[('v',512),('s',320),('s',512),('v',320),('s',384)]],'costF':[[('v',5),('v',6),('s',2),('s',3)]],'costL':[[('s',3),('v',4),('s',4),('v',5)]],'moveF':[[('s',896),('v',1152)]],'moveL':[[('s',1024),('v',1024)]],'invF':[('s',320),('s',320),('s',448),('v',320),('s',640)],'invL':[('s',448),('s',576),('s',448),('v',192),('s',384)],'ggF':[('s',832),('v',896),('s',320)],'ggL':[('s',1472),('v',576)]})
+CFG.update(row=256, moves=30000, slack=0.003, first=3000.0, guess=[(0.88, 1.56, 3.8, 165.0, 2200.0, 0.55), (1.04, 1.56, 3.8, 110.0, 2600.0, 0.7)])
+CFG["head"] = {k: v for k, v in CFG["head"].items() if k[-1] != "L"}
+CFG["head"].update(warm=20000,setup=9000,j33=9500,late=-6000,zero=-1000,invF=2500,sig0F=12000,hash0F=6000,clsF=3000,ggF=3000,preF=3000,ggL=-2000,diagL=-2000,invL=500)
+CFG.update({'ach':[[('v',576),('s',640),('s',384),('v',256),('s',192)]],'cost':[[('s',4),('v',5),('s',4),('v',3)]],'move':[[('s',704),('v',1344)]],'inv':[('s',512),('s',256),('s',640),('v',128),('s',512)],'home':[('s',448),('v',832),('s',512),('v',256)],'tg2':[('s',14),('v',2)],'gg':[('s',832),('v',576),('s',640)],'achF':[[('v',640),('s',320),('v',576),('s',512)]],'achL':[[('v',640),('s',768),('s',256),('v',192),('s',192)]],'costF':[[('v',5),('v',5),('s',3),('s',3)]],'costL':[[('s',4),('v',4),('s',4),('v',4)]],'moveF':[[('s',1024),('v',1024)]],'moveL':[[('s',960),('v',1088)]],'invF':[('s',576),('s',512),('v',320),('s',640)],'invL':[('s',448),('s',448),('s',640),('v',256),('s',256)],'ggF':[('s',1024),('v',1024)],'ggL':[('s',2048)],'kordL':{0:[1,4,2,0,5,3]}})
+CFG.update(twin=0, first=800.0, row=512, eng={}, seed=1, passes=[(34000, 0.0015, 0.6, 0.5), (10000, 0.001, 0.0, 0.0)])
+CFG["head"].update(learn=3000, efw=-3000, sbest=5000)
+CFG.update(j33v=4, seed=3, start=(0.95, 1.56, 3.8, 150.0, 3000.0, 0.55), passes=[(26000, 0.0015, 0.6, 0.5), (6000, 0.001, 0.0, 0.0)],
+           guess=[(0.88, 1.56, 3.8, 165.0, 2900.0, 0.5), (1.04, 1.56, 3.8, 110.0, 2800.0, 0.7)])
+CFG.update(seed=6, j33v=0, achF=[[('v', 512), ('s', 512), ('v', 448), ('s', 576)]],
+           invF=[('s', 640), ('s', 512), ('v', 256), ('s', 640)])
+CFG.update(early=[(0.88, 1.56, 3.8, 165.0, 2700.0, 0.25), (1.04, 1.56, 3.8, 110.0, 2800.0, 0.4)],
+           passes=[(26000, 0.0015, 0.6, 0.5, "guess"), (6000, 0.001, 0.0, 0.0, "guess"), (14000, 0.0004, 0.6, 0.5, "early"),
+                   (4000, 0.0004, 0.0, 0.0, "early")])
+CFG.update(seed=3, early=[(0.85, 1.56, 3.8, 225.0, 2900.0, 0.35), (1.0, 1.56, 3.8, 130.0, 2700.0, 0.4)],
+           passes=[(34000, 0.0015, 0.6, 0.5, "early"), (8000, 0.001, 0.0, 0.0, "early")])
 ORDER = {}
 
 
 def lengths(ops, guess):
-    cy, gather, scatter, wake, remote = guess
+    cy, gather, scatter, wake, remote, load = (tuple(guess) + (1.0,))[:6]
     cost = [(o["c"][0] + o["c"][1] * gather + o["c"][2] * scatter) * cy for o in ops]
-    done = [remote if o["done"] is None else o["done"] for o in ops]
+    done = [remote if o["done"] is None else o["done"] and 1800.0 + (o["done"] - 1800.0) * load for o in ops]
+    done[min(i for i, o in enumerate(ops) if o["done"] is None)] += CFG["first"]
     pred = [[(d, done[d] + wake) for d in o["deps"] | o["after"]] + [(d, 0.0) for d in o["order"]] for o in ops]
     return cost, done, pred
 
 
 def improve(ops, seq, C):
+    for moves, slack, mean, near, guess in C["passes"]:
+        seq = refine(ops, seq, C, moves, slack, mean, near, C[guess])
+    return seq
+
+
+def refine(ops, seq, C, moves, slack, mean, near, guess):
     n = len(ops)
     eng = [o["eng"] for o in ops]
-    guesses = [lengths(ops, z) for z in C["guess"]]
-    before = [[d for d, _ in p] for p in guesses[0][2]]
+    guesses = [lengths(ops, z) for z in guess]
+    before = [set(d for d, _ in p) for p in guesses[0][2]]
+    final = [i for i in range(n) if ops[i]["part"] == "home"]
 
     def run(seq, k):
         cost, done, pred = guesses[k]
@@ -103,16 +132,45 @@ def improve(ops, seq, C):
                 if end[d] + lt > t:
                     t, j = end[d] + lt, d
             end[i], by[i], last[eng[i]] = t + cost[i], j, i
-        i = max(range(n), key=lambda z: end[z] + done[z])
-        return end[i] + done[i], i, by
+        i = max(final, key=lambda z: end[z] + done[z])
+        return end[i] + done[i] + mean * sum(end) / n, i, by
+
+    def swap(seq, u, v, ahead):
+        a, b = seq.index(u), seq.index(v)
+        seg = seq[a:b + 1]
+        mark = {v if ahead else u}
+        if ahead:
+            for i in reversed(seg):
+                if i in mark:
+                    mark.update(before[i])
+        else:
+            for i in seg:
+                if not mark.isdisjoint(before[i]):
+                    mark.add(i)
+        if a > b or (u in mark and v in mark):
+            return None
+        return seq[:a] + [i for i in seg if (i in mark) == ahead] + [i for i in seg if (i in mark) != ahead] + seq[b + 1:]
+
+    count, tag = {}, []
+    for o in ops:
+        k = (o["part"], o["t"], o["eng"])
+        count[k] = count.get(k, 0) + 1
+        tag.append((o["part"], o["eng"], count[k]))
+    twin = {(tag[i], ops[i]["t"]): i for i in range(n)}
+    state = [C["seed"]]
+
+    def draw():
+        state[0] = (state[0] * 6364136223846793005 + 1442695040888963407) % 2 ** 64
+        return (state[0] >> 11) / 2.0 ** 53
 
     runs = [run(seq, k) for k in range(len(guesses))]
     unit = [z[0] for z in runs]
     now = best = float(len(runs))
-    kept, seed = seq, 1
-    for move in range(C["moves"]):
-        seed = (seed * 1103515245 + 12345) % 2147483648
-        _, i, by = runs[(seed >> 8) % len(runs)]
+    kept = seq
+    for move in range(moves):
+        _, i, by = runs[int(draw() * len(runs))]
+        if draw() < near:
+            i = n // 8 + int(draw() * (n - n // 8))
         links = []
         while by[i] >= 0:
             if eng[by[i]] == eng[i] and by[i] not in before[i]:
@@ -120,27 +178,26 @@ def improve(ops, seq, C):
             i = by[i]
         if not links:
             continue
-        u, v = links[(seed >> 12) % len(links)]
-        a, b = seq.index(u), seq.index(v)
-        if seed >> 27 & 1:
-            mark = {v}
-            for i in seq[b:a - 1 if a else None:-1]:
-                if i in mark:
-                    mark.update(before[i])
-            if u in mark:
-                continue
-            new = seq[:a] + [i for i in seq[a:b + 1] if i in mark] + [i for i in seq[a:b + 1] if i not in mark] + seq[b + 1:]
-        else:
-            mark = {u}
-            for i in seq[a + 1:b + 1]:
-                if any(d in mark for d in before[i]):
-                    mark.add(i)
-            if v in mark:
-                continue
-            new = seq[:a] + [i for i in seq[a:b + 1] if i not in mark] + [i for i in seq[a:b + 1] if i in mark] + seq[b + 1:]
+        u, v = links[int(draw() * (min(6, len(links)) if draw() < near else len(links)))]
+        if draw() < 0.2:
+            q = [i for i in seq if eng[i] == eng[u]]
+            p, k = q.index(u), 1 + int(3 * draw())
+            if draw() < 0.5:
+                u = q[max(0, p - k)]
+            else:
+                v = q[min(len(q) - 1, p + 1 + k)]
+        ahead = draw() < 0.5
+        new = swap(seq, u, v, ahead)
+        if new is None:
+            continue
+        if draw() < 0.8:
+            for dt in (-3, -2, -1, 1, 2, 3):
+                x, y = twin.get((tag[u], ops[u]["t"] + dt)), twin.get((tag[v], ops[v]["t"] + dt))
+                if x is not None and y is not None:
+                    new = swap(new, x, y, ahead) or new
         tried = [run(new, k) for k in range(len(guesses))]
         value = sum(z[0] / w for z, w in zip(tried, unit))
-        if value <= now + C["slack"] * (1.0 - move / C["moves"]) * ((seed >> 4) % 16) / 16:
+        if value <= now - slack * (1.0 - move / moves) * math.log(1.0 - draw()):
             seq, runs, now = new, tried, value
             if now < best:
                 kept, best = seq, now
@@ -149,16 +206,46 @@ def improve(ops, seq, C):
 
 def issue_order(ops, C):
     n = len(ops)
-    cost, done, pred = lengths(ops, C["guess"][0])
+    cost, done, pred = lengths(ops, C["start"])
     succ = [[] for _ in range(n)]
     left = [len(p) for p in pred]
     for i in range(n):
         for d, lt in pred[i]:
             succ[d].append((i, lt))
     prio = [0.0] * n
-    for i in range(n - 1, -1, -1):
+    wait = list(left)
+    topo_order = [i for i in range(n) if not wait[i]]
+    for i in topo_order:
+        for j, _ in succ[i]:
+            wait[j] -= 1
+            if not wait[j]:
+                topo_order.append(j)
+    assert len(topo_order) == n
+    for i in reversed(topo_order):
         prio[i] = cost[i] + max([lt + prio[j] for j, lt in succ[i]] + [done[i]])
-    prio = [prio[i] + C["head"].get(ops[i]["part"], 0.0) + C["head"].get(ops[i]["step"], 0.0) for i in range(n)]
+    top = {}
+    for i, o in enumerate(ops):
+        top[o["part"], o["t"]] = max(top.get((o["part"], o["t"]), 0.0), prio[i])
+    when = C.get("when")
+    if when:
+        prio = [prio[i] - top[o["part"], o["t"]] - C["period"] * max(o["t"], 0) - when.get(o["step"], when[o["part"]])
+                for i, o in enumerate(ops)]
+        if C.get("static"):
+            at = [0.0] * n
+            for i, o in enumerate(ops):
+                at[i] = max([C["period"] * max(o["t"], 0) + when.get(o["step"], when[o["part"]])]
+                            + [at[d] + (cost[d] + lt if (ops[d]["part"], ops[d]["t"]) == (o["part"], o["t"]) else 1.0)
+                               for d, lt in pred[i]])
+            return sorted(range(n), key=lambda z: (at[z], z))
+    else:
+        short = lambda z: z.rstrip("0123456789") if z[:2] in ("in", "gg", "di") else z
+        prio = [prio[i] + C["head"].get(short(o["part"]), 0.0) + C["head"].get(short(o["part"]) + o["step"][-1], 0.0)
+                for i, o in enumerate(ops)]
+        count = {}
+        for i, o in enumerate(ops):
+            k = (o["part"], o["t"], o["eng"])
+            count[k] = count.get(k, 0) + 1
+            prio[i] += C.get("fine", {}).get(o["part"] + o["eng"] + str(count[k]), 0)
     free, cand = {}, {}
     rdy = [0.0] * n
     for i in range(n):
@@ -195,7 +282,7 @@ def rank_program(g, core, T, topo):
     Q = {"v": g.vector, "s": g.scalar, "p": g.tensor, "g": g, "y": g.sync}
     ops = []
     last_w, readers, sent = {}, {}, {}
-    part = ["setup", "-"]
+    part = ["setup", "-", -9]
 
     def op(eng, fn, r=(), w=(), sem=None, ext=(), c=(64, 0, 0), done=0.0):
         me = len(ops)
@@ -213,7 +300,7 @@ def rank_program(g, core, T, topo):
         after = set(sent[name] for name, _ in ext)
         ops.append({"eng": eng, "fn": fn, "deps": deps - order, "order": order, "after": after, "sem": sem,
                     "ext": list(ext), "need": False, "part": part[0], "step": part[0] + part[1], "c": c, "done": done,
-                    "more": []})
+                    "more": [], "t": part[2]})
         for x in r:
             readers.setdefault(x, []).append(me)
         for x in w:
@@ -250,7 +337,7 @@ def rank_program(g, core, T, topo):
     def mm(out, l, rhs, st, sp, r, w, n=64, ext=()):
         one = lambda: P.matmul(out, l, rhs, st, sp)
         o = ops[-1]
-        if o.get("row") == (r, w, ext) and o["c"][0] + max(64, n) // 2 <= 256:
+        if o.get("row") == (r, w, ext) and o["c"][0] + max(64, n) // 2 <= C["row"]:
             o["more"].append(one)
             o["c"] = (o["c"][0] + max(64, n) // 2, 0, 0)
         else:
@@ -275,10 +362,11 @@ def rank_program(g, core, T, topo):
         dst = T.cores[dst_rank]
         rid, pid = topo.addr(dst)[0], topo.addr(dst)[1]
         m = 0
-        for e in topo.engines(core, dst)[:NENG]:
+        lo, hi = C["eng"].get(rsem, (0, NENG))
+        for e in topo.engines(core, dst)[lo:hi]:
             m |= 1 << e
         sent[rsem] = op("g", lambda: g.remote_dma(out, a, T.sem[rsem], T.sem[lsem], pid, rid, m), r, (),
-                        sem=(lsem, NENG, False), c=cyc(550), done=None)
+                        sem=(lsem, hi - lo, False), c=cyc(550), done=None)
 
     def moved(eng, out, src, add, r, w, n):
         if eng == "s":
@@ -290,22 +378,20 @@ def rank_program(g, core, T, topo):
     EQ, GE, GT = ALU.is_equal, ALU.is_ge, ALU.is_gt
     CF = T.CF
     col = lambda j: CF[:, j:j + 1]
-    cK, cG, cO, cP, c17K, cM, cZ, cW1, cW2, cV1, cV2, cTH, cE, cB = range(14)
+    cK, cG, cO, cK8, cH, cP, c17K, cM, cZ, cW1, cW2, cV1, cV2, cTH, cE, cB, cN, cQ = range(18)
 
     c0 = rank % 8
     dma("y", T.X[:], T.x[:], "d_x", (), blk("X", 0, 2048), 4200.0)
     dma("s", T.NB0[:], T.nb[:, c0 * 128:c0 * 128 + 128], "d_nb0", (), ["NB0"], 2400.0)
     dma("s", T.WB[:, 0:2], T.w[:], "d_w", (), ["WB"], 2400.0)
-    dma("y", T.TAG[:, 0:H], T.tag[:], "d_tag", (), ["TAG"], 8500.0)
-    dma("y", T.NB[:], T.nb[:], "d_nb", (), ["NB"], 10800.0)
-    dma("y", T.EF[:, 0:H], T.ef[:], "d_ef", (), ["EF"], 15000.0)
+    dma("y", T.TAG[:, 0:H], T.tag[:], "d_tag", (), ["TAG"], 9000.0)
+    dma("y", T.NB[:], T.nb[:], "d_nb", (), ["NB"], 11700.0)
+    dma("y", T.EF[:, 0:H], T.ef[:], "d_ef", (), ["EF"], 16600.0)
+    if C["twin"]:
+        dma("y", T.TAGS[:, 0:H], T.tag[:], "d_twin", (), ["TAGS"], 21500.0)
 
     iota(T.PC1[:, 0:1], [[0, 1]], 0, 1, ["PC1"], 1, False)
     iota(T.I144[:], [[1, 144]], 0, 0, ["I144"], 144)
-    iota(T.IM[:], [[0, 8], [1, 16]], 0, 0, ["IM"], 128)
-    for q in range(NP):
-        b0, b1 = PARTS[q], PARTS[q + 1]
-        iota(T.PR0[:, 16 * b0:16 * b1], [[1, 16], [16, b1 - b0]], 16 * b0, 0, ["PR0%d" % q], 16 * (b1 - b0))
     iota(T.I16[:], [[1, 8], [0, 16]], 0, 0, ["I16"], 128)
     dma("g", T.THI[:, 0:1], T.th[:], "d_th", ["I16"], ["THI"], 4000.0, allow_slow_non_contiguous=True)
     for q in range(NP):
@@ -316,63 +402,90 @@ def rank_program(g, core, T, topo):
     ms(T.MK2[:], 0.0, ["MK2"], cyc(MKW // 2))
     ms(T.MK1[:, 0:MKW:16], 0.0, ["MK1"])
     ms(T.MK2[:, 0:MKW:16], 512.0, ["MK2"])
-    ms(T.SP[:], 0.0, blk("SP", 0, 128, 16), cyc(1024))
+    part[0] = "zero"
+    for j in range(4):
+        iota(T.SP[:, 512 * j:512 * j + 512], [[0, 512]], 0, 0, blk("SP", 32 * j, 32 * j + 32, 16), 512)
+    part[0] = "setup"
     ts(T.PI[:, 0:1], T.PC1[:, 0:1], 15, None, AND, None, ["PC1"], ["PI0"])
     ts(T.PI[:, 1:2], T.PC1[:, 0:1], 4, None, SHR, None, ["PC1"], ["PI1"])
     ts(T.PI[:, 2:3], T.PC1[:, 0:1], 1, None, AND, None, ["PC1"], ["PI2"])
-    cp(CF[:, 0:3], T.PI[:, 0:3], ["PI0", "PI1", "PI2"], ["CF"])
+    ts(T.PI[:, 3:4], T.PC1[:, 0:1], 7, None, AND, None, ["PC1"], ["PI3"])
+    ts(T.PI[:, 4:5], T.PC1[:, 0:1], 3, 1, SHR, AND, ["PC1"], ["PI4"])
+    cp(CF[:, 0:5], T.PI[:, 0:5], ["PI0", "PI1", "PI2", "PI3", "PI4"], ["CF"])
     cp(col(cP), T.PC1[:, 0:1], ["PC1"], ["cP"])
-    ts(T.PR1[:], T.IM[:], col(cK), None, EQ, None, ["IM", "CF"], ["PR1"])
-    tt(T.PR1[:], T.PR1[:], T.PR0[:], MUL, ["PR1"] + ["PR0%d" % q for q in range(NP)], ["PR1"], cyc(256))
-    scan(T.EV[:], T.MK1[:, 0:128], T.PR1[:], MUL, ADD, ["MK1", "PR1"], blk("EV", 0, 128, 16), cyc(128))
-    cp(T.IOT[:, 0:8], T.EV[:, 15:128:16], blk("EV", 0, 128, 16), ["IOTa"])
+    ts(col(cQ), col(cK8), 16.0, col(cH), MUL, ADD, ["CF"], ["cQ"])
+    ts(T.IOT[:, 0:8], T.I144[:, 0:16:2], col(cQ), None, ADD, None, ["I144", "cQ"], ["IOTa"])
     ts(T.IOT[:, 8:16], T.I144[:, 0:128:16], col(cK), None, ADD, None, ["I144", "CF"], ["IOTb"])
     for j, src, sc, bi in ((cZ, cG, 16.0, 15.0), (c17K, cK, 17.0, 0.0), (cM, cK, -64.0, 992.0)):
         act(col(j), col(src), ACT.Identity, ["CF"], ["c%d" % j], scale=sc, bias=bi)
-    cp(T.IOT0[:], T.IOT[:], ["IOTa", "IOTb"], ["IOT0"])
-    cp(T.LL0[:], T.NB0[:, 0:128].indirect(T.IOT0[:, 0:16]), ["NB0", "IOT0"], ["LL0", "LL0n"], gat(256))
+    cp(T.IOT0[:], T.IOT[:, 0:8], ["IOTa"], ["IOT0"])
+    cp(T.LL0[:], T.NB0[:, 0:128].indirect(T.IOT0[:, 0:8]), ["NB0", "IOT0"], ["LL0"], gat(128))
 
     cp(CF[:, cW1:cW1 + 2], T.WB[:, 0:2], ["WB"], ["cW"])
     ts(CF[:, cV1:cV1 + 2], T.WB[:, 0:2], 1.0 / 32, None, MUL, None, ["WB"], ["cV"])
     ts(T.Z[:], T.I144[:], col(cZ), 32.0, EQ, MUL, ["I144", "c%d" % cZ], ["Z"], cyc(144))
     for u in range(2):
         ts(T.WF[:, 128 * u:128 * u + 128], T.I16[:], col(cG), col(cW1 + u), EQ, MUL, ["I16", "CF", "cW"], ["WF%d" % u])
-    act(T.WN[:], T.WF[:], ACT.Copy, ["WF0", "WF1"], ["WN"], cyc(256), scale=-1.0)
-    act(T.ZW1[:], T.Z[:], ACT.Copy, ["Z", "cV"], ["ZW0"], cyc(144), scale=col(cV1))
-    act(T.ZW2[:], T.Z[:], ACT.Copy, ["Z", "cV"], ["ZW1"], cyc(144), scale=col(cV2))
+    ts(T.WN[:], T.WF[:], -1.0, None, MUL, None, ["WF0", "WF1"], ["WN"], cyc(128))
+    ts(T.ZW1[:], T.Z[:], col(cV1), None, MUL, None, ["Z", "cV"], ["ZW0"], cyc(72))
+    ts(T.ZW2[:], T.Z[:], col(cV2), None, MUL, None, ["Z", "cV"], ["ZW1"], cyc(72))
     ts(T.IDN[:], T.I144[:, 0:128], col(cP), None, EQ, None, ["I144", "cP"], ["IDN"], cyc(128))
-    act(T.NEG[:], T.IDN[:], ACT.Copy, ["IDN"], ["NEG"], cyc(128), scale=-1.0)
-    iota(T.ZR[:], [[0, 128]], 0, 0, ["ZR"], 128)
-    act(T.RK[:], T.MK1[:, 0:128], ACT.Identity, ["MK1"], ["RK"], cyc(128), scale=-BIG, bias=BIG)
-    act(T.RT[:], T.RK[:], ACT.Identity, ["RK"], ["RT"], cyc(128), bias=2.0)
+    ts(T.NEG[:], T.IDN[:], -1.0, None, MUL, None, ["IDN"], ["NEG"])
+    part[0] = "warm"
+    act(T.ZR[:], T.I144[:, 0:128], ACT.Silu, ["I144"], ["ZR"], cyc(1700), scale=0.0)
+    part[0] = "late"
+    iota(T.PR0[:], [[0, 128]], int(BIG), 0, ["PR0"], 128)
+    for buf, nm, v in ((T.RK, "RK", 0.0), (T.RT, "RT", 2.0)):
+        op("g", lambda buf=buf, v=v: g.affine_select(buf[:], T.PR0[:], [[0, 8], [1, 16]], EQ, v, 0, 0), ["PR0"], [nm],
+           c=cyc(460))
+    part[0] = "setup"
     ts(T.OB[:], T.I16[:], col(cG), 1.0 / UB, EQ, MUL, ["I16", "CF"], ["OB"])
     ts(col(cTH), T.THI[:, 0:1], 32.0, None, MUL, None, ["THI"], ["cTH"])
     part[0] = "j33"
+    for q in range(NP):
+        b0, b1 = PARTS[q], PARTS[q + 1]
+        iota(T.JR[:, 16 * b0:16 * b1], [[0, 2], [16, 8], [0, b1 - b0]], 0, 0, ["JR0"], 16 * (b1 - b0))
+        iota(T.JR[:, 128 + 16 * b0:128 + 16 * b1], [[1, 2], [0, 8], [2, b1 - b0]], 2 * b0, 0, ["JR1"], 16 * (b1 - b0))
     act(col(cE), col(cO), ACT.Identity, ["CF"], ["cE"], scale=-1.0, bias=1.0)
-    act(T.HB[:], T.I144[:, 0:16], ACT.Identity, ["I144", "CF"], ["HB"], scale=col(cO), bias=33.0)
+    act(T.JR[:, 0:128], T.JR[:, 0:128], ACT.Copy, ["JR0", "cE"], ["JR0"], cyc(128), scale=col(cE))
+    act(T.JR[:, 128:256], T.JR[:, 128:256], ACT.Copy, ["JR1", "CF"], ["JR1"], cyc(128), scale=col(cO))
+    tt(T.JR[:, 0:128], T.JR[:, 0:128], T.JR[:, 128:256], ADD, ["JR0", "JR1"], ["JR0"], cyc(256))
+    act(T.HB[:], T.I144[:, 0:16], ACT.Identity, ["I144", "cE"], ["HB"], scale=col(cE), bias=33.0)
     for j in range(16):
-        act(T.J33[:, 128 * j:128 * j + 128], T.I144[:, 0:128], ACT.Identity if j else ACT.Silu, ["I144", "cE", "HB"],
-            ["J33.%d" % j], cyc(128 if j else 1700), scale=col(cE), bias=T.HB[:, j:j + 1])
+        if j < C["j33v"]:
+            ts(T.J33[:, j:2048:16], T.JR[:, 0:128], T.HB[:, j:j + 1], None, ADD, None, ["JR0", "HB"], ["J33.%d" % j],
+               cyc(128))
+        else:
+            act(T.J33[:, j:2048:16], T.JR[:, 0:128], ACT.Identity, ["JR0", "HB"], ["J33.%d" % j], cyc(128),
+                bias=T.HB[:, j:j + 1])
     part[0] = "late"
     act(col(cB), col(cO), ACT.Identity, ["CF"], ["cB"], scale=127.0 / 256, bias=1.0 / 256)
-    act(T.ZB[:], T.Z[:], ACT.Copy, ["Z", "cB"], ["ZB"], cyc(144), scale=col(cB))
-    act(T.Z2[:], T.Z[:], ACT.Copy, ["Z"], ["Z2"], cyc(144), scale=2.0)
-    act(T.ZN[:], T.Z[:], ACT.Copy, ["Z"], ["ZN"], cyc(144), scale=-1.0)
-    act(T.N256[:], T.IDN[:], ACT.Copy, ["IDN"], ["N256"], cyc(128), scale=-256.0 / UB)
+    ts(T.ZB[:], T.Z[:], col(cB), None, MUL, None, ["Z", "cB"], ["ZB"], cyc(72))
+    if not C["ggL"]:
+        act(T.ZF[:], T.Z[:], ACT.Copy, ["Z", "cB"], ["ZF"], cyc(144), scale=col(cB))
+    ts(T.Z2[:], T.Z[:], 2.0, None, MUL, None, ["Z"], ["Z2"], cyc(72))
+    ts(T.ZN[:], T.Z[:], -1.0, None, MUL, None, ["Z"], ["ZN"], cyc(72))
+    act(col(cN), col(cK), ACT.Identity, ["CF"], ["cN"], scale=-1.0 / UB, bias=-129.0 / UB)
+    for j, z in enumerate((col(cN), -16.0 / UB, -32.0 / UB, -64.0 / UB)):
+        ts(T.NL[:, 128 * j:128 * j + 128], T.IDN[:], z, None, MUL, None, ["IDN", "cN"], ["NL%d" % j])
     iota(T.KD[:], [[0, 8], [-1, 3]], 0, 0, ["KDa", "KD"], 24)
-    iota(T.JD[:], [[0, 2], [-1, 3]], 0, 0, ["JDa", "KD2"], 6)
+    iota(T.JD[:], [[0, 4], [-1, 3]], 0, 0, ["JDa", "KD2"], 12)
     iota(T.U9[:, 0:8], [[0, 8]], 0, 0, ["U0"], 8)
     iota(T.FOUR[:], [[0, 128]], 4, 0, ["FOUR"], 128)
     op("g", lambda: g.affine_select(T.LT[:], T.OB[:], [[1, 128]], GE, 0.0, 0, -1), ["OB"], ["LT"], c=cyc(460))
-    iota(T.TAG[:, H:H + 64], [[0, 64]], 0, 0, ["TAGt"], 64)
     for t in range(ST - 1):
-        iota(T["SQ%d" % t][:, 32:288], [[0, 256]], 0, 0, ["SQo%d" % t], 256)
-    act(T.EF[:, H:H + 64], T.I144[:, 0:64], ACT.Identity, ["I144", "c%d" % c17K], ["EFt"], scale=0.0, bias=col(c17K))
-    act(T.KB[:, 445:446], T.IDN[:, 0:1], ACT.Copy, ["IDN"], ["KSc"], scale=-112.0)
-    act(T.CIC[:], T.IOT[:, 8:16], ACT.Identity, ["IOTb"], ["CIC"], bias=-127.0)
+        iota(T["SQ%d" % t][:, 32:64], [[0, 32]], 0, 0, ["SQo%d" % t], 32)
+    act(T.EF[:, H:H + 16], T.I144[:, 0:16], ACT.Identity, ["I144", "c%d" % c17K], ["EFt"], scale=0.0, bias=col(c17K))
+    for j, v in enumerate((-112.0, M33 / 4, -M33 / 4)):
+        act(T.KB[:, 445 + 48 * j:446 + 48 * j], T.IDN[:, 0:1], ACT.Copy, ["IDN"] + ["KSc"][:j], ["KSc"], scale=v)
+    iota(T.RD[:], [[0, 20]], 1, 0, ["RD"], 20)
+    iota(T.RD[:, 11:12], [[0, 1]], -1, 0, ["RD"], 1)
+    act(T.CIC[:], T.IOT[:, 8:16], ACT.Identity, ["IOTb"], ["CIC"], bias=128.0)
     act(T.SIG[:, 0:2], T.I144[:, 0:32:16], ACT.Identity, ["I144", "CF"], ["SIG"], bias=col(cK))
-    for j, v in ((1, 1.0), (2, 4097.0)):
-        act(T.SIG[:, 2 * j:2 * j + 2], T.SIG[:, 0:2], ACT.Identity, ["SIG"], ["SIG%d" % j], bias=v)
+    for j, sc, v in ((1, 1.0, 1.0), (2, 4.0, 4 * 4097.0 - 1)):
+        act(T.SIG[:, 2 * j:2 * j + 2], T.SIG[:, 0:2], ACT.Identity, ["SIG"], ["SIG%d" % j], scale=sc, bias=v)
+    iota(T.IM[:, 0:32], [[0, 2], [1, 16]], 0, 0, ["IM"], 32)
+    ts(T.DK[:], T.IM[:, 0:32], col(cK), None, EQ, None, ["IM", "CF"], ["DK"])
     for s in range(2):
         ts(T.DT[:, 34 * s:34 * s + 34], T.I144[:, 0:34], T.SIG[:, 2 + s:3 + s], T.SIG[:, 4 + s:5 + s], EQ, MUL,
            ["I144", "SIG1", "SIG2"], ["DT%d" % s])
@@ -383,15 +496,18 @@ def rank_program(g, core, T, topo):
     W = T.TAG[:, 0:H]
     bank = [0]
 
-    def compact(src, n, k, KB, KD, r, sfx, ext=()):
-        CI, CA, CP, CG = T["CI" + sfx], T["CA" + sfx], T["CP" + sfx], T["CG" + sfx]
+    def compact(src, n, KB, KD, r, sfx, ext=()):
+        CI, CA, CP, CG, k = T["CI" + sfx], T["CA" + sfx], T["CP" + sfx], T.CG, n
         for u, buf in enumerate((T.ZW1, T.ZW2)):
             for a in range(16):
-                mm(T.PC[:, u * n:u * n + n], sel(buf, a), src[:, a:16 * n:16], a == 0, a == 15, r + ["ZW%d" % u], ["P_C"],
-                   64, ext)
+                mm(T.PC[:, u * n:u * n + n], sel(buf, a), src(a), a == 0, a == 15, r + ["ZW%d" % u], ["P_C"], 64, ext)
         cp(CI[:], T.PC[:, 0:2 * n], ["P_C"], ["CI" + sfx])
         ts(CA[:], CI[:], H - 1, None, AND, None, ["CI" + sfx], ["CA" + sfx])
         tt(CP[:], CA[:, 0:n], CA[:, n:2 * n], MUL, ["CA" + sfx], ["CP" + sfx])
+        if sfx:
+            ts(KD[:, 2:3 * n:3], CA[:, n:2 * n], -4096.0, -32.0, ADD, MUL, ["CA" + sfx], ["KD" + sfx])
+            tt(KB[:, 77:30 + 48 * k:48], CP[:, 0:k], KD[:, 2:3 * k:3], SUB, ["CP" + sfx, "KD" + sfx], ["CH" + sfx])
+            return
         ts(CG[:], CP[:], 5, H - 1, SHR, AND, ["CP" + sfx], ["CG" + sfx])
         ts(KD[:, 2:3 * k:3], CA[:, n:n + k], -1.0, None, MUL, None, ["CA" + sfx], ["KD" + sfx])
         tt(KB[:, 77:30 + 48 * k:48], CG[:, 0:k], CA[:, n:n + k], ADD, ["CG" + sfx, "CA" + sfx], ["CH" + sfx])
@@ -416,20 +532,24 @@ def rank_program(g, core, T, topo):
 
     def serve(t):
         SQ, RP = T["SQ%d" % t], T["RP%d" % t]
-        arr = [("req%d" % t, NENG)]
+        many = lambda z: (z, C["eng"].get(z, (0, NENG))[1] - C["eng"].get(z, (0, NENG))[0])
+        arr = [many("req%d" % t)]
         own = "SQo%d" % t
+        apart = t < C["twin"]
+        TS, tsn, k, hn = (T.TAGS, "TAGS", 32, "HAo") if apart else (T.TAG, "TAG", 64, "HAs")
         part[0] = "shash"
         for u in range(2):
             wf = T.WF[:, 128 * u:128 * u + 128]
             for s in range(2):
-                mm(T.PU0[:, 64 * u + s:64 * u + 32:2], wf, SQ[:, 16 * s:16 * s + 16], True, True, ["WF%d" % u], ["P_U0"],
-                   64, arr)
-            mm(T.PU0[:, 64 * u + 32:64 * u + 64], wf, SQ[:, 32:64], True, True, [own, "WF%d" % u], ["P_U0"])
-        hashes(T.PU0, "P_U0", 64, T.VI[:], lambda a, b: T.VA[:, a:b], T.VR[:], T.V2[:], T.HS[:], "s",
-               [(0, 32, col(cM)), (32, 64, 32.0)])
+                mm(T.PU0[:, k * u + s:k * u + 32:2], wf, SQ[:, 16 * s:16 * s + 16], True, True, ["WF0", "WF1", own],
+                   ["P_U0"], 64, arr)
+            if not apart:
+                mm(T.PU0[:, 64 * u + 32:64 * u + 64], wf, SQ[:, 32:64], True, True, ["WF0", "WF1", own], ["P_U0"], 64, arr)
+        hashes(T.PU0, "P_U0", k, T.VI[:, 0:2 * k], lambda a, b: T.VA[:, a:b], T.VR[:, 0:k], T.V2[:, 0:k], T.HS[:, 0:k], "s",
+               [(0, 32, col(cM)), (32, 64, 32.0)][:k // 32])
         cp(T.HSU[:], T.HS[:, 0:32], ["HAs"], ["HSU"])
         part[0] = "spre"
-        compact(SQ, 4, 2, T.JB, T.JD, [own], "2", arr)
+        compact(lambda a: SQ[:, a:32:16], 2, T.JB, T.JD, [], "2", arr)
         part[0] = "scost"
         for s in range(2):
             for m in range(16):
@@ -437,11 +557,11 @@ def rank_program(g, core, T, topo):
         a0 = 0
         for eng, k in C["tg2"]:
             x, y, nm = 32 * a0, 32 * (a0 + k), str(a0)
-            tags = W.indirect(T.HSU[:, x // 16:y // 16])
+            tags = TS[:, 0:H].indirect(T.HSU[:, x // 16:y // 16])
             if eng == "s":
-                act(T.TG2[:, x:y], tags, ACT.Copy, ["TAG", "HSU"], ["TG2" + nm], gat(y - x))
+                act(T.TG2[:, x:y], tags, ACT.Copy, [tsn, "HSU"], ["TG2" + nm], gat(y - x))
             else:
-                cp(T.TG2[:, x:y], tags, ["TAG", "HSU"], ["TG2" + nm], gat(y - x))
+                cp(T.TG2[:, x:y], tags, [tsn, "HSU"], ["TG2" + nm], gat(y - x))
             tt(T.M2[:, x:y], T.TG2[:, x:y], T.PS[:, x:y], MAX, ["TG2" + nm, "P_S"], ["M2" + nm], cyc(y - x))
             for j, (z, buf, r) in enumerate(((T.ZN, T.TG2, ["ZN", "TG2" + nm]), (T.Z2, T.M2, ["Z2", "M2" + nm]))):
                 for a in range(a0, a0 + k):
@@ -450,30 +570,40 @@ def rank_program(g, core, T, topo):
         part[0] = "sbest"
         least(T.JB, T.JD, T.J1, T.PK1, "P_K1", 0, 2, "s", "2")
         cp(T.J3[:], T.J1[:, 2:6:3], ["K1s"], ["J3"])
-        ts(T.J4[:], T.J3[:], H - 1, None, AND, None, ["J3"], ["J4"])
+        ts(T.J4[:], T.J3[:], 5, H - 1, ASR, AND, ["J3"], ["J4"])
         cp(T.J6[:], T.J4[:], ["J4"], ["J6"])
         ts(T.G1[:], T.EF[:, 0:H].indirect(T.J6[:, 0:2]), 257.0, None, MUL, None, ["EF", "J6"], ["G1"], gat(32))
         ts(RP[:], T.G1[:], 4, 255, SHR, AND, ["G1"], ["RP%d" % t])
         send((rank - 1 - t % (NR - 1)) % NR, T["RL%d" % t][:], RP[:], "rep%d" % t, "lp%d" % t, ["RP%d" % t])
+        part[0] = "own"
+        if apart:
+            for u in range(2):
+                mm(T.PD1[:, 32 * u:32 * u + 32], T.WF[:, 128 * u:128 * u + 128], SQ[:, 32:64], True, True,
+                   [own, "WF0", "WF1"], ["P_D1"])
+            hashes(T.PD1, "P_D1", 32, T.VI[:, 64:128], lambda a, b: T.VA[:, 64 + a:64 + b], T.VR[:, 32:64], T.V2[:, 32:64],
+                   T.HS[:, 32:64], "o", [(0, 32, 32.0)])
+        tt(T.H0[:], T.HS[:, 32:64], T.DK[:], MUL, [hn, "DK"], ["H0"])
         part[0] = "first"
-        tt(T.CH2[:], T.CG2[:, 2:4], T.CA2[:, 6:8], ADD, ["CG2", "CA2"], ["CHo"])
-        ts(T.H0[:], T.CH2[:], H - 1, None, AND, None, ["CHo"], ["H0"])
-        ts(T.E[:, 33:68:34], T.H0[:], 1.0, None, ADD, None, ["H0"], ["Eh"])
         for s in range(2):
-            ts(T.E[:, 34 * s + 1:34 * s + 33], T.HS[:, 32:64], T.E[:, 34 * s + 33:34 * s + 34], -1.0, SUB, EQ,
-               ["HAs", "Eh"], ["Ee%d" % s])
-        scan(T.ES[:], T.DD[:], T.E[:], MUL, MAX, ["DD", "Ee0", "Ee1", "Eh", "Ei"], ["ES"], cyc(68))
-        ts(T.DU[:], T.ES[:, 33:68:34], -1.0, None, ADD, None, ["ES"], ["DU"])
-        cp(T.TAG[:, 0:H + 64].indirect(T.DU[:, 0:2]), SQ[:, 32:64], ["DU", own], ["TAG", "TAGt"], sca(32))
+            h0 = T.E[:, 34 * s + 33:34 * s + 34]
+            op("v", lambda h0=h0, s=s: V.tensor_reduce(h0, T.H0[:, 16 * s:16 * s + 16], AX.X, ADD), ["H0"], ["Eh%d" % s])
+            ts(T.E[:, 34 * s + 1:34 * s + 33], T.HS[:, 32:64], h0, 0.25, EQ, MUL, [hn, "Eh%d" % s], ["Ee%d" % s])
+        scan(T.ES[:], T.DD[:], T.E[:], MUL, MAX, ["DD", "Ee0", "Ee1", "Eh0", "Eh1", "Ei"], ["ES"], cyc(68))
+        cp(T.DU[:], T.ES[:, 33:68:34], ["ES"], ["DU"])
+        cp(T.TAG[:, 0:H + 64].indirect(T.DU[:, 0:2]), SQ[:, 32:64], ["DU", own], ["TAG"], sca(32))
+        if t + 1 < C["twin"]:
+            part[0] = "twin"
+            cp(T.TAGS[:, 0:H + 64].indirect(T.DU[:, 0:2]), SQ[:, 32:64], ["DU", own], ["TAGS"], sca(32))
         part[0] = "efw"
         cp(T.EF[:, 0:H + 64].indirect(T.DU[:, 0:2]), T["RL%d" % t][:], ["DU"], ["EF", "EFt"], sca(32),
-           [("rep%d" % t, NENG)])
+           [many("rep%d" % t)])
 
     def slots(LN, lnn, sfx):
         part[0] = "gg"
         a = 0
         for eng, k in C["gg" + sfx]:
             b = a + k
+            part[0] = "gg%d" % (a // 1024)
             if LN is not None:
                 moved(eng, T.GB[:, a:b], T.IW[:, 0:2048].indirect(LN[:, a // 16:b // 16]), -32.0, ["IW", lnn],
                       blk("GB", a, b), k)
@@ -485,17 +615,22 @@ def rank_program(g, core, T, topo):
         part[0] = "diag"
         for h, nm in enumerate(C["dbank"]):
             PI, pi, a = T["P" + nm], "P_" + nm, 1024 * h
+            part[0] = "diag%d" % h
             for k in range(16):
-                mm(PI[:, 0:64], sel(T.ZB, k), T.GB[:, a + k:a + 1024:16], k == 0, k == 15, ["ZB"] + blk("GB", a, a + 1024),
-                   [pi])
-            ts(T.GL[:, 64 * h:64 * h + 64], PI[:, 0:64], -129.0, None, ADD, None, [pi], ["GL.%d" % h])
+                if C["gg" + sfx]:
+                    mm(PI[:, 0:64], sel(T.ZB, k), T.GB[:, a + k:a + 1024:16], k == 0, k == 15,
+                       ["ZB"] + blk("GB", a, a + 1024), [pi])
+                else:
+                    mm(PI[:, 0:64], sel(T.ZF, k), T.IW[:, a + k:a + 1024:16], k == 0, k == 15, ["ZF", "IW"], [pi], 256)
+            ts(T.GL[:, 64 * h:64 * h + 64], PI[:, 0:64], -129.0 * (1 if C["gg" + sfx] else 33), None, ADD, None, [pi],
+               ["GL.%d" % h])
 
     for t in range(ST):
         last = t == ST - 1
         LL, ln = T["LL%d" % (t % 2)], "LL%d" % (t % 2)
         LN, lnn = T["LL%d" % ((t + 1) % 2)], "LL%d" % ((t + 1) % 2)
         sfx = "F" if t == 0 else "L" if last else ""
-        part[1] = sfx or "-"
+        part[1], part[2] = sfx or "-", t
         for q in range(NP):
             b0, b1 = PARTS[q], PARTS[q + 1]
             n, p0, p1 = 16 * (b1 - b0), 16 * b0, 16 * b1
@@ -537,13 +672,18 @@ def rank_program(g, core, T, topo):
                 mm(T.PC[:, 128:128 + n], T.NEG[:], T.MN[:, a + 15:b:16], False, True, ["NEG"] + mnn, ["P_C"], n)
                 act(T.SP[:, a:b:16], T.PC[:, 128:128 + n], ACT.Copy, ["P_C"], spn, cyc(n))
             part[0] = "sj"
+            if last and NP == 1:
+                continue
             for j in range(b1 - b0):
                 mm(T.PC[:, p0 + 16 * j:p0 + 16 * j + 16], T.IDN[:], T.SP[:, a + 16 * j:b:n], True, True, ["IDN"] + spn,
                    ["P_C"])
             act(T.SJ[:, p0:p1], T.PC[:, p0:p1], ACT.Copy, ["P_C"], ["SJ" + sq], cyc(n))
         sjn = ["SJ%d" % q for q in range(NP)]
         part[0] = "pre"
-        compact(T.SJ, 8, 8, T.KB, T.KD, sjn, "")
+        if NP == 1:
+            compact(lambda a: T.SP[:, 128 * a:128 * a + 128:16], 8, T.KB, T.KD, blk("SP", 0, 128, 16), "")
+        else:
+            compact(lambda a: T.SJ[:, a:128:16], 8, T.KB, T.KD, sjn, "")
         for q in range(NP):
             b0, b1 = PARTS[q], PARTS[q + 1]
             n, p0, p1 = 16 * (b1 - b0), 16 * b0, 16 * b1
@@ -560,16 +700,20 @@ def rank_program(g, core, T, topo):
                 if kind == "s":
                     PD, pd = T["PD%d" % bank[0]], "P_D%d" % bank[0]
                     bank[0] = 1 - bank[0]
+                    part[0] = "s16"
                     mm(PD[:, 0:y - x], T.ZR[:], T.MK1[:, 0:y - x], True, False, ["ZR", "MK1"], [pd], y - x)
                     for m in range(16):
                         mm(PD[:, m:y - x:16], T.NEG[:], T.SP[:, x:y:16], False, False, ["NEG"] + spn, [pd])
+                    part[0] = "cost" + sq
                     act(T.D[:, x:y], tags, ACT.Copy, ["TAG"] + htn, dn, gat(y - x))
                     mm(PD[:, 0:y - x], T.IDN[:], T.D[:, x:y], False, True, ["IDN"] + dn, [pd], y - x)
                     act(T.N2[:, x:y], PD[:, 0:y - x], ACT.Abs, [pd], nn, cyc(y - x))
                 else:
                     sn = blk("S16", x, y, 16)
                     if kind in "vw":
+                        part[0] = "s16"
                         scan(T.S16[:, x:y], T.MK1[:, 0:y - x], T.SP[:, x:y], MUL, ADD, ["MK1"] + spn, sn, cyc((y - x) // 2))
+                        part[0] = "cost" + sq
                     else:
                         PD, pd = T["PD%d" % bank[0]], "P_D%d" % bank[0]
                         bank[0] = 1 - bank[0]
@@ -612,9 +756,10 @@ def rank_program(g, core, T, topo):
                 a = b
         part[0] = "inv"
         a = 0
-        for eng, k in C["inv" + sfx]:
-            to = T.IW[:, 0:2048].indirect(LL[:, 128 + a // 16:128 + (a + k) // 16])
-            r = [ln + "n"] + blk("J33", a, a + k, 128)
+        for i, (eng, k) in enumerate(C["inv" + sfx]):
+            part[0] = "inv%d" % i
+            to = T.IW[:, 0:2048].indirect(LL[:, a // 16:(a + k) // 16])
+            r = [ln, "ZR"] + blk("J33", 0, 16, 1)
             if eng == "s":
                 act(to, T.J33[:, a:a + k], ACT.Silu, r, ["IW"], sca(k))
             else:
@@ -633,31 +778,39 @@ def rank_program(g, core, T, topo):
             break
         un, ksn = ["U%d" % q for q in range(NP)], ["KS%d" % q for q in range(NP)]
         part[0] = "learn"
-        mm(T.PC[:, 0:8], T.LT[:], T.U9[:, 8:16], True, False, ["LT"] + un, ["P_C"])
-        mm(T.PC[:, 0:8], T.N256[:], T.U9[:, 8:16], False, False, ["N256"] + un, ["P_C"])
+        mm(T.PC[:, 0:8], T.IDN[:], T.CIC[:], True, False, ["IDN", "CIC"], ["P_C"])
+        r = ["LT", "OB", "NL0", "NL1", "NL2", "NL3", "U0"] + un
+        mm(T.PC[:, 0:8], T.LT[:], T.U9[:, 8:16], False, False, r, ["P_C"])
         for d in range(1, 8):
-            mm(T.PC[:, 0:8], T.OB[:], T.U9[:, 8 - d:16 - d], False, d == 7, ["OB", "U0"] + un, ["P_C"])
-        tt(T.POI[:], T.PC[:, 0:8], T.CIC[:], MIN, ["P_C", "CIC"], ["POI"])
-        ts(T.POS[:], T.POI[:], 255.0, None, ADD, None, ["POI"], ["POS"])
+            mm(T.PC[:, 0:8], T.OB[:], T.U9[:, 8 - d:16 - d], False, False, r, ["P_C"])
+        for j, (a, b, k) in enumerate(((0, 8, 1), (1, 8, 2), (2, 4, 1), (6, 8, 1), (4, 8, 1))):
+            z = (0, 1, 2, 2, 3)[j]
+            mm(T.PC[:, a:b:k], T.NL[:, 128 * z:128 * z + 128], T.U9[:, 8 + a:8 + b:k], False, j == 4, r, ["P_C"])
+        cp(T.POS[:], T.PC[:, 0:8], ["P_C"], ["POS"])
         SQ = T["SQ%d" % t]
-        cp(SQ[:, 32:288].indirect(T.POS[:, 0:8]), T.SJ[:], ["POS"] + sjn, ["SQo%d" % t], sca(128))
+        cp(SQ[:, 32:416].indirect(T.POS[:, 0:8]), T.SJ[:], ["POS"] + sjn, ["SQo%d" % t], sca(128))
         send((rank + 1 + t % (NR - 1)) % NR, SQ[:, 0:32], SQ[:, 32:64], "req%d" % t, "lq%d" % t, ["SQo%d" % t])
         part[0] = "count"
         for b in range(8):
             mm(T.PD0[:, 0:1], T.OB[:], T.U9[:, 8 + b:9 + b], b == 0, b == 7, ["OB"] + un, ["P_D0"])
-        ts(T.E[:, 0:68:34], T.SIG[:, 0:2], T.PD0[:, 0:1], None, GE, None, ["SIG", "P_D0"], ["Ei"])
+        ts(T.E[:, 0:68:34], T.SIG[:, 0:2], T.PD0[:, 0:1], 0.25, GE, MUL, ["SIG", "P_D0"], ["Ei"])
         part[0] = "cls"
-        op("v", lambda: V.tensor_reduce(T.RS[:, 0:1], T.KB[:, 61:446:48], AX.X, ADD), ksn + ["KSc"], ["RS0"])
-        mm(T.PS[:, 0:1], T.FOUR[:], T.RS[:, 0:1], True, True, ["FOUR", "RS0"], ["P_S"], 256)
-        ts(T.RS[:, 1:2], T.PS[:, 0:1], M33, M33, ADD, SUB, ["P_S"], ["RS1"])
-        ts(T.RS[:, 2:3], T.PS[:, 0:1], T.RS[:, 1:2], None, SUB, None, ["P_S", "RS1"], ["RS2"])
-        ts(T.O3[:], T.IOT[:], T.RS[:, 2:3], 448.0, ADD, ADD, ["IOTa", "IOTb", "RS2"], ["O3"])
-        cp(LN[:, 0:128], T.NB[:, 0:1024].indirect(T.O3[:, 0:8]), ["NB", "O3"], [lnn], gat(128))
-        part[0] = "clsn"
-        cp(LN[:, 128:256], T.NB[:, 0:1024].indirect(T.O3[:, 8:16]), ["NB", "O3"], [lnn + "n"], gat(128))
+        mm(T.PS[:, 0:11], T.FOUR[:], T.KB[:, 61:542:48], True, True, ["FOUR", "KSc"] + ksn, ["P_S"], 256)
+        mm(T.PS[:, 11:20], T.FOUR[:], T.KB[:, 61:446:48], True, True, ["FOUR", "KSc"] + ksn, ["P_S"], 256)
+        scan(T.RS[:], T.RD[:], T.PS[:, 0:20], MUL, ADD, ["RD", "P_S"], ["RS2"])
+        ts(T.O3[:], T.IOT[:, 0:8], T.RS[:, 19:20], 448.0, ADD, ADD, ["IOTa", "RS2"], ["O3"])
+        cp(LN[:], T.NB[:, 0:1024].indirect(T.O3[:, 0:8]), ["NB", "O3"], [lnn], gat(128))
         slots(LN, lnn, sfx)
         serve(t)
 
+    named = {}
+    for i, o in enumerate(ops):
+        named.setdefault((o["part"], o["eng"], o["t"]), []).append(i)
+    for eng, steps, chain in C.get("rules", ()):
+        for t in steps:
+            row = [named[p, eng, -9 if p in ("setup", "j33", "late", "zero") else t + dt][k] for p, k, dt in chain]
+            for a, b in zip(row, row[1:]):
+                ops[b]["order"].add(a)
     if C.get("fresh") or "seq" not in ORDER:
         ORDER["seq"] = improve(ops, issue_order(ops, C), C)
     seq = ORDER["seq"]

import math

from concourse.mybir import AluOpType as ALU, ActivationFunctionType as ACT, AxisListType as AX

NR, ST, H = 4, 5, 4096
MKW = 768
F32, BF, I32, U16 = "float32", "bfloat16", "int32", "uint16"
BIG = 524288.0
UB = 1048576
M33 = 12884901888.0


def _sb(n, d):
    return ("sbuf", [128, n], d)


SCRATCH = {
    "X": _sb(2048, BF), "GB": _sb(2048, BF), "A": _sb(2048, BF), "A2B": _sb(2048, BF),
    "MX": _sb(2048, BF), "MN": _sb(2048, BF), "SP": _sb(2048, BF), "S16": _sb(2048, BF),
    "NB": _sb(1024, I32), "NB0": _sb(128, I32), "TAG": _sb(H + 64, BF), "EF": _sb(H + 64, BF),
    "D": _sb(2048, BF), "N2": _sb(2048, BF), "TG2": _sb(512, BF), "M2": _sb(512, BF), "SJ": _sb(128, BF),
    "WB": _sb(8, BF), "THI": _sb(4, I32), "PC1": _sb(4, I32), "PI": _sb(8, I32), "CF": _sb(24, F32),
    "I144": _sb(144, F32), "I16": _sb(128, BF), "IM": _sb(128, BF), "PR0": _sb(128, BF),
    "BASE": _sb(128, F32), "Z": _sb(144, BF), "Z2": _sb(144, BF), "ZN": _sb(144, BF),
    "ZW1": _sb(144, BF), "ZW2": _sb(144, BF), "WF": _sb(256, BF), "WN": _sb(256, BF), "IDN": _sb(128, BF),
    "NEG": _sb(128, BF), "NL": _sb(512, BF), "ZR": _sb(128, BF), "OB": _sb(128, BF), "LT": _sb(128, BF),
    "IW": _sb(2048, F32), "J33": _sb(2048, F32), "ZB": _sb(144, BF), "ZF": _sb(144, F32), "GL": _sb(128, U16), "HB": _sb(16, F32), "JR": _sb(256, BF),
    "FOUR": _sb(128, F32), "MK1": _sb(MKW, BF), "MK2": _sb(MKW, BF), "RK": _sb(128, BF), "RT": _sb(128, BF),
    "IOT": _sb(16, F32), "IOT0": _sb(8, U16), "CIC": _sb(8, BF), "SIG": _sb(8, F32),
    "DD": _sb(68, F32), "DT": _sb(68, F32), "LL0": _sb(128, U16), "LL1": _sb(128, U16),
    "UI": _sb(256, I32), "UA": _sb(256, I32), "PR": _sb(128, F32), "P2": _sb(128, I32), "HA": _sb(128, I32),
    "HT": _sb(128, U16),
    "VI": _sb(128, I32), "VA": _sb(128, I32), "VR": _sb(64, F32), "V2": _sb(64, I32), "HS": _sb(64, I32),
    "HSU": _sb(32, U16),
    "CI": _sb(16, I32), "CA": _sb(16, I32), "CP": _sb(8, I32), "CG": _sb(8, I32),
    "CI2": _sb(4, I32), "CA2": _sb(4, I32), "CP2": _sb(2, I32),
    "KB": _sb(544, F32), "KD": _sb(24, F32), "K1": _sb(24, F32), "K3": _sb(8, I32),
    "K4": _sb(8, I32), "K6": _sb(16, U16), "U9": _sb(16, BF),
    "JB": _sb(128, F32), "JD": _sb(12, F32), "J1": _sb(6, F32), "J3": _sb(2, I32), "J4": _sb(2, I32),
    "J6": _sb(2, U16), "H0": _sb(32, F32), "DK": _sb(32, BF), "TAGS": _sb(H + 64, BF), "EV": _sb(128, F32), "IDX": _sb(128, U16),
    "RS": _sb(20, F32), "RD": _sb(20, F32), "O3": _sb(8, U16), "POS": _sb(8, U16),
    "G1": _sb(32, I32), "E": _sb(68, F32), "ES": _sb(68, F32), "DU": _sb(2, U16),
}
for _t in range(ST - 1):
    SCRATCH["SQ%d" % _t] = _sb(416, BF)
    SCRATCH["RP%d" % _t] = _sb(32, I32)
    SCRATCH["RL%d" % _t] = _sb(32, I32)
for _n in ("PU0", "PU1", "PK0", "PK1", "PC", "PD0", "PD1", "PS"):
    SCRATCH[_n] = ("psum", [128, 512], F32)

SEMAPHORES = (["qv", "qs", "qp", "qg", "d_nb0", "d_w", "d_x", "d_tag", "d_ef", "d_nb", "d_th", "d_twin"]
              + ["d_y%d" % i for i in range(8)]
              + ["req%d" % t for t in range(ST - 1)] + ["rep%d" % t for t in range(ST - 1)]
              + ["lq%d" % t for t in range(ST - 1)] + ["lp%d" % t for t in range(ST - 1)])

CFG = {
    "parts": [0, 3, 8],
    "ach": [[("v", 64), ("s", 192), ("s", 256), ("s", 256)], [("s", 448), ("s", 512), ("s", 320)]],
    "cost": [[("s", 10), ("v", 6)], [("s", 6), ("s", 6), ("v", 2), ("v", 2)]],
    "kord": {0: [0, 2, 1], 1: [5, 2, 4, 3, 0, 1]},
    "move": [[("v", 256), ("v", 192), ("v", 320)], [("v", 448), ("v", 832)]],
    "movei": [[("s", 768)], [("s", 640), ("v", 640)]],
    "invs": [0, 4],
    "inv": [[512, 512, 512, 512], [512, 512]],
    "invv": [256, 256, 256, 256],
    "home": [[("s", 1024), ("v", 1024)], [("s", 512), ("v", 512), ("s", 512), ("v", 512)]],
    "hend": [1, 2],
    "spv": [1, 1],
    "tg2": [("v", 16)],
    "neng": 16,
    "guess": [(0.9, 1.56, 3.8, 160.0, 2700.0), (1.1, 1.9, 2.2, 160.0, 3500.0), (1.1, 1.25, 5.3, 160.0, 2500.0)],
    "win": 40.0, "beta": 1.0, "moves": 2000, "slack": 0.002,
    "head": {"move0": -200.0, "cls": -900.0, "spre": 2200.0, "hash1": -200.0, "count": 1500.0, "move1": -3800.0,
             "learn": 100.0, "scost": 1200.0, "best0": 3000.0, "sig0": 2000.0, "cost0": -500.0, "shash": 2400.0,
             "first": 1100.0, "sbest": -500.0, "cost1": -1500.0, "pre": -400.0, "efw": -200.0},
}
CFG.update(dict(twin=1, parts=[0, 8], hend=[1], dbank=["U1", "K1"], guess=[(0.95, 1.56, 3.8, 150.0, 2700.0)], moves=0))
CFG.update({'ach':[[('v',576),('s',448),('s',512),('v',192),('s',320)]],'cost':[[('s',4),('v',4),('s',4),('v',4)]],'kord':{0:[1,4,2,0,5,3]},'move':[[('s',960),('v',1088)]],'inv':[('s',448),('s',512),('s',448),('v',64),('s',576)],'home':[('s',448),('v',448),('v',448),('s',128),('s',576)],'spv':[0],'tg2':[('s',4),('v',12)],'win':0.0,'beta':2.5,'gg':[('s',960),('v',576),('s',384),('s',128)],'achF':[[('v',448),('s',512),('v',512),('s',576)]],'achL':[[('v',512),('s',384),('s',512),('v',192),('s',128),('s',320)]],'costF':[[('v',5),('v',5),('s',4),('v',2)]],'costL':[[('s',3),('v',6),('s',4),('v',3)]],'kordF':{},'kordL':{},'moveF':[[('s',1024),('v',1024)]],'moveL':[[('s',896),('v',1152)]],'invF':[('s',384),('s',384),('s',448),('v',128),('s',704)],'invL':[('s',384),('s',768),('s',128),('v',192),('s',192),('s',384)],'ggF':[('s',1088),('v',640),('s',320)],'ggL':[('s',1728),('v',192),('s',128)],'head':{'sp0':1000,'count':-2200,'cls':6200,'home':1700,'shash':11300,'best0':-700,'scost':1800,'pre':-4700,'spre':2900,'sbest':1800,'sig0':600,'learn':300,'move0':6900,'clsn':-1600,'setup':4700,'diag':3900,'efw':-700,'sj':1900,'gg':1500,'hash0':3900,'inv':-2700,'cost0':-900,'first':-1000,'j33':8200,'late':-4500,'diagF':4500,'hash0F':2400,'sig0F':6700,'sjF':3700,'efwF':-8900,'homeF':500,'ggF':-500,'countF':-2800,'cost0F':6100,'clsnF':-600,'invF':2200,'clsF':-400,'learnF':-2700,'sbestF':800,'preF':3000,'move0F':3800,'sp0F':-700,'spreF':-1900,'shashF':2000,'best0F':-1500,'firstF':400,'best0L':-800,'sp0L':3600,'invL':1800,'move0L':-1500,'preL':3100,'diagL':-1100,'hash0L':2000,'homeL':-2300,'sig0L':100,'ggL':-2100,'cost0L':-700,'sjL':5700}})


CFG.update(eng={"req0": (0, 8), "rep0": (8, 16)}, first=2500.0, twin=1, when=None, moves=20000, slack=0.004, seed=1, start=(0.95, 1.56, 3.8, 150.0, 2400.0, 0.55),
           guess=[(0.88, 1.56, 3.8, 165.0, 2200.0, 0.55), (1.04, 1.56, 3.8, 110.0, 2600.0, 0.7), (1.1, 1.4, 4.6, 160.0, 2600.0, 0.45)])
CFG['head'].update({'setup':7200,'j33':6800,'late':-5700,'diagF':5800,'hash0F':3300,'sig0F':7200,'sjF':900,'efwF':-11900,'homeF':-5700,'ggF':-1000,'countF':400,'cost0F':2100,'invF':1300,'clsF':300,'learnF':-2700,'sbestF':6100,'preF':5500,'move0F':7500,'sp0F':-3200,'spreF':-3200,'shashF':4200,'best0F':-2500,'firstF':-2000,'ownF':4100,'scostF':-700})
CFG.update({'ach':[[('v',640),('s',576),('s',384),('v',192),('s',256)]],'cost':[[('s',4),('v',4),('s',4),('v',4)]],'move':[[('s',896),('v',1152)]],'inv':[('s',448),('s',256),('s',704),('v',128),('s',512)],'home':[('s',768),('v',576),('v',320),('s',256),('s',128)],'tg2':[('s',12),('v',4)],'gg':[('s',640),('v',576),('s',832)],'achF':[[('v',448),('s',128),('v',768),('s',704)]],'achL':[[('v',512),('s',320),('s',512),('v',320),('s',384)]],'costF':[[('v',5),('v',6),('s',2),('s',3)]],'costL':[[('s',3),('v',4),('s',4),('v',5)]],'moveF':[[('s',896),('v',1152)]],'moveL':[[('s',1024),('v',1024)]],'invF':[('s',320),('s',320),('s',448),('v',320),('s',640)],'invL':[('s',448),('s',576),('s',448),('v',192),('s',384)],'ggF':[('s',832),('v',896),('s',320)],'ggL':[('s',1472),('v',576)]})
CFG.update(row=256, moves=30000, slack=0.003, first=3000.0, guess=[(0.88, 1.56, 3.8, 165.0, 2200.0, 0.55), (1.04, 1.56, 3.8, 110.0, 2600.0, 0.7)])
CFG["head"] = {k: v for k, v in CFG["head"].items() if k[-1] != "L"}
CFG["head"].update(warm=20000,setup=9000,j33=9500,late=-6000,zero=-1000,invF=2500,sig0F=12000,hash0F=6000,clsF=3000,ggF=3000,preF=3000,ggL=-2000,diagL=-2000,invL=500)
CFG.update({'ach':[[('v',576),('s',640),('s',384),('v',256),('s',192)]],'cost':[[('s',4),('v',5),('s',4),('v',3)]],'move':[[('s',704),('v',1344)]],'inv':[('s',512),('s',256),('s',640),('v',128),('s',512)],'home':[('s',448),('v',832),('s',512),('v',256)],'tg2':[('s',14),('v',2)],'gg':[('s',832),('v',576),('s',640)],'achF':[[('v',640),('s',320),('v',576),('s',512)]],'achL':[[('v',640),('s',768),('s',256),('v',192),('s',192)]],'costF':[[('v',5),('v',5),('s',3),('s',3)]],'costL':[[('s',4),('v',4),('s',4),('v',4)]],'moveF':[[('s',1024),('v',1024)]],'moveL':[[('s',960),('v',1088)]],'invF':[('s',576),('s',512),('v',320),('s',640)],'invL':[('s',448),('s',448),('s',640),('v',256),('s',256)],'ggF':[('s',1024),('v',1024)],'ggL':[('s',2048)],'kordL':{0:[1,4,2,0,5,3]}})
CFG.update(twin=0, first=800.0, row=512, eng={}, seed=1, passes=[(34000, 0.0015, 0.6, 0.5), (10000, 0.001, 0.0, 0.0)])
CFG["head"].update(learn=3000, efw=-3000, sbest=5000)
CFG.update(j33v=4, seed=3, start=(0.95, 1.56, 3.8, 150.0, 3000.0, 0.55), passes=[(26000, 0.0015, 0.6, 0.5), (6000, 0.001, 0.0, 0.0)],
           guess=[(0.88, 1.56, 3.8, 165.0, 2900.0, 0.5), (1.04, 1.56, 3.8, 110.0, 2800.0, 0.7)])
CFG.update(seed=6, j33v=0, achF=[[('v', 512), ('s', 512), ('v', 448), ('s', 576)]],
           invF=[('s', 640), ('s', 512), ('v', 256), ('s', 640)])
CFG.update(early=[(0.88, 1.56, 3.8, 165.0, 2700.0, 0.25), (1.04, 1.56, 3.8, 110.0, 2800.0, 0.4)],
           passes=[(26000, 0.0015, 0.6, 0.5, "guess"), (6000, 0.001, 0.0, 0.0, "guess"), (14000, 0.0004, 0.6, 0.5, "early"),
                   (4000, 0.0004, 0.0, 0.0, "early")])
CFG.update(seed=3, early=[(0.85, 1.56, 3.8, 225.0, 2900.0, 0.35), (1.0, 1.56, 3.8, 130.0, 2700.0, 0.4)],
           passes=[(34000, 0.0015, 0.6, 0.5, "early"), (8000, 0.001, 0.0, 0.0, "early")])
ORDER = {}


def lengths(ops, guess):
    cy, gather, scatter, wake, remote, load = (tuple(guess) + (1.0,))[:6]
    cost = [(o["c"][0] + o["c"][1] * gather + o["c"][2] * scatter) * cy for o in ops]
    done = [remote if o["done"] is None else o["done"] and 1800.0 + (o["done"] - 1800.0) * load for o in ops]
    done[min(i for i, o in enumerate(ops) if o["done"] is None)] += CFG["first"]
    pred = [[(d, done[d] + wake) for d in o["deps"] | o["after"]] + [(d, 0.0) for d in o["order"]] for o in ops]
    return cost, done, pred


def improve(ops, seq, C):
    for moves, slack, mean, near, guess in C["passes"]:
        seq = refine(ops, seq, C, moves, slack, mean, near, C[guess])
    return seq


def refine(ops, seq, C, moves, slack, mean, near, guess):
    n = len(ops)
    eng = [o["eng"] for o in ops]
    guesses = [lengths(ops, z) for z in guess]
    before = [set(d for d, _ in p) for p in guesses[0][2]]
    final = [i for i in range(n) if ops[i]["part"] == "home"]

    def run(seq, k):
        cost, done, pred = guesses[k]
        end, by, last = [0.0] * n, [-1] * n, {}
        for i in seq:
            j = last.get(eng[i], -1)
            t = end[j] if j >= 0 else 0.0
            for d, lt in pred[i]:
                if end[d] + lt > t:
                    t, j = end[d] + lt, d
            end[i], by[i], last[eng[i]] = t + cost[i], j, i
        i = max(final, key=lambda z: end[z] + done[z])
        return end[i] + done[i] + mean * sum(end) / n, i, by

    def swap(seq, u, v, ahead):
        a, b = seq.index(u), seq.index(v)
        seg = seq[a:b + 1]
        mark = {v if ahead else u}
        if ahead:
            for i in reversed(seg):
                if i in mark:
                    mark.update(before[i])
        else:
            for i in seg:
                if not mark.isdisjoint(before[i]):
                    mark.add(i)
        if a > b or (u in mark and v in mark):
            return None
        return seq[:a] + [i for i in seg if (i in mark) == ahead] + [i for i in seg if (i in mark) != ahead] + seq[b + 1:]

    count, tag = {}, []
    for o in ops:
        k = (o["part"], o["t"], o["eng"])
        count[k] = count.get(k, 0) + 1
        tag.append((o["part"], o["eng"], count[k]))
    twin = {(tag[i], ops[i]["t"]): i for i in range(n)}
    state = [C["seed"]]

    def draw():
        state[0] = (state[0] * 6364136223846793005 + 1442695040888963407) % 2 ** 64
        return (state[0] >> 11) / 2.0 ** 53

    runs = [run(seq, k) for k in range(len(guesses))]
    unit = [z[0] for z in runs]
    now = best = float(len(runs))
    kept = seq
    for move in range(moves):
        _, i, by = runs[int(draw() * len(runs))]
        if draw() < near:
            i = n // 8 + int(draw() * (n - n // 8))
        links = []
        while by[i] >= 0:
            if eng[by[i]] == eng[i] and by[i] not in before[i]:
                links.append((by[i], i))
            i = by[i]
        if not links:
            continue
        u, v = links[int(draw() * (min(6, len(links)) if draw() < near else len(links)))]
        if draw() < 0.2:
            q = [i for i in seq if eng[i] == eng[u]]
            p, k = q.index(u), 1 + int(3 * draw())
            if draw() < 0.5:
                u = q[max(0, p - k)]
            else:
                v = q[min(len(q) - 1, p + 1 + k)]
        ahead = draw() < 0.5
        new = swap(seq, u, v, ahead)
        if new is None:
            continue
        if draw() < 0.8:
            for dt in (-3, -2, -1, 1, 2, 3):
                x, y = twin.get((tag[u], ops[u]["t"] + dt)), twin.get((tag[v], ops[v]["t"] + dt))
                if x is not None and y is not None:
                    new = swap(new, x, y, ahead) or new
        tried = [run(new, k) for k in range(len(guesses))]
        value = sum(z[0] / w for z, w in zip(tried, unit))
        if value <= now - slack * (1.0 - move / moves) * math.log(1.0 - draw()):
            seq, runs, now = new, tried, value
            if now < best:
                kept, best = seq, now
    return kept


def issue_order(ops, C):
    n = len(ops)
    cost, done, pred = lengths(ops, C["start"])
    succ = [[] for _ in range(n)]
    left = [len(p) for p in pred]
    for i in range(n):
        for d, lt in pred[i]:
            succ[d].append((i, lt))
    prio = [0.0] * n
    wait = list(left)
    topo_order = [i for i in range(n) if not wait[i]]
    for i in topo_order:
        for j, _ in succ[i]:
            wait[j] -= 1
            if not wait[j]:
                topo_order.append(j)
    assert len(topo_order) == n
    for i in reversed(topo_order):
        prio[i] = cost[i] + max([lt + prio[j] for j, lt in succ[i]] + [done[i]])
    top = {}
    for i, o in enumerate(ops):
        top[o["part"], o["t"]] = max(top.get((o["part"], o["t"]), 0.0), prio[i])
    when = C.get("when")
    if when:
        prio = [prio[i] - top[o["part"], o["t"]] - C["period"] * max(o["t"], 0) - when.get(o["step"], when[o["part"]])
                for i, o in enumerate(ops)]
        if C.get("static"):
            at = [0.0] * n
            for i, o in enumerate(ops):
                at[i] = max([C["period"] * max(o["t"], 0) + when.get(o["step"], when[o["part"]])]
                            + [at[d] + (cost[d] + lt if (ops[d]["part"], ops[d]["t"]) == (o["part"], o["t"]) else 1.0)
                               for d, lt in pred[i]])
            return sorted(range(n), key=lambda z: (at[z], z))
    else:
        short = lambda z: z.rstrip("0123456789") if z[:2] in ("in", "gg", "di") else z
        prio = [prio[i] + C["head"].get(short(o["part"]), 0.0) + C["head"].get(short(o["part"]) + o["step"][-1], 0.0)
                for i, o in enumerate(ops)]
        count = {}
        for i, o in enumerate(ops):
            k = (o["part"], o["t"], o["eng"])
            count[k] = count.get(k, 0) + 1
            prio[i] += C.get("fine", {}).get(o["part"] + o["eng"] + str(count[k]), 0)
    free, cand = {}, {}
    rdy = [0.0] * n
    for i in range(n):
        free[ops[i]["eng"]] = 0.0
        cand.setdefault(ops[i]["eng"], [])
        if left[i] == 0:
            cand[ops[i]["eng"]].append(i)
    seq = []
    while len(seq) < n:
        t0, e = min((max(free[e], min(rdy[i] for i in cand[e])), e) for e in cand if cand[e])
        i = max((j for j in cand[e] if rdy[j] <= t0 + C["win"]), key=lambda j: (prio[j], -j))
        end = t0 + cost[i]
        for j in cand[e]:
            if rdy[j] > t0 + C["win"] and prio[j] > prio[i] and (rdy[j] - t0) * C["beta"] < end - rdy[j]:
                i = j
        cand[e].remove(i)
        free[e] = max(t0, rdy[i]) + cost[i]
        seq.append(i)
        for j, lt in succ[i]:
            rdy[j] = max(rdy[j], free[e] + lt)
            left[j] -= 1
            if left[j] == 0:
                cand[ops[j]["eng"]].append(j)
    return seq


def rank_program(g, core, T, topo):
    rank = T.rank_of(core)
    if rank is None:
        return
    C = CFG
    PARTS, NENG = C["parts"], C["neng"]
    NP = len(PARTS) - 1
    Q = {"v": g.vector, "s": g.scalar, "p": g.tensor, "g": g, "y": g.sync}
    ops = []
    last_w, readers, sent = {}, {}, {}
    part = ["setup", "-", -9]

    def op(eng, fn, r=(), w=(), sem=None, ext=(), c=(64, 0, 0), done=0.0):
        me = len(ops)
        deps = set()
        for x in r:
            if x in last_w:
                deps.add(last_w[x])
            if x[:2] == "P_":
                deps.update(q for q in readers.get(x, ()) if ops[q]["eng"] != eng)
        for x in w:
            if x in last_w:
                deps.add(last_w[x])
            deps.update(readers.get(x, ()))
        order = set(d for d in deps if eng == "p" and ops[d]["eng"] == "p")
        after = set(sent[name] for name, _ in ext)
        ops.append({"eng": eng, "fn": fn, "deps": deps - order, "order": order, "after": after, "sem": sem,
                    "ext": list(ext), "need": False, "part": part[0], "step": part[0] + part[1], "c": c, "done": done,
                    "more": [], "t": part[2]})
        for x in r:
            readers.setdefault(x, []).append(me)
        for x in w:
            last_w[x] = me
            readers[x] = []
        return me

    V, S, P = g.vector, g.scalar, g.tensor
    cyc = lambda n: (max(64, n), 0, 0)
    gat = lambda n: (70, n, 0)
    sca = lambda n: (70, 0, n)
    blk = lambda name, a, b, k=64: ["%s.%d" % (name, j) for j in range(a // k, (b + k - 1) // k)]

    def ts(out, in0, s1, s2, o0, o1, r, w, c=cyc(64)):
        if o1 is None:
            return op("v", lambda: V.tensor_scalar(out, in0, s1, None, o0), r, w, c=c)
        return op("v", lambda: V.tensor_scalar(out, in0, s1, s2, o0, o1), r, w, c=c)

    def tt(out, a, b, o, r, w, c=cyc(64)):
        return op("v", lambda: V.tensor_tensor(out, a, b, o), r, w, c=c)

    def cp(out, a, r, w, c=cyc(64), ext=()):
        return op("v", lambda: V.tensor_copy(out, a), r, w, ext=ext, c=c)

    def ms(out, v, w, c=cyc(64)):
        return op("v", lambda: V.memset(out, v), (), w, c=c)

    def scan(out, d0, d1, o0, o1, r, w, c=cyc(64)):
        return op("v", lambda: V.tensor_tensor_scan(out, d0, d1, 0.0, o0, o1), r, w, c=c)

    def act(out, a, f, r, w, c=cyc(64), **kw):
        return op("s", lambda: S.activation(out, a, f, **kw), r, w, c=c)

    def mm(out, l, rhs, st, sp, r, w, n=64, ext=()):
        one = lambda: P.matmul(out, l, rhs, st, sp)
        o = ops[-1]
        if o.get("row") == (r, w, ext) and o["c"][0] + max(64, n) // 2 <= C["row"]:
            o["more"].append(one)
            o["c"] = (o["c"][0] + max(64, n) // 2, 0, 0)
        else:
            op("p", one, r, w, ext=ext, c=(max(64, n) // 2, 0, 0))
            ops[-1]["row"] = (r, w, ext)

    def iota(out, pat, base, cm, w, n, flag=True):
        if flag:
            op("g", lambda: g.iota(out, pat, base, cm, allow_small_or_imprecise_dtypes=True), (), w, c=cyc(157 + 2 * n))
        else:
            op("g", lambda: g.iota(out, pat, base, cm), (), w, c=cyc(157 + 2 * n))

    def dma(eng, out, a, sem, r, w, done, **kw):
        op(eng, lambda: Q[eng].dma_start(out, a, **kw), r, list(w) + ["Q" + eng], sem=(sem, 16, True),
           c=cyc(500 if eng == "g" else 64), done=done)
        o = ops[-1]
        prev = set(d for d in o["deps"] if ops[d]["eng"] == eng and ops[d]["sem"] is not None)
        o["deps"] = o["deps"] - prev
        o["order"] = prev

    def send(dst_rank, out, a, rsem, lsem, r):
        dst = T.cores[dst_rank]
        rid, pid = topo.addr(dst)[0], topo.addr(dst)[1]
        m = 0
        lo, hi = C["eng"].get(rsem, (0, NENG))
        for e in topo.engines(core, dst)[lo:hi]:
            m |= 1 << e
        sent[rsem] = op("g", lambda: g.remote_dma(out, a, T.sem[rsem], T.sem[lsem], pid, rid, m), r, (),
                        sem=(lsem, hi - lo, False), c=cyc(550), done=None)

    def moved(eng, out, src, add, r, w, n):
        if eng == "s":
            return act(out, src, ACT.Identity, r, w, gat(n), bias=add)
        return ts(out, src, add, None, ADD, None, r, w, gat(n))

    AND, SHR, ASR, ADD, SUB, MUL, MAX, MIN = (ALU.bitwise_and, ALU.logical_shift_right, ALU.arith_shift_right, ALU.add,
                                              ALU.subtract, ALU.mult, ALU.max, ALU.min)
    EQ, GE, GT = ALU.is_equal, ALU.is_ge, ALU.is_gt
    CF = T.CF
    col = lambda j: CF[:, j:j + 1]
    cK, cG, cO, cK8, cH, cP, c17K, cM, cZ, cW1, cW2, cV1, cV2, cTH, cE, cB, cN, cQ = range(18)

    c0 = rank % 8
    dma("y", T.X[:], T.x[:], "d_x", (), blk("X", 0, 2048), 4200.0)
    dma("s", T.NB0[:], T.nb[:, c0 * 128:c0 * 128 + 128], "d_nb0", (), ["NB0"], 2400.0)
    dma("s", T.WB[:, 0:2], T.w[:], "d_w", (), ["WB"], 2400.0)
    dma("y", T.TAG[:, 0:H], T.tag[:], "d_tag", (), ["TAG"], 9000.0)
    dma("y", T.NB[:], T.nb[:], "d_nb", (), ["NB"], 11700.0)
    dma("y", T.EF[:, 0:H], T.ef[:], "d_ef", (), ["EF"], 16600.0)
    if C["twin"]:
        dma("y", T.TAGS[:, 0:H], T.tag[:], "d_twin", (), ["TAGS"], 21500.0)

    iota(T.PC1[:, 0:1], [[0, 1]], 0, 1, ["PC1"], 1, False)
    iota(T.I144[:], [[1, 144]], 0, 0, ["I144"], 144)
    iota(T.I16[:], [[1, 8], [0, 16]], 0, 0, ["I16"], 128)
    dma("g", T.THI[:, 0:1], T.th[:], "d_th", ["I16"], ["THI"], 4000.0, allow_slow_non_contiguous=True)
    for q in range(NP):
        b0, b1 = PARTS[q], PARTS[q + 1]
        iota(T.BASE[:, 16 * b0:16 * b1], [[256, b1 - b0], [256 * (b1 - b0), 16]], 0, 0, ["BASE%d" % q], 16 * (b1 - b0))

    ms(T.MK1[:], 1.0, ["MK1"], cyc(MKW // 2))
    ms(T.MK2[:], 0.0, ["MK2"], cyc(MKW // 2))
    ms(T.MK1[:, 0:MKW:16], 0.0, ["MK1"])
    ms(T.MK2[:, 0:MKW:16], 512.0, ["MK2"])
    part[0] = "zero"
    for j in range(4):
        iota(T.SP[:, 512 * j:512 * j + 512], [[0, 512]], 0, 0, blk("SP", 32 * j, 32 * j + 32, 16), 512)
    part[0] = "setup"
    ts(T.PI[:, 0:1], T.PC1[:, 0:1], 15, None, AND, None, ["PC1"], ["PI0"])
    ts(T.PI[:, 1:2], T.PC1[:, 0:1], 4, None, SHR, None, ["PC1"], ["PI1"])
    ts(T.PI[:, 2:3], T.PC1[:, 0:1], 1, None, AND, None, ["PC1"], ["PI2"])
    ts(T.PI[:, 3:4], T.PC1[:, 0:1], 7, None, AND, None, ["PC1"], ["PI3"])
    ts(T.PI[:, 4:5], T.PC1[:, 0:1], 3, 1, SHR, AND, ["PC1"], ["PI4"])
    cp(CF[:, 0:5], T.PI[:, 0:5], ["PI0", "PI1", "PI2", "PI3", "PI4"], ["CF"])
    cp(col(cP), T.PC1[:, 0:1], ["PC1"], ["cP"])
    ts(col(cQ), col(cK8), 16.0, col(cH), MUL, ADD, ["CF"], ["cQ"])
    ts(T.IOT[:, 0:8], T.I144[:, 0:16:2], col(cQ), None, ADD, None, ["I144", "cQ"], ["IOTa"])
    ts(T.IOT[:, 8:16], T.I144[:, 0:128:16], col(cK), None, ADD, None, ["I144", "CF"], ["IOTb"])
    for j, src, sc, bi in ((cZ, cG, 16.0, 15.0), (c17K, cK, 17.0, 0.0), (cM, cK, -64.0, 992.0)):
        act(col(j), col(src), ACT.Identity, ["CF"], ["c%d" % j], scale=sc, bias=bi)
    cp(T.IOT0[:], T.IOT[:, 0:8], ["IOTa"], ["IOT0"])
    cp(T.LL0[:], T.NB0[:, 0:128].indirect(T.IOT0[:, 0:8]), ["NB0", "IOT0"], ["LL0"], gat(128))

    cp(CF[:, cW1:cW1 + 2], T.WB[:, 0:2], ["WB"], ["cW"])
    ts(CF[:, cV1:cV1 + 2], T.WB[:, 0:2], 1.0 / 32, None, MUL, None, ["WB"], ["cV"])
    ts(T.Z[:], T.I144[:], col(cZ), 32.0, EQ, MUL, ["I144", "c%d" % cZ], ["Z"], cyc(144))
    for u in range(2):
        ts(T.WF[:, 128 * u:128 * u + 128], T.I16[:], col(cG), col(cW1 + u), EQ, MUL, ["I16", "CF", "cW"], ["WF%d" % u])
    ts(T.WN[:], T.WF[:], -1.0, None, MUL, None, ["WF0", "WF1"], ["WN"], cyc(128))
    ts(T.ZW1[:], T.Z[:], col(cV1), None, MUL, None, ["Z", "cV"], ["ZW0"], cyc(72))
    ts(T.ZW2[:], T.Z[:], col(cV2), None, MUL, None, ["Z", "cV"], ["ZW1"], cyc(72))
    ts(T.IDN[:], T.I144[:, 0:128], col(cP), None, EQ, None, ["I144", "cP"], ["IDN"], cyc(128))
    ts(T.NEG[:], T.IDN[:], -1.0, None, MUL, None, ["IDN"], ["NEG"])
    part[0] = "warm"
    act(T.ZR[:], T.I144[:, 0:128], ACT.Silu, ["I144"], ["ZR"], cyc(1700), scale=0.0)
    part[0] = "late"
    iota(T.PR0[:], [[0, 128]], int(BIG), 0, ["PR0"], 128)
    for buf, nm, v in ((T.RK, "RK", 0.0), (T.RT, "RT", 2.0)):
        op("g", lambda buf=buf, v=v: g.affine_select(buf[:], T.PR0[:], [[0, 8], [1, 16]], EQ, v, 0, 0), ["PR0"], [nm],
           c=cyc(460))
    part[0] = "setup"
    ts(T.OB[:], T.I16[:], col(cG), 1.0 / UB, EQ, MUL, ["I16", "CF"], ["OB"])
    ts(col(cTH), T.THI[:, 0:1], 32.0, None, MUL, None, ["THI"], ["cTH"])
    part[0] = "j33"
    for q in range(NP):
        b0, b1 = PARTS[q], PARTS[q + 1]
        iota(T.JR[:, 16 * b0:16 * b1], [[0, 2], [16, 8], [0, b1 - b0]], 0, 0, ["JR0"], 16 * (b1 - b0))
        iota(T.JR[:, 128 + 16 * b0:128 + 16 * b1], [[1, 2], [0, 8], [2, b1 - b0]], 2 * b0, 0, ["JR1"], 16 * (b1 - b0))
    act(col(cE), col(cO), ACT.Identity, ["CF"], ["cE"], scale=-1.0, bias=1.0)
    act(T.JR[:, 0:128], T.JR[:, 0:128], ACT.Copy, ["JR0", "cE"], ["JR0"], cyc(128), scale=col(cE))
    act(T.JR[:, 128:256], T.JR[:, 128:256], ACT.Copy, ["JR1", "CF"], ["JR1"], cyc(128), scale=col(cO))
    tt(T.JR[:, 0:128], T.JR[:, 0:128], T.JR[:, 128:256], ADD, ["JR0", "JR1"], ["JR0"], cyc(256))
    act(T.HB[:], T.I144[:, 0:16], ACT.Identity, ["I144", "cE"], ["HB"], scale=col(cE), bias=33.0)
    for j in range(16):
        if j < C["j33v"]:
            ts(T.J33[:, j:2048:16], T.JR[:, 0:128], T.HB[:, j:j + 1], None, ADD, None, ["JR0", "HB"], ["J33.%d" % j],
               cyc(128))
        else:
            act(T.J33[:, j:2048:16], T.JR[:, 0:128], ACT.Identity, ["JR0", "HB"], ["J33.%d" % j], cyc(128),
                bias=T.HB[:, j:j + 1])
    part[0] = "late"
    act(col(cB), col(cO), ACT.Identity, ["CF"], ["cB"], scale=127.0 / 256, bias=1.0 / 256)
    ts(T.ZB[:], T.Z[:], col(cB), None, MUL, None, ["Z", "cB"], ["ZB"], cyc(72))
    if not C["ggL"]:
        act(T.ZF[:], T.Z[:], ACT.Copy, ["Z", "cB"], ["ZF"], cyc(144), scale=col(cB))
    ts(T.Z2[:], T.Z[:], 2.0, None, MUL, None, ["Z"], ["Z2"], cyc(72))
    ts(T.ZN[:], T.Z[:], -1.0, None, MUL, None, ["Z"], ["ZN"], cyc(72))
    act(col(cN), col(cK), ACT.Identity, ["CF"], ["cN"], scale=-1.0 / UB, bias=-129.0 / UB)
    for j, z in enumerate((col(cN), -16.0 / UB, -32.0 / UB, -64.0 / UB)):
        ts(T.NL[:, 128 * j:128 * j + 128], T.IDN[:], z, None, MUL, None, ["IDN", "cN"], ["NL%d" % j])
    iota(T.KD[:], [[0, 8], [-1, 3]], 0, 0, ["KDa", "KD"], 24)
    iota(T.JD[:], [[0, 4], [-1, 3]], 0, 0, ["JDa", "KD2"], 12)
    iota(T.U9[:, 0:8], [[0, 8]], 0, 0, ["U0"], 8)
    iota(T.FOUR[:], [[0, 128]], 4, 0, ["FOUR"], 128)
    op("g", lambda: g.affine_select(T.LT[:], T.OB[:], [[1, 128]], GE, 0.0, 0, -1), ["OB"], ["LT"], c=cyc(460))
    for t in range(ST - 1):
        iota(T["SQ%d" % t][:, 32:64], [[0, 32]], 0, 0, ["SQo%d" % t], 32)
    act(T.EF[:, H:H + 16], T.I144[:, 0:16], ACT.Identity, ["I144", "c%d" % c17K], ["EFt"], scale=0.0, bias=col(c17K))
    for j, v in enumerate((-112.0, M33 / 4, -M33 / 4)):
        act(T.KB[:, 445 + 48 * j:446 + 48 * j], T.IDN[:, 0:1], ACT.Copy, ["IDN"] + ["KSc"][:j], ["KSc"], scale=v)
    iota(T.RD[:], [[0, 20]], 1, 0, ["RD"], 20)
    iota(T.RD[:, 11:12], [[0, 1]], -1, 0, ["RD"], 1)
    act(T.CIC[:], T.IOT[:, 8:16], ACT.Identity, ["IOTb"], ["CIC"], bias=128.0)
    act(T.SIG[:, 0:2], T.I144[:, 0:32:16], ACT.Identity, ["I144", "CF"], ["SIG"], bias=col(cK))
    for j, sc, v in ((1, 1.0, 1.0), (2, 4.0, 4 * 4097.0 - 1)):
        act(T.SIG[:, 2 * j:2 * j + 2], T.SIG[:, 0:2], ACT.Identity, ["SIG"], ["SIG%d" % j], scale=sc, bias=v)
    iota(T.IM[:, 0:32], [[0, 2], [1, 16]], 0, 0, ["IM"], 32)
    ts(T.DK[:], T.IM[:, 0:32], col(cK), None, EQ, None, ["IM", "CF"], ["DK"])
    for s in range(2):
        ts(T.DT[:, 34 * s:34 * s + 34], T.I144[:, 0:34], T.SIG[:, 2 + s:3 + s], T.SIG[:, 4 + s:5 + s], EQ, MUL,
           ["I144", "SIG1", "SIG2"], ["DT%d" % s])
    act(T.DD[:], T.DT[:], ACT.Identity, ["DT0", "DT1"], ["DD"], bias=1.0)
    act(T.DD[:, 0:68:34], T.I144[:, 0:2], ACT.Copy, ["I144"], ["DD"], scale=0.0)

    sel = lambda buf, a: buf[:, 15 - a:143 - a]
    W = T.TAG[:, 0:H]
    bank = [0]

    def compact(src, n, KB, KD, r, sfx, ext=()):
        CI, CA, CP, CG, k = T["CI" + sfx], T["CA" + sfx], T["CP" + sfx], T.CG, n
        for u, buf in enumerate((T.ZW1, T.ZW2)):
            for a in range(16):
                mm(T.PC[:, u * n:u * n + n], sel(buf, a), src(a), a == 0, a == 15, r + ["ZW%d" % u], ["P_C"], 64, ext)
        cp(CI[:], T.PC[:, 0:2 * n], ["P_C"], ["CI" + sfx])
        ts(CA[:], CI[:], H - 1, None, AND, None, ["CI" + sfx], ["CA" + sfx])
        tt(CP[:], CA[:, 0:n], CA[:, n:2 * n], MUL, ["CA" + sfx], ["CP" + sfx])
        if sfx:
            ts(KD[:, 2:3 * n:3], CA[:, n:2 * n], -4096.0, -32.0, ADD, MUL, ["CA" + sfx], ["KD" + sfx])
            tt(KB[:, 77:30 + 48 * k:48], CP[:, 0:k], KD[:, 2:3 * k:3], SUB, ["CP" + sfx, "KD" + sfx], ["CH" + sfx])
            return
        ts(CG[:], CP[:], 5, H - 1, SHR, AND, ["CP" + sfx], ["CG" + sfx])
        ts(KD[:, 2:3 * k:3], CA[:, n:n + k], -1.0, None, MUL, None, ["CA" + sfx], ["KD" + sfx])
        tt(KB[:, 77:30 + 48 * k:48], CG[:, 0:k], CA[:, n:n + k], ADD, ["CG" + sfx, "CA" + sfx], ["CH" + sfx])

    def least(KB, KD, K1, PK, pk, b0, b1, sfx, c):
        n = 16 * (b1 - b0)
        scan(KB[:, 48 * b0 + 16:48 * b1 + 16:3], T.RK[:, 0:n], PK[:, 0:n], ADD, MIN, ["RK", pk], ["KS" + sfx], cyc(n))
        scan(KB[:, 48 * b0:48 * b1:3], T.RT[:, 0:n], PK[:, 0:n], ADD, MIN, ["RT", pk], ["KT" + sfx], cyc(n))
        scan(K1[:, 3 * b0:3 * b1], KD[:, 3 * b0:3 * b1], KB[:, 48 * b0 + 45:48 * b1 + 30:16], MUL, ADD,
             ["KS" + sfx, "KT" + sfx, "KD" + c, "CH" + c, "KDa", "JDa"], ["K1" + sfx])

    def hashes(PU, pn, n, UI, UA, PR, P2, HA, sfx, cs):
        cp(UI, PU[:, 0:2 * n], [pn], ["UI" + sfx], cyc(2 * n))
        ts(UA(0, 2 * n), UI, H - 1, None, AND, None, ["UI" + sfx], ["UA" + sfx], cyc(2 * n))
        tt(PR, UA(0, n), UA(n, 2 * n), MUL, ["UA" + sfx], ["PR" + sfx], cyc(2 * n))
        for j, (a, b, c) in enumerate(cs):
            ts(PU[:, 2 * n + a:2 * n + b], UA(n + a, n + b), -4096.0, c, ADD, MUL, ["UA" + sfx, "c%d" % cM, pn],
               ["PA%d" % j + sfx], cyc(b - a))
        tt(P2, PR, PU[:, 2 * n:3 * n], ADD, ["PR" + sfx, pn] + ["PA%d" % j + sfx for j in range(len(cs))], ["P2" + sfx],
           cyc(n))
        ts(HA, P2, 5, H - 1, ASR, AND, ["P2" + sfx], ["HA" + sfx], cyc(n))

    def serve(t):
        SQ, RP = T["SQ%d" % t], T["RP%d" % t]
        many = lambda z: (z, C["eng"].get(z, (0, NENG))[1] - C["eng"].get(z, (0, NENG))[0])
        arr = [many("req%d" % t)]
        own = "SQo%d" % t
        apart = t < C["twin"]
        TS, tsn, k, hn = (T.TAGS, "TAGS", 32, "HAo") if apart else (T.TAG, "TAG", 64, "HAs")
        part[0] = "shash"
        for u in range(2):
            wf = T.WF[:, 128 * u:128 * u + 128]
            for s in range(2):
                mm(T.PU0[:, k * u + s:k * u + 32:2], wf, SQ[:, 16 * s:16 * s + 16], True, True, ["WF0", "WF1", own],
                   ["P_U0"], 64, arr)
            if not apart:
                mm(T.PU0[:, 64 * u + 32:64 * u + 64], wf, SQ[:, 32:64], True, True, ["WF0", "WF1", own], ["P_U0"], 64, arr)
        hashes(T.PU0, "P_U0", k, T.VI[:, 0:2 * k], lambda a, b: T.VA[:, a:b], T.VR[:, 0:k], T.V2[:, 0:k], T.HS[:, 0:k], "s",
               [(0, 32, col(cM)), (32, 64, 32.0)][:k // 32])
        cp(T.HSU[:], T.HS[:, 0:32], ["HAs"], ["HSU"])
        part[0] = "spre"
        compact(lambda a: SQ[:, a:32:16], 2, T.JB, T.JD, [], "2", arr)
        part[0] = "scost"
        for s in range(2):
            for m in range(16):
                mm(T.PS[:, 16 * s + m:512:32], T.IDN[:], SQ[:, 16 * s:16 * s + 16], True, True, ["IDN"], ["P_S"], 64, arr)
        a0 = 0
        for eng, k in C["tg2"]:
            x, y, nm = 32 * a0, 32 * (a0 + k), str(a0)
            tags = TS[:, 0:H].indirect(T.HSU[:, x // 16:y // 16])
            if eng == "s":
                act(T.TG2[:, x:y], tags, ACT.Copy, [tsn, "HSU"], ["TG2" + nm], gat(y - x))
            else:
                cp(T.TG2[:, x:y], tags, [tsn, "HSU"], ["TG2" + nm], gat(y - x))
            tt(T.M2[:, x:y], T.TG2[:, x:y], T.PS[:, x:y], MAX, ["TG2" + nm, "P_S"], ["M2" + nm], cyc(y - x))
            for j, (z, buf, r) in enumerate(((T.ZN, T.TG2, ["ZN", "TG2" + nm]), (T.Z2, T.M2, ["Z2", "M2" + nm]))):
                for a in range(a0, a0 + k):
                    mm(T.PK1[:, 0:32], sel(z, a), buf[:, 32 * a:32 * a + 32], j + a == 0, j + a == 16, r, ["P_K1"])
            a0 += k
        part[0] = "sbest"
        least(T.JB, T.JD, T.J1, T.PK1, "P_K1", 0, 2, "s", "2")
        cp(T.J3[:], T.J1[:, 2:6:3], ["K1s"], ["J3"])
        ts(T.J4[:], T.J3[:], 5, H - 1, ASR, AND, ["J3"], ["J4"])
        cp(T.J6[:], T.J4[:], ["J4"], ["J6"])
        ts(T.G1[:], T.EF[:, 0:H].indirect(T.J6[:, 0:2]), 257.0, None, MUL, None, ["EF", "J6"], ["G1"], gat(32))
        ts(RP[:], T.G1[:], 4, 255, SHR, AND, ["G1"], ["RP%d" % t])
        send((rank - 1 - t % (NR - 1)) % NR, T["RL%d" % t][:], RP[:], "rep%d" % t, "lp%d" % t, ["RP%d" % t])
        part[0] = "own"
        if apart:
            for u in range(2):
                mm(T.PD1[:, 32 * u:32 * u + 32], T.WF[:, 128 * u:128 * u + 128], SQ[:, 32:64], True, True,
                   [own, "WF0", "WF1"], ["P_D1"])
            hashes(T.PD1, "P_D1", 32, T.VI[:, 64:128], lambda a, b: T.VA[:, 64 + a:64 + b], T.VR[:, 32:64], T.V2[:, 32:64],
                   T.HS[:, 32:64], "o", [(0, 32, 32.0)])
        tt(T.H0[:], T.HS[:, 32:64], T.DK[:], MUL, [hn, "DK"], ["H0"])
        part[0] = "first"
        for s in range(2):
            h0 = T.E[:, 34 * s + 33:34 * s + 34]
            op("v", lambda h0=h0, s=s: V.tensor_reduce(h0, T.H0[:, 16 * s:16 * s + 16], AX.X, ADD), ["H0"], ["Eh%d" % s])
            ts(T.E[:, 34 * s + 1:34 * s + 33], T.HS[:, 32:64], h0, 0.25, EQ, MUL, [hn, "Eh%d" % s], ["Ee%d" % s])
        scan(T.ES[:], T.DD[:], T.E[:], MUL, MAX, ["DD", "Ee0", "Ee1", "Eh0", "Eh1", "Ei"], ["ES"], cyc(68))
        cp(T.DU[:], T.ES[:, 33:68:34], ["ES"], ["DU"])
        cp(T.TAG[:, 0:H + 64].indirect(T.DU[:, 0:2]), SQ[:, 32:64], ["DU", own], ["TAG"], sca(32))
        if t + 1 < C["twin"]:
            part[0] = "twin"
            cp(T.TAGS[:, 0:H + 64].indirect(T.DU[:, 0:2]), SQ[:, 32:64], ["DU", own], ["TAGS"], sca(32))
        part[0] = "efw"
        cp(T.EF[:, 0:H + 64].indirect(T.DU[:, 0:2]), T["RL%d" % t][:], ["DU"], ["EF", "EFt"], sca(32),
           [many("rep%d" % t)])

    def slots(LN, lnn, sfx):
        part[0] = "gg"
        a = 0
        for eng, k in C["gg" + sfx]:
            b = a + k
            part[0] = "gg%d" % (a // 1024)
            if LN is not None:
                moved(eng, T.GB[:, a:b], T.IW[:, 0:2048].indirect(LN[:, a // 16:b // 16]), -32.0, ["IW", lnn],
                      blk("GB", a, b), k)
            elif eng == "s":
                act(T.GB[:, a:b], T.IW[:, a:b], ACT.Identity, ["IW"], blk("GB", a, b), cyc(k), bias=-32.0)
            else:
                ts(T.GB[:, a:b], T.IW[:, a:b], -32.0, None, ADD, None, ["IW"], blk("GB", a, b), cyc(k))
            a = b
        part[0] = "diag"
        for h, nm in enumerate(C["dbank"]):
            PI, pi, a = T["P" + nm], "P_" + nm, 1024 * h
            part[0] = "diag%d" % h
            for k in range(16):
                if C["gg" + sfx]:
                    mm(PI[:, 0:64], sel(T.ZB, k), T.GB[:, a + k:a + 1024:16], k == 0, k == 15,
                       ["ZB"] + blk("GB", a, a + 1024), [pi])
                else:
                    mm(PI[:, 0:64], sel(T.ZF, k), T.IW[:, a + k:a + 1024:16], k == 0, k == 15, ["ZF", "IW"], [pi], 256)
            ts(T.GL[:, 64 * h:64 * h + 64], PI[:, 0:64], -129.0 * (1 if C["gg" + sfx] else 33), None, ADD, None, [pi],
               ["GL.%d" % h])

    for t in range(ST):
        last = t == ST - 1
        LL, ln = T["LL%d" % (t % 2)], "LL%d" % (t % 2)
        LN, lnn = T["LL%d" % ((t + 1) % 2)], "LL%d" % ((t + 1) % 2)
        sfx = "F" if t == 0 else "L" if last else ""
        part[1], part[2] = sfx or "-", t
        for q in range(NP):
            b0, b1 = PARTS[q], PARTS[q + 1]
            n, p0, p1 = 16 * (b1 - b0), 16 * b0, 16 * b1
            sq = str(q)
            part[0] = "sig" + sq
            a = 16 * p0
            for eng, k in C["ach" + sfx][q]:
                b = a + k
                if t == 0:
                    src, r = T.X[:, 0:2048].indirect(LL[:, a // 16:b // 16]), blk("X", 0, 2048) + [ln]
                else:
                    src, r = T.A2B[:, 0:2048].indirect(T.GL[:, a // 16:b // 16]), blk("B", 0, 2048) + blk("GL", a // 16, b // 16)
                moved(eng, T.A[:, a:b], src, 0.0, r, blk("A", a, b), k)
                scan(T.MX[:, a:b], T.MK1[:, 0:k], T.A[:, a:b], MUL, MAX, ["MK1"] + blk("A", a, b), blk("MX", a, b),
                     cyc(k // 2))
                scan(T.MN[:, a:b], T.MK2[:, 0:k], T.A[:, a:b], ADD, MIN, ["MK2"] + blk("A", a, b), blk("MN", a, b),
                     cyc(k // 2))
                a = b
            a, b = 16 * p0, 16 * p1
            mxn, mnn, spn = blk("MX", a, b), blk("MN", a, b), blk("SP", p0, p1, 16)
            if q + 1 in C["hend"]:
                part[0] = "hash" + sq
                k = C["hend"].index(q + 1)
                h0 = 16 * PARTS[([0] + C["hend"])[k]]
                PU, pu, hn = T["PU%d" % (k % 2)], "P_U%d" % (k % 2), p1 - h0
                for u in range(2):
                    mm(PU[:, hn * u:hn * u + hn], T.WF[:, 128 * u:128 * u + 128], T.MX[:, 16 * h0 + 15:b:16], True, False,
                       blk("MX", 16 * h0, b) + ["WF%d" % u], [pu], hn)
                    mm(PU[:, hn * u:hn * u + hn], T.WN[:, 128 * u:128 * u + 128], T.MN[:, 16 * h0 + 15:b:16], False, True,
                       blk("MN", 16 * h0, b) + ["WN"], [pu], hn)
                hashes(PU, pu, hn, T.UI[:, 2 * h0:2 * p1], lambda x, y, o=2 * h0: T.UA[:, o + x:o + y], T.PR[:, h0:p1],
                       T.P2[:, h0:p1], T.HA[:, h0:p1], sq, [(0, hn, col(cM))])
                cp(T.HT[:, h0:p1], T.HA[:, h0:p1], ["HA" + sq], blk("HT", h0, p1, 16), cyc(hn))
            part[0] = "sp" + sq
            if C["spv"][q]:
                tt(T.SP[:, a:b:16], T.MX[:, a + 15:b:16], T.MN[:, a + 15:b:16], SUB, mxn + mnn, spn, cyc(2 * n))
            else:
                mm(T.PC[:, 128:128 + n], T.IDN[:], T.MX[:, a + 15:b:16], True, False, ["IDN"] + mxn, ["P_C"], n)
                mm(T.PC[:, 128:128 + n], T.NEG[:], T.MN[:, a + 15:b:16], False, True, ["NEG"] + mnn, ["P_C"], n)
                act(T.SP[:, a:b:16], T.PC[:, 128:128 + n], ACT.Copy, ["P_C"], spn, cyc(n))
            part[0] = "sj"
            if last and NP == 1:
                continue
            for j in range(b1 - b0):
                mm(T.PC[:, p0 + 16 * j:p0 + 16 * j + 16], T.IDN[:], T.SP[:, a + 16 * j:b:n], True, True, ["IDN"] + spn,
                   ["P_C"])
            act(T.SJ[:, p0:p1], T.PC[:, p0:p1], ACT.Copy, ["P_C"], ["SJ" + sq], cyc(n))
        sjn = ["SJ%d" % q for q in range(NP)]
        part[0] = "pre"
        if NP == 1:
            compact(lambda a: T.SP[:, 128 * a:128 * a + 128:16], 8, T.KB, T.KD, blk("SP", 0, 128, 16), "")
        else:
            compact(lambda a: T.SJ[:, a:128:16], 8, T.KB, T.KD, sjn, "")
        for q in range(NP):
            b0, b1 = PARTS[q], PARTS[q + 1]
            n, p0, p1 = 16 * (b1 - b0), 16 * b0, 16 * b1
            sq = str(q)
            PK, pk = T["PK%d" % (q % 2)], "P_K%d" % (q % 2)
            spn, htn = blk("SP", p0, p1, 16), blk("HT", p0, p1, 16)
            part[0] = "cost" + sq
            todo = []
            a0 = 0
            for kind, k in C["cost" + sfx][q]:
                x, y = 16 * p0 + n * a0, 16 * p0 + n * (a0 + k)
                tags = W.indirect(T.HT[:, x // 16:y // 16])
                dn, nn = blk("D", x, y, 16), blk("N", x, y, 16)
                if kind == "s":
                    PD, pd = T["PD%d" % bank[0]], "P_D%d" % bank[0]
                    bank[0] = 1 - bank[0]
                    part[0] = "s16"
                    mm(PD[:, 0:y - x], T.ZR[:], T.MK1[:, 0:y - x], True, False, ["ZR", "MK1"], [pd], y - x)
                    for m in range(16):
                        mm(PD[:, m:y - x:16], T.NEG[:], T.SP[:, x:y:16], False, False, ["NEG"] + spn, [pd])
                    part[0] = "cost" + sq
                    act(T.D[:, x:y], tags, ACT.Copy, ["TAG"] + htn, dn, gat(y - x))
                    mm(PD[:, 0:y - x], T.IDN[:], T.D[:, x:y], False, True, ["IDN"] + dn, [pd], y - x)
                    act(T.N2[:, x:y], PD[:, 0:y - x], ACT.Abs, [pd], nn, cyc(y - x))
                else:
                    sn = blk("S16", x, y, 16)
                    if kind in "vw":
                        part[0] = "s16"
                        scan(T.S16[:, x:y], T.MK1[:, 0:y - x], T.SP[:, x:y], MUL, ADD, ["MK1"] + spn, sn, cyc((y - x) // 2))
                        part[0] = "cost" + sq
                    else:
                        PD, pd = T["PD%d" % bank[0]], "P_D%d" % bank[0]
                        bank[0] = 1 - bank[0]
                        for m in range(16):
                            mm(PD[:, m:y - x:16], T.IDN[:], T.SP[:, x:y:16], True, True, ["IDN"] + spn, [pd])
                        act(T.S16[:, x:y], PD[:, 0:y - x], ACT.Copy, [pd], sn, cyc(y - x))
                    tt(T.D[:, x:y], tags, T.S16[:, x:y], SUB, ["TAG"] + htn + sn, dn, gat(y - x))
                    if kind in "wy":
                        act(T.N2[:, x:y], T.D[:, x:y], ACT.Abs, dn, nn, cyc(y - x))
                    else:
                        ts(T.N2[:, x:y], T.D[:, x:y], 0.0, -2.0, MIN, MUL, dn, nn, cyc((y - x) // 2))
                        todo.append((T.D, a0, k, dn))
                todo.append((T.N2, a0, k, nn))
                a0 += k
            order = C["kord" + sfx].get(q) or range(len(todo))
            for i, z in enumerate(order):
                buf, a0, k, nm = todo[z]
                for a in range(a0, a0 + k):
                    j = 16 * p0 + n * a
                    mm(PK[:, 0:n], sel(T.Z, a), buf[:, j:j + n], i == 0 and a == a0,
                       i == len(todo) - 1 and a == a0 + k - 1, ["Z"] + nm, [pk], n)
            part[0] = "best" + sq
            least(T.KB, T.KD, T.K1, PK, pk, b0, b1, sq, "")
            ts(T.U9[:, 8 + b0:8 + b1], T.KB[:, 48 * b0 + 61:48 * b1 + 14:48], col(cTH), float(UB), GT, MUL,
               ["KS" + sq, "cTH"], ["U" + sq])
            tt(T.K3[:, b0:b1], T.K1[:, 3 * b0 + 2:3 * b1:3], T.U9[:, 8 + b0:8 + b1], ADD, ["K1" + sq, "U" + sq], ["K3" + sq])
            ts(T.K4[:, b0:b1], T.K3[:, b0:b1], UB + H - 1, None, AND, None, ["K3" + sq], ["K4" + sq])
            K6 = T.K6[:, 2 * b0:b0 + b1]
            ts(K6, T.K4[:, b0:b1], float(H), None, MIN, None, ["K4" + sq], ["K6" + sq])
            evn = blk("EV", p0, p1, 16)
            tt(T.EV[:, p0:p1], T.EF[:, 0:H + 16].indirect(K6), T.BASE[:, p0:p1], ADD,
               ["EF", "EFt", "K6" + sq, "BASE" + sq], evn, gat(n))
            ts(T.IDX[:, p0:p1], T.EV[:, p0:p1], 1.0 / 16, -15.0 / 32, MUL, ADD, evn, ["IDX" + sq], cyc(n))
            part[0] = "move" + sq
            a = 16 * p0
            for eng, k in C["move" + sfx][q]:
                b = a + k
                moved(eng, T.A2B[:, a:b], T.A[:, 16 * p0:16 * p1].indirect(T.IDX[:, a // 16:b // 16]), 0.0,
                      blk("A", 16 * p0, 16 * p1) + ["IDX" + sq], blk("B", a, b), k)
                a = b
        part[0] = "inv"
        a = 0
        for i, (eng, k) in enumerate(C["inv" + sfx]):
            part[0] = "inv%d" % i
            to = T.IW[:, 0:2048].indirect(LL[:, a // 16:(a + k) // 16])
            r = [ln, "ZR"] + blk("J33", 0, 16, 1)
            if eng == "s":
                act(to, T.J33[:, a:a + k], ACT.Silu, r, ["IW"], sca(k))
            else:
                cp(to, T.J33[:, a:a + k], r, ["IW"], sca(k))
            a += k
        if last:
            slots(None, None, sfx)
            part[0] = "home"
            a = 0
            for i, (eng, k) in enumerate(C["home"]):
                b = a + k
                moved(eng, T.X[:, a:b], T.A2B[:, 0:2048].indirect(T.GL[:, a // 16:b // 16]), 0.0,
                      blk("GL", a // 16, b // 16) + blk("B", 0, 2048), blk("X", a, b), k)
                dma("y", T.y[:, a:b], T.X[:, a:b], "d_y%d" % i, blk("X", a, b), (), 2000.0 + 1.3 * k)
                a = b
            break
        un, ksn = ["U%d" % q for q in range(NP)], ["KS%d" % q for q in range(NP)]
        part[0] = "learn"
        mm(T.PC[:, 0:8], T.IDN[:], T.CIC[:], True, False, ["IDN", "CIC"], ["P_C"])
        r = ["LT", "OB", "NL0", "NL1", "NL2", "NL3", "U0"] + un
        mm(T.PC[:, 0:8], T.LT[:], T.U9[:, 8:16], False, False, r, ["P_C"])
        for d in range(1, 8):
            mm(T.PC[:, 0:8], T.OB[:], T.U9[:, 8 - d:16 - d], False, False, r, ["P_C"])
        for j, (a, b, k) in enumerate(((0, 8, 1), (1, 8, 2), (2, 4, 1), (6, 8, 1), (4, 8, 1))):
            z = (0, 1, 2, 2, 3)[j]
            mm(T.PC[:, a:b:k], T.NL[:, 128 * z:128 * z + 128], T.U9[:, 8 + a:8 + b:k], False, j == 4, r, ["P_C"])
        cp(T.POS[:], T.PC[:, 0:8], ["P_C"], ["POS"])
        SQ = T["SQ%d" % t]
        cp(SQ[:, 32:416].indirect(T.POS[:, 0:8]), T.SJ[:], ["POS"] + sjn, ["SQo%d" % t], sca(128))
        send((rank + 1 + t % (NR - 1)) % NR, SQ[:, 0:32], SQ[:, 32:64], "req%d" % t, "lq%d" % t, ["SQo%d" % t])
        part[0] = "count"
        for b in range(8):
            mm(T.PD0[:, 0:1], T.OB[:], T.U9[:, 8 + b:9 + b], b == 0, b == 7, ["OB"] + un, ["P_D0"])
        ts(T.E[:, 0:68:34], T.SIG[:, 0:2], T.PD0[:, 0:1], 0.25, GE, MUL, ["SIG", "P_D0"], ["Ei"])
        part[0] = "cls"
        mm(T.PS[:, 0:11], T.FOUR[:], T.KB[:, 61:542:48], True, True, ["FOUR", "KSc"] + ksn, ["P_S"], 256)
        mm(T.PS[:, 11:20], T.FOUR[:], T.KB[:, 61:446:48], True, True, ["FOUR", "KSc"] + ksn, ["P_S"], 256)
        scan(T.RS[:], T.RD[:], T.PS[:, 0:20], MUL, ADD, ["RD", "P_S"], ["RS2"])
        ts(T.O3[:], T.IOT[:, 0:8], T.RS[:, 19:20], 448.0, ADD, ADD, ["IOTa", "RS2"], ["O3"])
        cp(LN[:], T.NB[:, 0:1024].indirect(T.O3[:, 0:8]), ["NB", "O3"], [lnn], gat(128))
        slots(LN, lnn, sfx)
        serve(t)

    named = {}
    for i, o in enumerate(ops):
        named.setdefault((o["part"], o["eng"], o["t"]), []).append(i)
    for eng, steps, chain in C.get("rules", ()):
        for t in steps:
            row = [named[p, eng, -9 if p in ("setup", "j33", "late", "zero") else t + dt][k] for p, k, dt in chain]
            for a, b in zip(row, row[1:]):
                ops[b]["order"].add(a)
    if C.get("fresh") or "seq" not in ORDER:
        ORDER["seq"] = improve(ops, issue_order(ops, C), C)
    seq = ORDER["seq"]
    pos = {}
    for i in seq:
        o = ops[i]
        if o["sem"] is None:
            pos[o["eng"]] = pos.get(o["eng"], 0) + 1
            o["pos"] = pos[o["eng"]]
    at = {i: k for k, i in enumerate(seq)}
    know = {e: {} for e in Q}
    for i in seq:
        o = ops[i]
        k = know[o["eng"]]
        waits = []
        for d in sorted(o["deps"], key=lambda z: -at[z]):
            x = ops[d]
            key, val = (x["eng"], x["pos"]) if x["sem"] is None else (x["sem"][0], 1)
            if k.get(key, 0) >= val:
                continue
            waits.append(d)
            x["need"] = True
            k[key] = val
            for kk, vv in x["know"].items():
                if k.get(kk, 0) < vv:
                    k[kk] = vv
        ex = []
        for name, c in o["ext"]:
            if k.get(name, 0) < 1:
                ex.append((name, c))
                k[name] = 1
        o["waits"], o["ex"], o["know"] = waits, ex, dict(k)
    cnt = {}
    for i in seq:
        o = ops[i]
        q = Q[o["eng"]]
        for d in o["waits"]:
            x = ops[d]
            if x["sem"] is None:
                q.wait_ge(T.sem["q" + x["eng"]], x["cnt"])
            else:
                q.wait_ge(T.sem[x["sem"][0]], x["sem"][1])
        for name, c in o["ex"]:
            q.wait_ge(T.sem[name], c)
        ins = o["fn"]()
        for fn in o["more"]:
            ins = fn()
        if o["sem"] is None:
            if o["need"]:
                cnt[o["eng"]] = cnt.get(o["eng"], 0) + 1
                o["cnt"] = cnt[o["eng"]]
                ins.then_inc(T.sem["q" + o["eng"]], 1)
        elif o["sem"][2]:
            ins.then_inc(T.sem[o["sem"][0]], 16)
    for o in ops:
        if o["sem"] is not None and not o["need"]:
            Q[o["eng"]].wait_ge(T.sem[o["sem"][0]], o["sem"][1])
